import numpy as np
import ml_dtypes


def mxq(x, axis, fmt="e4m3"):
    dtype, down = {"e4m3": (ml_dtypes.float8_e4m3fn, 7), "e5m2": (ml_dtypes.float8_e5m2, 14)}[fmt]
    v = np.moveaxis(np.asarray(x, np.float32).astype(ml_dtypes.bfloat16).astype(np.float64), axis, -1)
    blocks = v.reshape(v.shape[:-1] + (-1, 32))
    amax = np.abs(blocks).max(-1, keepdims=True)
    byte = np.maximum(np.where(amax > 0, np.frexp(amax)[1] - 1 + 127, 0) - down, 1)
    scale = np.exp2(byte - 127.0)
    codes = (blocks / scale).astype(np.float32).astype(dtype).astype(np.float64)
    return np.moveaxis((codes * scale).reshape(v.shape), -1, axis)


WIDE = False


def mx_kscale(k):
    if not WIDE:
        return np.ones(k)
    levels = np.array([18, -18])
    if k % 512:
        return np.exp2(np.random.permutation(np.resize(levels, k // 32))).repeat(32)
    a = np.empty((k // 512, 16))
    for p in range(k // 512):
        a[p, :8] = np.random.permutation(np.resize(levels, 8))
        for g in range(8):
            far = levels[np.abs(levels - a[p, g]) >= 10]
            a[p, g + 8] = far[np.random.randint(len(far))]
    return np.exp2(a.ravel()).repeat(32)


def f64(x):
    return np.asarray(x).astype(np.float64)


def striped(idx):
    return np.tile(np.asarray(idx).reshape(-1, 16).T, (8, 1)).astype(np.uint16)


def unstriped(offs):
    return offs[:16].T.reshape(-1).astype(np.int64)


B, N, T, D, R = 1, 1024, 2048, 512, 512


def setup_inputs():
    n = np.random.standard_normal
    idx = np.random.permutation(T)[:B * N]
    s = mx_kscale(D)[:, None]
    z = mx_kscale(R)[:, None]
    r = np.random.uniform(0.5, 2.0, T)
    x = n((B, D, R))
    return {
        "xT": (x * s).astype(np.float32),
        "wT": (n((D, T)) * (1.00 / np.sqrt(D)) / s / r).astype(np.float32),
        "wt": (np.random.uniform(0.5, 1.5, (B, R, 1)) * 1.0 / np.sqrt(R) * z).astype(np.float32),
        "ts": np.tile(r, (128, 1)).astype(np.float32),
        "xm": (x.transpose(0, 2, 1) / z).astype(np.float32),
        "offs": striped(idx),
    }


def reference(xT, wT, wt, ts, xm, offs):
    idx = unstriped(offs)
    pick = lambda x: x[:, idx].reshape(x.shape[0], B, N).transpose(1, 0, 2)
    a = mxq(f64(xT), 1, "e4m3").transpose(0, 2, 1) @ mxq(pick(f64(wT)), 1, "e4m3")
    ts_ = pick(f64(ts))[:, :1, :]
    a = a * ts_
    t = a[:, :, :N // 2] - a[:, :, N // 2:]
    q = f64(wt) / (1.0 + np.exp(t))
    g = np.concatenate([-q, q], -1)
    g = g * ts_
    dw = mxq(f64(xm), 1, "e4m3").transpose(0, 2, 1) @ mxq(g, 1, "e5m2")
    gw = np.zeros((D, T))
    gw[:, idx] = dw.transpose(1, 0, 2).reshape(D, B * N)
    return gw

@@ -1,0 +1,249 @@
+from contextlib import ExitStack
+
+import concourse.mybir as mybir
+from concourse.masks import make_identity
+
+F32 = mybir.dt.float32
+BF16 = mybir.dt.bfloat16
+U32 = mybir.dt.uint32
+U16 = mybir.dt.uint16
+U8 = mybir.dt.uint8
+E4M3 = mybir.dt.float8_e4m3fn_x4
+E5M2 = mybir.dt.float8_e5m2_x4
+ACT = mybir.ActivationFunctionType
+ALU = mybir.AluOpType
+
+P = 128
+PACK = 4
+N, T, D, R = 1024, 2048, 512, 512
+HALF = N // 2
+CHUNK = 256
+PIECE = 512
+FLOPS = 2 * 2 * N * D * R
+
+
+def tile_attend_gbpr_w_ts_kernel(tc, xT, wT, wt, ts, xm, offs, out):
+    nc = tc.nc
+    with ExitStack() as ctx:
+        keep = ctx.enter_context(tc.tile_pool(name="keep", bufs=1))
+        ring = ctx.enter_context(tc.tile_pool(name="ring", bufs=2))
+        sums = ctx.enter_context(tc.tile_pool(name="sums", bufs=4))
+        ps_a = ctx.enter_context(tc.psum_pool(name="ps_a", bufs=4))
+        ps_t = ctx.enter_context(tc.psum_pool(name="ps_t", bufs=2))
+        ps_d = ctx.enter_context(tc.psum_pool(name="ps_d", bufs=2))
+
+        def slots(first, count):
+            return offsets[:, first // 16 : (first + count) // 16]
+
+        offsets = keep.tile([P, N // 16], U16, name="offsets")
+        nc.sync.dma_start(offsets[:], offs)
+        wt_cols = keep.tile([P, PACK], F32, name="wt_cols")
+        nc.sync.dma_start(out=wt_cols[:], in_=wt[0].rearrange("(p t) o -> p (t o)", t=PACK))
+
+        ts_win = keep.tile([P, T], F32, name="ts_win")
+        nc.vector.memset(ts_win[:].bitcast(U32), 0)
+        ident = keep.tile([P, P], F32, name="ident")
+        make_identity(nc, ident[:])
+        warm = keep.tile([P, 1], F32, name="warm")
+        nc.scalar.activation(out=warm[:], in_=ident[:, 0:1], func=ACT.Sigmoid)
+
+        w_rows = wT.rearrange("(p u e) c -> p u e c", u=2, e=2)
+        w_raw = {}
+        for u in range(2):
+            for k in range(T // PIECE):
+                w_raw[u, k] = keep.tile([P, 2, PIECE], F32, name="w_raw%d_%d" % (u, k))
+                nc.sync.dma_start(out=w_raw[u, k][:], in_=w_rows[:, u, :, k * PIECE : (k + 1) * PIECE])
+                if (u, k) == (0, 2):
+                    nc.sync.dma_start(out=ts_win[0:1, :], in_=ts[0:1, :])
+        x_rows = xT[0].rearrange("(p t) r -> p t r", t=PACK)
+        x_raw = []
+        for k in range(2):
+            x_raw.append(keep.tile([P, PACK, R // 2], F32, name="x_raw%d" % k))
+            nc.sync.dma_start(out=x_raw[k][:], in_=x_rows[:, :, k * (R // 2) : (k + 1) * (R // 2)])
+        xm_raw = keep.tile([P, PACK, D], F32, name="xm_raw")
+        nc.sync.dma_start(out=xm_raw[:], in_=xm[0].rearrange("(p t) d -> p t d", t=PACK))
+
+        out_win = []
+        for j in range(D // P):
+            out_win.append(keep.tile([P, T], F32, name="out_win%d" % j))
+            (nc.vector if j == 0 else nc.gpsimd).memset(out_win[j][:].bitcast(U32), 0)
+
+        wt_wide = keep.tile([P, PACK, P], F32, name="wt_wide")
+        nc.vector.tensor_copy(out=wt_wide[:], in_=wt_cols[:].unsqueeze(2).to_broadcast([P, PACK, P]))
+        wt_ps = ps_a.tile([P, PACK, P], F32, name="acc")
+        for t in range(PACK):
+            nc.tensor.transpose(wt_ps[:, t, :], wt_wide[:, t, :], ident[:])
+        wt_row = keep.tile([P, P, PACK], F32, name="wt_row")
+        nc.vector.tensor_copy(out=wt_row[:], in_=wt_ps[:].rearrange("p t m -> p m t"))
+        wt_flat = wt_row[:].rearrange("p m t -> p (m t)")
+
+        ts_got = keep.tile([P, N], F32, name="ts_got")
+        nc.vector.tensor_copy(out=ts_got[:], in_=ts_win[:].indirect(offsets[:]))
+        ts_col = []
+        for side in range(2):
+            ts_ps = ps_a.tile([P, 4, P], F32, name="acc")
+            for b in range(4):
+                first = side * HALF + b * P
+                nc.tensor.transpose(ts_ps[:, b, :], ts_got[:, first : first + P], ident[:])
+            ts_col.append(keep.tile([P, 4], F32, name="ts_col%d" % side))
+            nc.vector.tensor_scalar(
+                out=ts_col[side][:], in0=ts_ps[:, :, 0], scalar1=(-1.0, 1.0)[side], scalar2=None, op0=ALU.mult
+            )
+
+        w_pair = [keep.tile([P, T, 2], BF16, name="w_pair%d" % u) for u in range(2)]
+        w_got = keep.tile([P, N, PACK], BF16, name="w_got", align_bytes=64)
+        w_got_words = w_got[:].rearrange("p n t -> p (n t)").bitcast(U32).rearrange("p (n u) -> p n u", u=2)
+        w_codes = keep.tile([P, N], U32, name="w_codes", align_bytes=64)
+        w_scales = keep.tile([P, N], U8, name="w_scales", align_bytes=64)
+
+        def cast_piece(u, k, on_vector):
+            dst = w_pair[u][:, k * PIECE : (k + 1) * PIECE, :]
+            src = w_raw[u, k][:].rearrange("p e c -> p c e")
+            if on_vector:
+                nc.vector.tensor_copy(out=dst, in_=src)
+            else:
+                nc.scalar.activation(out=dst, in_=src, func=ACT.Copy)
+
+        def gather_pairs(u, first, count):
+            window = w_pair[u][:].rearrange("p c e -> p (c e)").bitcast(U32)
+            nc.vector.tensor_copy(out=w_got_words[:, first : first + count, u], in_=window.indirect(slots(first, count)))
+
+        def quantize(codes, scales, grouped, first, count, fmt):
+            nc.vector.quantize_mx(
+                out=codes[:, first : first + count].bitcast(fmt),
+                scales=scales[:, first : first + count],
+                in_=grouped[:, first : first + count, :].rearrange("p n t -> p (n t)"),
+            )
+
+        def interleave(dst, src):
+            nc.scalar.activation(
+                out=dst.rearrange("p (c i) t -> p c t i", i=4),
+                in_=src.rearrange("p t (c i) -> p c t i", i=4),
+                func=ACT.Copy,
+            )
+
+        for k in range(T // PIECE):
+            cast_piece(0, k, k == 3)
+        gather_pairs(0, 0, N)
+        for k in range(T // PIECE):
+            cast_piece(1, k, k >= 2)
+
+        def table_operand(c):
+            for side in range(2):
+                gather_pairs(1, side * HALF + c * CHUNK, CHUNK)
+            for side in range(2):
+                quantize(w_codes, w_scales, w_got, side * HALF + c * CHUNK, CHUNK, E4M3)
+
+        table_operand(0)
+
+        x_grouped = keep.tile([P, R, PACK], BF16, name="x_grouped", align_bytes=64)
+        x_codes = keep.tile([P, R], U32, name="x_codes", align_bytes=64)
+        x_scales = keep.tile([P, R], U8, name="x_scales", align_bytes=64)
+        for k in range(2):
+            interleave(x_grouped[:, k * (R // 2) : (k + 1) * (R // 2), :], x_raw[k][:])
+            quantize(x_codes, x_scales, x_grouped, k * (R // 2), R // 2, E4M3)
+
+        table_operand(1)
+
+        xm_grouped = keep.tile([P, D, PACK], BF16, name="xm_grouped", align_bytes=64)
+        xm_codes = keep.tile([P, D], U32, name="xm_codes", align_bytes=64)
+        xm_scales = keep.tile([P, D], U8, name="xm_scales", align_bytes=64)
+
+        def xm_operand(first, count):
+            interleave(xm_grouped[:, first : first + count, :], xm_raw[:, :, first : first + count])
+            quantize(xm_codes, xm_scales, xm_grouped, first, count, E4M3)
+
+        h_codes, h_scales = [], []
+
+        def gradient_operand(c):
+            h_grouped = keep.tile([P, 2 * CHUNK, PACK], BF16, name="h_grouped%d" % c, align_bytes=64)
+            h_words = h_grouped[:].rearrange("p n t -> p (n t)").bitcast(F32).rearrange("p (n u) -> p n u", u=2)
+            h_codes.append(keep.tile([P, 2 * CHUNK], U32, name="h_codes%d" % c, align_bytes=64))
+            h_scales.append(keep.tile([P, 2 * CHUNK], U8, name="h_scales%d" % c, align_bytes=64))
+            blocks = range(CHUNK // P)
+            score, sig = {}, {}
+            for b in blocks:
+                for side in range(2):
+                    first = side * HALF + c * CHUNK + b * P
+                    score[b, side] = ps_a.tile([P, R], F32, name="acc")
+                    nc.tensor.matmul_mx(
+                        out=score[b, side][:],
+                        lhsT=w_codes[:, first : first + P].bitcast(E4M3),
+                        lhsT_scale=w_scales[:, first : first + P],
+                        rhs=x_codes[:].bitcast(E4M3),
+                        rhs_scale=x_scales[:],
+                        start=True,
+                        stop=True,
+                    )
+            for b in blocks:
+                col = c * (CHUNK // P) + b
+                neg_pos = ring.tile([P, R], F32, name="neg_pos")
+                nc.scalar.activation(
+                    out=neg_pos[:], in_=score[b, 0][:], func=ACT.Copy, scale=ts_col[0][:, col : col + 1]
+                )
+                margin = ring.tile([P, R], F32, name="margin")
+                nc.vector.scalar_tensor_tensor(
+                    out=margin[:],
+                    in0=score[b, 1][:],
+                    scalar=ts_col[1][:, col : col + 1],
+                    in1=neg_pos[:],
+                    op0=ALU.mult,
+                    op1=ALU.add,
+                )
+                sig[b] = ring.tile([P, R], F32, name="sig")
+                nc.scalar.activation(out=sig[b][:], in_=margin[:], func=ACT.Sigmoid)
+            for b in blocks:
+                col = c * (CHUNK // P) + b
+                q = ring.tile([P, R], F32, name="q")
+                nc.vector.tensor_tensor(out=q[:], in0=sig[b][:], in1=wt_flat, op=ALU.mult)
+                for side in range(2):
+                    h = ring.tile([P, R], BF16, name="h%d" % side)
+                    scale = ts_col[side][:, col : col + 1]
+                    if c == 0 and side == 0:
+                        nc.vector.tensor_scalar(out=h[:], in0=q[:], scalar1=scale, scalar2=None, op0=ALU.mult)
+                    else:
+                        nc.scalar.activation(out=h[:], in_=q[:], func=ACT.Copy, scale=scale)
+                    words = h[:].bitcast(F32)
+                    turned = ps_t.tile([P, 2, P], F32, name="turned")
+                    for u in range(2):
+                        nc.tensor.transpose(turned[:, u, :], words[:, u : 2 * P : 2], ident[:])
+                    first = side * CHUNK + b * P
+                    nc.scalar.copy(out=h_words[:, first : first + P, :], in_=turned[:].rearrange("p u i -> p i u"))
+                    if c == 0:
+                        quantize(h_codes[c], h_scales[c], h_grouped, first, P, E5M2)
+            if c == 1:
+                quantize(h_codes[c], h_scales[c], h_grouped, 0, 2 * CHUNK, E5M2)
+
+        def scatter_sums(c, j):
+            acc = ps_d.tile([P, 2 * CHUNK], F32, name="dw")
+            nc.tensor.matmul_mx(
+                out=acc[:],
+                lhsT=xm_codes[:, j * P : (j + 1) * P].bitcast(E4M3),
+                lhsT_scale=xm_scales[:, j * P : (j + 1) * P],
+                rhs=h_codes[c][:].bitcast(E5M2),
+                rhs_scale=h_scales[c][:],
+                start=True,
+                stop=True,
+            )
+            dw = sums.tile([P, 2 * CHUNK], F32, name="dw_sb")
+            for side in range(2):
+                cols = slice(side * CHUNK, (side + 1) * CHUNK)
+                nc.scalar.copy(out=dw[:, cols], in_=acc[:, cols])
+            for side in range(2):
+                cols = slice(side * CHUNK, (side + 1) * CHUNK)
+                nc.vector.tensor_copy(
+                    out=out_win[j][:].indirect(slots(side * HALF + c * CHUNK, CHUNK)), in_=dw[:, cols]
+                )
+
+        gradient_operand(0)
+        xm_operand(0, P)
+        scatter_sums(0, 0)
+        xm_operand(P, P)
+        scatter_sums(0, 1)
+        xm_operand(2 * P, 2 * P)
+        gradient_operand(1)
+        scatter_sums(0, 2)
+        scatter_sums(0, 3)
+        for j in range(D // P):
+            scatter_sums(1, j)
+            nc.sync.dma_start(out=out[j * P : (j + 1) * P, :], in_=out_win[j][:])

@@ -19,6 +19,7 @@ N, T, D, R = 1024, 2048, 512, 512
 HALF = N // 2
 CHUNK = 256
 PIECE = 512
+WINDOWS = 3
 FLOPS = 2 * 2 * N * D * R
 
 
@@ -27,10 +28,10 @@ def tile_attend_gbpr_w_ts_kernel(tc, xT, wT, wt, ts, xm, offs, out):
     with ExitStack() as ctx:
         keep = ctx.enter_context(tc.tile_pool(name="keep", bufs=1))
         ring = ctx.enter_context(tc.tile_pool(name="ring", bufs=2))
-        sums = ctx.enter_context(tc.tile_pool(name="sums", bufs=4))
+        sums = ctx.enter_context(tc.tile_pool(name="sums", bufs=8))
         ps_a = ctx.enter_context(tc.psum_pool(name="ps_a", bufs=4))
         ps_t = ctx.enter_context(tc.psum_pool(name="ps_t", bufs=2))
-        ps_d = ctx.enter_context(tc.psum_pool(name="ps_d", bufs=2))
+        ps_d = ctx.enter_context(tc.psum_pool(name="ps_d", bufs=1))
 
         def slots(first, count):
             return offsets[:, first // 16 : (first + count) // 16]
@@ -60,22 +61,21 @@ def tile_attend_gbpr_w_ts_kernel(tc, xT, wT, wt, ts, xm, offs, out):
         for k in range(2):
             x_raw.append(keep.tile([P, PACK, R // 2], F32, name="x_raw%d" % k))
             nc.sync.dma_start(out=x_raw[k][:], in_=x_rows[:, :, k * (R // 2) : (k + 1) * (R // 2)])
-        xm_raw = keep.tile([P, PACK, D], F32, name="xm_raw")
-        nc.sync.dma_start(out=xm_raw[:], in_=xm[0].rearrange("(p t) d -> p t d", t=PACK))
+        xm_rows = xm[0].rearrange("(p t) d -> p t d", t=PACK)
+        xm_raw = []
+        for k in range(2):
+            xm_raw.append(keep.tile([P, PACK, D // 2], F32, name="xm_raw%d" % k))
+            nc.sync.dma_start(out=xm_raw[k][:], in_=xm_rows[:, :, k * (D // 2) : (k + 1) * (D // 2)])
 
         out_win = []
-        for j in range(D // P):
+        for j in range(WINDOWS):
             out_win.append(keep.tile([P, T], F32, name="out_win%d" % j))
-            (nc.vector if j == 0 else nc.gpsimd).memset(out_win[j][:].bitcast(U32), 0)
+            nc.vector.memset(out_win[j][:].bitcast(U32), 0)
 
-        wt_wide = keep.tile([P, PACK, P], F32, name="wt_wide")
-        nc.vector.tensor_copy(out=wt_wide[:], in_=wt_cols[:].unsqueeze(2).to_broadcast([P, PACK, P]))
-        wt_ps = ps_a.tile([P, PACK, P], F32, name="acc")
+        wt_ps = ps_d.tile([P, PACK, P], F32, name="wt_ps")
         for t in range(PACK):
-            nc.tensor.transpose(wt_ps[:, t, :], wt_wide[:, t, :], ident[:])
-        wt_row = keep.tile([P, P, PACK], F32, name="wt_row")
-        nc.vector.tensor_copy(out=wt_row[:], in_=wt_ps[:].rearrange("p t m -> p m t"))
-        wt_flat = wt_row[:].rearrange("p m t -> p (m t)")
+            nc.tensor.transpose(wt_ps[:, t, :], wt_cols[:, t : t + 1].to_broadcast([P, P]), ident[:])
+        wt_row = wt_ps[:].rearrange("p t m -> p m t")
 
         ts_got = keep.tile([P, N], F32, name="ts_got")
         nc.vector.tensor_copy(out=ts_got[:], in_=ts_win[:].indirect(offsets[:]))
@@ -96,9 +96,9 @@ def tile_attend_gbpr_w_ts_kernel(tc, xT, wT, wt, ts, xm, offs, out):
         w_codes = keep.tile([P, N], U32, name="w_codes", align_bytes=64)
         w_scales = keep.tile([P, N], U8, name="w_scales", align_bytes=64)
 
-        def cast_piece(u, k, on_vector):
-            dst = w_pair[u][:, k * PIECE : (k + 1) * PIECE, :]
-            src = w_raw[u, k][:].rearrange("p e c -> p c e")
+        def cast_piece(u, k, on_vector, lo=0, hi=PIECE):
+            dst = w_pair[u][:, k * PIECE + lo : k * PIECE + hi, :]
+            src = w_raw[u, k][:, :, lo:hi].rearrange("p e c -> p c e")
             if on_vector:
                 nc.vector.tensor_copy(out=dst, in_=src)
             else:
@@ -115,52 +115,56 @@ def tile_attend_gbpr_w_ts_kernel(tc, xT, wT, wt, ts, xm, offs, out):
                 in_=grouped[:, first : first + count, :].rearrange("p n t -> p (n t)"),
             )
 
-        def interleave(dst, src):
-            nc.scalar.activation(
-                out=dst.rearrange("p (c i) t -> p c t i", i=4),
-                in_=src.rearrange("p t (c i) -> p c t i", i=4),
-                func=ACT.Copy,
-            )
+        def interleave(dst, src, on_vector=False):
+            dst = dst.rearrange("p (c i) t -> p c t i", i=4)
+            src = src.rearrange("p t (c i) -> p c t i", i=4)
+            if on_vector:
+                nc.vector.tensor_copy(out=dst, in_=src)
+            else:
+                nc.scalar.activation(out=dst, in_=src, func=ACT.Copy)
 
         for k in range(T // PIECE):
             cast_piece(0, k, k == 3)
         gather_pairs(0, 0, N)
-        for k in range(T // PIECE):
-            cast_piece(1, k, k >= 2)
+        for k in range(T // PIECE - 1):
+            cast_piece(1, k, False)
+        cast_piece(1, 3, True, 0, 352)
+        cast_piece(1, 3, False, 352, PIECE)
 
-        def table_operand(c):
-            for side in range(2):
-                gather_pairs(1, side * HALF + c * CHUNK, CHUNK)
+        def quantize_table(c):
             for side in range(2):
                 quantize(w_codes, w_scales, w_got, side * HALF + c * CHUNK, CHUNK, E4M3)
 
-        table_operand(0)
+        for side in range(2):
+            gather_pairs(1, side * HALF, CHUNK)
+        quantize_table(0)
 
         x_grouped = keep.tile([P, R, PACK], BF16, name="x_grouped", align_bytes=64)
         x_codes = keep.tile([P, R], U32, name="x_codes", align_bytes=64)
         x_scales = keep.tile([P, R], U8, name="x_scales", align_bytes=64)
-        for k in range(2):
-            interleave(x_grouped[:, k * (R // 2) : (k + 1) * (R // 2), :], x_raw[k][:])
-            quantize(x_codes, x_scales, x_grouped, k * (R // 2), R // 2, E4M3)
+        interleave(x_grouped[:, 0 : 2 * P, :], x_raw[0][:])
+        quantize(x_codes, x_scales, x_grouped, 0, 2 * P, E4M3)
+        interleave(x_grouped[:, 2 * P : 3 * P, :], x_raw[1][:, :, 0:P])
+        interleave(x_grouped[:, 3 * P : 4 * P, :], x_raw[1][:, :, P : 2 * P], True)
+        quantize(x_codes, x_scales, x_grouped, 2 * P, 2 * P, E4M3)
+        for side in range(2):
+            gather_pairs(1, side * HALF + CHUNK, CHUNK)
 
-        table_operand(1)
-
-        xm_grouped = keep.tile([P, D, PACK], BF16, name="xm_grouped", align_bytes=64)
         xm_codes = keep.tile([P, D], U32, name="xm_codes", align_bytes=64)
         xm_scales = keep.tile([P, D], U8, name="xm_scales", align_bytes=64)
 
-        def xm_operand(first, count):
-            interleave(xm_grouped[:, first : first + count, :], xm_raw[:, :, first : first + count])
-            quantize(xm_codes, xm_scales, xm_grouped, first, count, E4M3)
+        def xm_operand(first, count, raw, stage):
+            interleave(stage, raw)
+            nc.vector.quantize_mx(
+                out=xm_codes[:, first : first + count].bitcast(E4M3),
+                scales=xm_scales[:, first : first + count],
+                in_=stage.rearrange("p n t -> p (n t)"),
+            )
 
-        h_codes, h_scales = [], []
+        blocks = range(CHUNK // P)
+        h_codes, h_scales, margin, q, h = {}, {}, {}, {}, {}
 
-        def gradient_operand(c):
-            h_grouped = keep.tile([P, 2 * CHUNK, PACK], BF16, name="h_grouped%d" % c, align_bytes=64)
-            h_words = h_grouped[:].rearrange("p n t -> p (n t)").bitcast(F32).rearrange("p (n u) -> p n u", u=2)
-            h_codes.append(keep.tile([P, 2 * CHUNK], U32, name="h_codes%d" % c, align_bytes=64))
-            h_scales.append(keep.tile([P, 2 * CHUNK], U8, name="h_scales%d" % c, align_bytes=64))
-            blocks = range(CHUNK // P)
+        def pair_weights(c):
             score, sig = {}, {}
             for b in blocks:
                 for side in range(2):
@@ -181,9 +185,9 @@ def tile_attend_gbpr_w_ts_kernel(tc, xT, wT, wt, ts, xm, offs, out):
                 nc.scalar.activation(
                     out=neg_pos[:], in_=score[b, 0][:], func=ACT.Copy, scale=ts_col[0][:, col : col + 1]
                 )
-                margin = ring.tile([P, R], F32, name="margin")
+                margin[c, b] = keep.tile([P, R], F32, name="margin%d_%d" % (c, b), align_bytes=64)
                 nc.vector.scalar_tensor_tensor(
-                    out=margin[:],
+                    out=margin[c, b][:],
                     in0=score[b, 1][:],
                     scalar=ts_col[1][:, col : col + 1],
                     in1=neg_pos[:],
@@ -191,19 +195,33 @@ def tile_attend_gbpr_w_ts_kernel(tc, xT, wT, wt, ts, xm, offs, out):
                     op1=ALU.add,
                 )
                 sig[b] = ring.tile([P, R], F32, name="sig")
-                nc.scalar.activation(out=sig[b][:], in_=margin[:], func=ACT.Sigmoid)
+                nc.scalar.activation(out=sig[b][:], in_=margin[c, b][:], func=ACT.Sigmoid)
+            for b in blocks:
+                q[c, b] = ring.tile([P, R], F32, name="q")
+                nc.vector.tensor_tensor(
+                    out=q[c, b][:].rearrange("p (m t) -> p m t", t=PACK),
+                    in0=sig[b][:].rearrange("p (m t) -> p m t", t=PACK),
+                    in1=wt_row,
+                    op=ALU.mult,
+                )
+
+        def gradient_operand(c):
+            h_grouped = keep.tile([P, 2 * CHUNK, PACK], BF16, name="h_grouped%d" % c, align_bytes=64)
+            h_words = h_grouped[:].rearrange("p n t -> p (n t)").bitcast(F32).rearrange("p (n u) -> p n u", u=2)
+            h_codes[c] = keep.tile([P, 2 * CHUNK], U32, name="h_codes%d" % c, align_bytes=64)
+            h_scales[c] = keep.tile([P, 2 * CHUNK], U8, name="h_scales%d" % c, align_bytes=64)
             for b in blocks:
                 col = c * (CHUNK // P) + b
-                q = ring.tile([P, R], F32, name="q")
-                nc.vector.tensor_tensor(out=q[:], in0=sig[b][:], in1=wt_flat, op=ALU.mult)
                 for side in range(2):
-                    h = ring.tile([P, R], BF16, name="h%d" % side)
+                    h[c, b, side] = keep.tile([P, R], BF16, name="h%d_%d_%d" % (c, b, side))
                     scale = ts_col[side][:, col : col + 1]
                     if c == 0 and side == 0:
-                        nc.vector.tensor_scalar(out=h[:], in0=q[:], scalar1=scale, scalar2=None, op0=ALU.mult)
+                        nc.vector.tensor_scalar(
+                            out=h[c, b, side][:], in0=q[c, b][:], scalar1=scale, scalar2=None, op0=ALU.mult
+                        )
                     else:
-                        nc.scalar.activation(out=h[:], in_=q[:], func=ACT.Copy, scale=scale)
-                    words = h[:].bitcast(F32)
+                        nc.scalar.activation(out=h[c, b, side][:], in_=q[c, b][:], func=ACT.Copy, scale=scale)
+                    words = h[c, b, side][:].bitcast(F32)
                     turned = ps_t.tile([P, 2, P], F32, name="turned")
                     for u in range(2):
                         nc.tensor.transpose(turned[:, u, :], words[:, u : 2 * P : 2], ident[:])
@@ -214,8 +232,8 @@ def tile_attend_gbpr_w_ts_kernel(tc, xT, wT, wt, ts, xm, offs, out):
             if c == 1:
                 quantize(h_codes[c], h_scales[c], h_grouped, 0, 2 * CHUNK, E5M2)
 
-        def scatter_sums(c, j):
-            acc = ps_d.tile([P, 2 * CHUNK], F32, name="dw")
+        def scatter_sums(c, j, pool, last_stage=None):
+            acc = pool.tile([P, 2 * CHUNK], F32, name="acc")
             nc.tensor.matmul_mx(
                 out=acc[:],
                 lhsT=xm_codes[:, j * P : (j + 1) * P].bitcast(E4M3),
@@ -225,25 +243,32 @@ def tile_attend_gbpr_w_ts_kernel(tc, xT, wT, wt, ts, xm, offs, out):
                 start=True,
                 stop=True,
             )
-            dw = sums.tile([P, 2 * CHUNK], F32, name="dw_sb")
             for side in range(2):
-                cols = slice(side * CHUNK, (side + 1) * CHUNK)
-                nc.scalar.copy(out=dw[:, cols], in_=acc[:, cols])
-            for side in range(2):
-                cols = slice(side * CHUNK, (side + 1) * CHUNK)
-                nc.vector.tensor_copy(
-                    out=out_win[j][:].indirect(slots(side * HALF + c * CHUNK, CHUNK)), in_=dw[:, cols]
-                )
+                if side == 1 and last_stage is not None:
+                    dw = last_stage
+                else:
+                    dw = sums.tile([P, CHUNK], F32, name="dw")[:]
+                nc.scalar.copy(out=dw, in_=acc[:, side * CHUNK : (side + 1) * CHUNK])
+                window = out_win[j % WINDOWS][:].indirect(slots(side * HALF + c * CHUNK, CHUNK))
+                nc.vector.tensor_copy(out=window, in_=dw)
 
+        def store(j):
+            nc.sync.dma_start(out=out[j * P : (j + 1) * P, :], in_=out_win[j % WINDOWS][:])
+
+        pair_weights(0)
         gradient_operand(0)
-        xm_operand(0, P)
-        scatter_sums(0, 0)
-        xm_operand(P, P)
-        scatter_sums(0, 1)
-        xm_operand(2 * P, 2 * P)
+        quantize_table(1)
+        xm_stage = keep.tile([P, D // 2, PACK], BF16, name="xm_stage", align_bytes=64)
+        xm_operand(0, D // 2, xm_raw[0][:], xm_stage[:])
+        scatter_sums(0, 0, ps_d)
+        pair_weights(1)
+        xm_operand(D // 2, D // 2, xm_raw[1][:], margin[1, 0][:].bitcast(BF16).rearrange("p (n t) -> p n t", t=PACK))
+        scatter_sums(0, 1, ps_d)
         gradient_operand(1)
-        scatter_sums(0, 2)
-        scatter_sums(0, 3)
-        for j in range(D // P):
-            scatter_sums(1, j)
-            nc.sync.dma_start(out=out[j * P : (j + 1) * P, :], in_=out_win[j][:])
+        scatter_sums(0, 2, ps_a, h[1, 1, 1][:].bitcast(F32))
+        for j in range(WINDOWS):
+            scatter_sums(1, j, ps_a)
+            store(j)
+        scatter_sums(0, 3, ps_a)
+        scatter_sums(1, 3, ps_a)
+        store(3)

@@ -70,7 +70,7 @@ def tile_attend_gbpr_w_ts_kernel(tc, xT, wT, wt, ts, xm, offs, out):
         out_win = []
         for j in range(WINDOWS):
             out_win.append(keep.tile([P, T], F32, name="out_win%d" % j))
-            nc.vector.memset(out_win[j][:].bitcast(U32), 0)
+            (nc.gpsimd if j < 2 else nc.vector).memset(out_win[j][:].bitcast(U32), 0)
 
         wt_ps = ps_d.tile([P, PACK, P], F32, name="wt_ps")
         for t in range(PACK):
@@ -162,10 +162,10 @@ def tile_attend_gbpr_w_ts_kernel(tc, xT, wT, wt, ts, xm, offs, out):
             )
 
         blocks = range(CHUNK // P)
-        h_codes, h_scales, margin, q, h = {}, {}, {}, {}, {}
+        h_codes, h_scales, margin, sig, h = {}, {}, {}, {}, {}
 
         def pair_weights(c):
-            score, sig = {}, {}
+            score = {}
             for b in blocks:
                 for side in range(2):
                     first = side * HALF + c * CHUNK + b * P
@@ -194,16 +194,13 @@ def tile_attend_gbpr_w_ts_kernel(tc, xT, wT, wt, ts, xm, offs, out):
                     op0=ALU.mult,
                     op1=ALU.add,
                 )
-                sig[b] = ring.tile([P, R], F32, name="sig")
-                nc.scalar.activation(out=sig[b][:], in_=margin[c, b][:], func=ACT.Sigmoid)
+                sig[c, b] = keep.tile([P, R], F32, name="sig%d_%d" % (c, b))
+                nc.scalar.activation(out=sig[c, b][:], in_=margin[c, b][:], func=ACT.Sigmoid)
+
+        def row_weights(c):
             for b in blocks:
-                q[c, b] = ring.tile([P, R], F32, name="q")
-                nc.vector.tensor_tensor(
-                    out=q[c, b][:].rearrange("p (m t) -> p m t", t=PACK),
-                    in0=sig[b][:].rearrange("p (m t) -> p m t", t=PACK),
-                    in1=wt_row,
-                    op=ALU.mult,
-                )
+                rows = sig[c, b][:].rearrange("p (m t) -> p m t", t=PACK)
+                nc.vector.tensor_tensor(out=rows, in0=rows, in1=wt_row, op=ALU.mult)
 
         def gradient_operand(c):
             h_grouped = keep.tile([P, 2 * CHUNK, PACK], BF16, name="h_grouped%d" % c, align_bytes=64)
@@ -215,12 +212,17 @@ def tile_attend_gbpr_w_ts_kernel(tc, xT, wT, wt, ts, xm, offs, out):
                 for side in range(2):
                     h[c, b, side] = keep.tile([P, R], BF16, name="h%d_%d_%d" % (c, b, side))
                     scale = ts_col[side][:, col : col + 1]
-                    if c == 0 and side == 0:
-                        nc.vector.tensor_scalar(
-                            out=h[c, b, side][:], in0=q[c, b][:], scalar1=scale, scalar2=None, op0=ALU.mult
+                    if c == 0:
+                        nc.vector.scalar_tensor_tensor(
+                            out=h[c, b, side][:].rearrange("p (m t) -> p m t", t=PACK),
+                            in0=sig[c, b][:].rearrange("p (m t) -> p m t", t=PACK),
+                            scalar=scale,
+                            in1=wt_row,
+                            op0=ALU.mult,
+                            op1=ALU.mult,
                         )
                     else:
-                        nc.scalar.activation(out=h[c, b, side][:], in_=q[c, b][:], func=ACT.Copy, scale=scale)
+                        nc.scalar.activation(out=h[c, b, side][:], in_=sig[c, b][:], func=ACT.Copy, scale=scale)
                     words = h[c, b, side][:].bitcast(F32)
                     turned = ps_t.tile([P, 2, P], F32, name="turned")
                     for u in range(2):
@@ -255,13 +257,14 @@ def tile_attend_gbpr_w_ts_kernel(tc, xT, wT, wt, ts, xm, offs, out):
         def store(j):
             nc.sync.dma_start(out=out[j * P : (j + 1) * P, :], in_=out_win[j % WINDOWS][:])
 
+        quantize_table(1)
         pair_weights(0)
         gradient_operand(0)
-        quantize_table(1)
         xm_stage = keep.tile([P, D // 2, PACK], BF16, name="xm_stage", align_bytes=64)
         xm_operand(0, D // 2, xm_raw[0][:], xm_stage[:])
         scatter_sums(0, 0, ps_d)
         pair_weights(1)
+        row_weights(1)
         xm_operand(D // 2, D // 2, xm_raw[1][:], margin[1, 0][:].bitcast(BF16).rearrange("p (n t) -> p n t", t=PACK))
         scatter_sums(0, 1, ps_d)
         gradient_operand(1)

@@ -20,6 +20,7 @@ HALF = N // 2
 CHUNK = 256
 PIECE = 512
 WINDOWS = 3
+W_LOADS = ((0, 0, 1024), (0, 1024, 1024), (1, 0, 1024), (1, 1024, 512), (1, 1536, 512))
 FLOPS = 2 * 2 * N * D * R
 
 
@@ -50,12 +51,13 @@ def tile_attend_gbpr_w_ts_kernel(tc, xT, wT, wt, ts, xm, offs, out):
 
         w_rows = wT.rearrange("(p u e) c -> p u e c", u=2, e=2)
         w_raw = {}
-        for u in range(2):
-            for k in range(T // PIECE):
-                w_raw[u, k] = keep.tile([P, 2, PIECE], F32, name="w_raw%d_%d" % (u, k))
-                nc.sync.dma_start(out=w_raw[u, k][:], in_=w_rows[:, u, :, k * PIECE : (k + 1) * PIECE])
-                if (u, k) == (0, 2):
-                    nc.sync.dma_start(out=ts_win[0:1, :], in_=ts[0:1, :])
+        for u, first, count in W_LOADS:
+            raw = keep.tile([P, 2, count], F32, name="w_raw%d_%d" % (u, first))
+            nc.sync.dma_start(out=raw[:], in_=w_rows[:, u, :, first : first + count])
+            for k in range(count // PIECE):
+                w_raw[u, first // PIECE + k] = raw[:, :, k * PIECE : (k + 1) * PIECE]
+            if (u, first) == (0, 0):
+                nc.sync.dma_start(out=ts_win[0:1, :], in_=ts[0:1, :])
         x_rows = xT[0].rearrange("(p t) r -> p t r", t=PACK)
         x_raw = []
         for k in range(2):
@@ -127,7 +129,7 @@ def tile_attend_gbpr_w_ts_kernel(tc, xT, wT, wt, ts, xm, offs, out):
             cast_piece(0, k, k == 3)
         gather_pairs(0, 0, N)
         for k in range(T // PIECE - 1):
-            cast_piece(1, k, False)
+            cast_piece(1, k, k == 2)
         cast_piece(1, 3, True, 0, 352)
         cast_piece(1, 3, False, 352, PIECE)
 
@@ -224,18 +226,19 @@ def tile_attend_gbpr_w_ts_kernel(tc, xT, wT, wt, ts, xm, offs, out):
                     else:
                         nc.scalar.activation(out=h[c, b, side][:], in_=sig[c, b][:], func=ACT.Copy, scale=scale)
                     words = h[c, b, side][:].bitcast(F32)
-                    turned = ps_t.tile([P, 2, P], F32, name="turned")
+                    bank = ps_t.tile([P, R], F32, name="turned")
+                    turned = bank[:, 0 : 2 * P].rearrange("p (u i) -> p u i", u=2)
                     for u in range(2):
                         nc.tensor.transpose(turned[:, u, :], words[:, u : 2 * P : 2], ident[:])
                     first = side * CHUNK + b * P
-                    nc.scalar.copy(out=h_words[:, first : first + P, :], in_=turned[:].rearrange("p u i -> p i u"))
+                    nc.scalar.copy(out=h_words[:, first : first + P, :], in_=turned.rearrange("p u i -> p i u"))
                     if c == 0:
                         quantize(h_codes[c], h_scales[c], h_grouped, first, P, E5M2)
             if c == 1:
                 quantize(h_codes[c], h_scales[c], h_grouped, 0, 2 * CHUNK, E5M2)
+            return bank
 
-        def scatter_sums(c, j, pool, last_stage=None):
-            acc = pool.tile([P, 2 * CHUNK], F32, name="acc")
+        def table_sums(c, j, acc):
             nc.tensor.matmul_mx(
                 out=acc[:],
                 lhsT=xm_codes[:, j * P : (j + 1) * P].bitcast(E4M3),
@@ -245,14 +248,18 @@ def tile_attend_gbpr_w_ts_kernel(tc, xT, wT, wt, ts, xm, offs, out):
                 start=True,
                 stop=True,
             )
+            return acc
+
+        def scatter(c, j, side, acc):
+            dw = sums.tile([P, CHUNK], F32, name="dw")
+            nc.scalar.copy(out=dw[:], in_=acc[:, side * CHUNK : (side + 1) * CHUNK])
+            window = out_win[j % WINDOWS][:].indirect(slots(side * HALF + c * CHUNK, CHUNK))
+            nc.vector.tensor_copy(out=window, in_=dw[:])
+
+        def scatter_sums(c, j, acc):
+            table_sums(c, j, acc)
             for side in range(2):
-                if side == 1 and last_stage is not None:
-                    dw = last_stage
-                else:
-                    dw = sums.tile([P, CHUNK], F32, name="dw")[:]
-                nc.scalar.copy(out=dw, in_=acc[:, side * CHUNK : (side + 1) * CHUNK])
-                window = out_win[j % WINDOWS][:].indirect(slots(side * HALF + c * CHUNK, CHUNK))
-                nc.vector.tensor_copy(out=window, in_=dw)
+                scatter(c, j, side, acc)
 
         def store(j):
             nc.sync.dma_start(out=out[j * P : (j + 1) * P, :], in_=out_win[j % WINDOWS][:])
@@ -262,16 +269,23 @@ def tile_attend_gbpr_w_ts_kernel(tc, xT, wT, wt, ts, xm, offs, out):
         gradient_operand(0)
         xm_stage = keep.tile([P, D // 2, PACK], BF16, name="xm_stage", align_bytes=64)
         xm_operand(0, D // 2, xm_raw[0][:], xm_stage[:])
-        scatter_sums(0, 0, ps_d)
+        scatter_sums(0, 0, ps_d.tile([P, 2 * CHUNK], F32, name="acc"))
         pair_weights(1)
         row_weights(1)
         xm_operand(D // 2, D // 2, xm_raw[1][:], margin[1, 0][:].bitcast(BF16).rearrange("p (n t) -> p n t", t=PACK))
-        scatter_sums(0, 1, ps_d)
-        gradient_operand(1)
-        scatter_sums(0, 2, ps_a, h[1, 1, 1][:].bitcast(F32))
-        for j in range(WINDOWS):
-            scatter_sums(1, j, ps_a)
-            store(j)
-        scatter_sums(0, 3, ps_a)
-        scatter_sums(1, 3, ps_a)
+        scatter_sums(0, 1, ps_d.tile([P, 2 * CHUNK], F32, name="acc"))
+        last_bank = gradient_operand(1)
+        scatter_sums(0, 2, last_bank)
+        late = [table_sums(1, j, ps_a.tile([P, 2 * CHUNK], F32, name="acc")) for j in range(WINDOWS)]
+        for j, side in ((0, 0), (1, 0), (0, 1), (2, 0), (1, 1), (2, 1)):
+            scatter(1, j, side, late[j])
+            if side == 1:
+                store(j)
+        dw_last = keep.tile([P, 2, 2, CHUNK], F32, name="dw_last")
+        for c in range(2):
+            acc = table_sums(c, 3, ps_a.tile([P, 2 * CHUNK], F32, name="acc"))
+            nc.scalar.copy(out=dw_last[:, :, c, :], in_=acc[:].rearrange("p (s n) -> p s n", s=2))
+        nc.vector.tensor_copy(
+            out=out_win[3 % WINDOWS][:].indirect(offsets[:]), in_=dw_last[:].rearrange("p s c n -> p (s c n)")
+        )
         store(3)

@@ -6,6 +6,7 @@ from concourse.masks import make_identity
 F32 = mybir.dt.float32
 BF16 = mybir.dt.bfloat16
 U32 = mybir.dt.uint32
+I32 = mybir.dt.int32
 U16 = mybir.dt.uint16
 U8 = mybir.dt.uint8
 E4M3 = mybir.dt.float8_e4m3fn_x4
@@ -18,9 +19,8 @@ PACK = 4
 N, T, D, R = 1024, 2048, 512, 512
 HALF = N // 2
 CHUNK = 256
-PIECE = 512
 WINDOWS = 3
-W_LOADS = ((0, 0, 1024), (0, 1024, 1024), (1, 0, 1024), (1, 1024, 512), (1, 1536, 512))
+W_LOADS = ((0, 0, 1024, 0), (0, 1024, 512, 512), (0, 1536, 512, 384), (1, 0, 1024, 0), (1, 1024, 512, 512), (1, 1536, 512, 384))
 FLOPS = 2 * 2 * N * D * R
 
 
@@ -29,35 +29,36 @@ def tile_attend_gbpr_w_ts_kernel(tc, xT, wT, wt, ts, xm, offs, out):
     with ExitStack() as ctx:
         keep = ctx.enter_context(tc.tile_pool(name="keep", bufs=1))
         ring = ctx.enter_context(tc.tile_pool(name="ring", bufs=2))
-        sums = ctx.enter_context(tc.tile_pool(name="sums", bufs=8))
+        sums = ctx.enter_context(tc.tile_pool(name="sums", bufs=16))
+        early = ctx.enter_context(tc.tile_pool(name="early", bufs=1))
         ps_a = ctx.enter_context(tc.psum_pool(name="ps_a", bufs=4))
-        ps_t = ctx.enter_context(tc.psum_pool(name="ps_t", bufs=2))
-        ps_d = ctx.enter_context(tc.psum_pool(name="ps_d", bufs=1))
+        ps_b = ctx.enter_context(tc.psum_pool(name="ps_b", bufs=3))
+        ps_w = ctx.enter_context(tc.psum_pool(name="ps_w", bufs=1))
 
         def slots(first, count):
             return offsets[:, first // 16 : (first + count) // 16]
 
-        offsets = keep.tile([P, N // 16], U16, name="offsets")
-        nc.sync.dma_start(offsets[:], offs)
-        wt_cols = keep.tile([P, PACK], F32, name="wt_cols")
-        nc.sync.dma_start(out=wt_cols[:], in_=wt[0].rearrange("(p t) o -> p (t o)", t=PACK))
-
         ts_win = keep.tile([P, T], F32, name="ts_win")
-        nc.vector.memset(ts_win[:].bitcast(U32), 0)
+        nc.sync.dma_start(out=ts_win[P - 1 : P, :], in_=ts[0:1, :])
+        nc.vector.memset(ts_win[0 : P - 1, :].bitcast(U32), 0)
         ident = keep.tile([P, P], F32, name="ident")
         make_identity(nc, ident[:])
         warm = keep.tile([P, 1], F32, name="warm")
         nc.scalar.activation(out=warm[:], in_=ident[:, 0:1], func=ACT.Sigmoid)
 
+        offsets = keep.tile([P, N // 16], U16, name="offsets")
+        nc.sync.dma_start(offsets[:], offs)
+        wt_cols = keep.tile([P, PACK], F32, name="wt_cols")
         w_rows = wT.rearrange("(p u e) c -> p u e c", u=2, e=2)
-        w_raw = {}
-        for u, first, count in W_LOADS:
-            raw = keep.tile([P, 2, count], F32, name="w_raw%d_%d" % (u, first))
-            nc.sync.dma_start(out=raw[:], in_=w_rows[:, u, :, first : first + count])
-            for k in range(count // PIECE):
-                w_raw[u, first // PIECE + k] = raw[:, :, k * PIECE : (k + 1) * PIECE]
-            if (u, first) == (0, 0):
-                nc.sync.dma_start(out=ts_win[0:1, :], in_=ts[0:1, :])
+        w_raw = []
+        for k, (u, first, count, on_vector) in enumerate(W_LOADS):
+            if k == 3:
+                w_raw.append(early.tile([P, 2, count], F32, name="w_raw3", offset=0))
+            else:
+                w_raw.append(keep.tile([P, 2, count], F32, name="w_raw%d" % k))
+            nc.sync.dma_start(out=w_raw[k][:], in_=w_rows[:, u, :, first : first + count])
+            if k == 2:
+                nc.sync.dma_start(out=wt_cols[:], in_=wt[0].rearrange("(p t) o -> p (t o)", t=PACK))
         x_rows = xT[0].rearrange("(p t) r -> p t r", t=PACK)
         x_raw = []
         for k in range(2):
@@ -69,46 +70,68 @@ def tile_attend_gbpr_w_ts_kernel(tc, xT, wT, wt, ts, xm, offs, out):
             xm_raw.append(keep.tile([P, PACK, D // 2], F32, name="xm_raw%d" % k))
             nc.sync.dma_start(out=xm_raw[k][:], in_=xm_rows[:, :, k * (D // 2) : (k + 1) * (D // 2)])
 
-        out_win = []
-        for j in range(WINDOWS):
-            out_win.append(keep.tile([P, T], F32, name="out_win%d" % j))
-            (nc.gpsimd if j < 2 else nc.vector).memset(out_win[j][:].bitcast(U32), 0)
+        out_win = {}
+        for j in range(2):
+            out_win[j] = keep.tile([P, T], F32, name="out_win%d" % j)
+            nc.gpsimd.memset(out_win[j][:].bitcast(U32), 0)
 
-        wt_ps = ps_d.tile([P, PACK, P], F32, name="wt_ps")
+        ts_got = keep.tile([P, N], F32, name="ts_got")
+        nc.vector.tensor_copy(out=ts_got[:], in_=ts_win[:].indirect(offsets[:]))
+        ts_ps = []
+        for side in range(2):
+            ts_ps.append(ps_a.tile([P, 4, P], F32, name="acc"))
+            for b in range(4):
+                first = side * HALF + b * P
+                nc.tensor.transpose(ts_ps[side][:, b, :], ts_got[:, first : first + P], ident[:])
+
+        wt_ps = ps_w.tile([P, PACK, P], F32, name="wt_ps")
         for t in range(PACK):
             nc.tensor.transpose(wt_ps[:, t, :], wt_cols[:, t : t + 1].to_broadcast([P, P]), ident[:])
         wt_row = wt_ps[:].rearrange("p t m -> p m t")
 
-        ts_got = keep.tile([P, N], F32, name="ts_got")
-        nc.vector.tensor_copy(out=ts_got[:], in_=ts_win[:].indirect(offsets[:]))
-        ts_col = []
-        for side in range(2):
-            ts_ps = ps_a.tile([P, 4, P], F32, name="acc")
-            for b in range(4):
-                first = side * HALF + b * P
-                nc.tensor.transpose(ts_ps[:, b, :], ts_got[:, first : first + P], ident[:])
-            ts_col.append(keep.tile([P, 4], F32, name="ts_col%d" % side))
-            nc.vector.tensor_scalar(
-                out=ts_col[side][:], in0=ts_ps[:, :, 0], scalar1=(-1.0, 1.0)[side], scalar2=None, op0=ALU.mult
-            )
-
         w_pair = [keep.tile([P, T, 2], BF16, name="w_pair%d" % u) for u in range(2)]
-        w_got = keep.tile([P, N, PACK], BF16, name="w_got", align_bytes=64)
-        w_got_words = w_got[:].rearrange("p n t -> p (n t)").bitcast(U32).rearrange("p (n u) -> p n u", u=2)
-        w_codes = keep.tile([P, N], U32, name="w_codes", align_bytes=64)
-        w_scales = keep.tile([P, N], U8, name="w_scales", align_bytes=64)
+        w_got, w_codes, w_scales = [], [], []
+        for c in range(2):
+            w_got.append(keep.tile([P, 2 * CHUNK, PACK], BF16, name="w_got%d" % c, align_bytes=64))
+            w_scales.append(keep.tile([P, 2 * CHUNK], U8, name="w_scales%d" % c, align_bytes=64))
 
-        def cast_piece(u, k, on_vector, lo=0, hi=PIECE):
-            dst = w_pair[u][:, k * PIECE + lo : k * PIECE + hi, :]
-            src = w_raw[u, k][:, :, lo:hi].rearrange("p e c -> p c e")
+        w_codes.append(keep.tile([P, 2 * CHUNK], U32, name="w_codes0", align_bytes=64))
+
+        def cast(k, lo, hi, on_vector):
+            u, first = W_LOADS[k][0:2]
+            dst = w_pair[u][:, first + lo : first + hi, :]
+            src = w_raw[k][:, :, lo:hi].rearrange("p e c -> p c e")
             if on_vector:
                 nc.vector.tensor_copy(out=dst, in_=src)
             else:
                 nc.scalar.activation(out=dst, in_=src, func=ACT.Copy)
 
-        def gather_pairs(u, first, count):
-            window = w_pair[u][:].rearrange("p c e -> p (c e)").bitcast(U32)
-            nc.vector.tensor_copy(out=w_got_words[:, first : first + count, u], in_=window.indirect(slots(first, count)))
+        def cast_load(k):
+            count, on_vector = W_LOADS[k][2:4]
+            if on_vector < count:
+                cast(k, 0, count - on_vector, False)
+            if on_vector:
+                cast(k, count - on_vector, count, True)
+
+        stage = keep.tile([P, 3 * N + CHUNK], U32, name="stage", align_bytes=64)
+        second = (N, N + HALF + CHUNK)
+
+        def window(u):
+            return w_pair[u][:].rearrange("p c e -> p (c e)").bitcast(U32)
+
+        def gather_second(c):
+            for side in range(2):
+                first = second[c] + side * HALF
+                nc.vector.tensor_copy(
+                    out=stage[:, first : first + CHUNK], in_=window(1).indirect(slots(side * HALF + c * CHUNK, CHUNK))
+                )
+
+        def weave(c):
+            apart = second[c] - c * CHUNK
+            src = stage[:, c * CHUNK : c * CHUNK + 2 * apart].bitcast(I32).rearrange("p (u s i) -> p s i u", u=2, i=HALF)
+            src = src[:, 0:2, 0:CHUNK, :]
+            dst = w_got[c][:].rearrange("p n t -> p (n t)").bitcast(I32).rearrange("p (s i u) -> p s i u", s=2, u=2)
+            nc.vector.tensor_copy(out=dst, in_=src)
 
         def quantize(codes, scales, grouped, first, count, fmt):
             nc.vector.quantize_mx(
@@ -125,118 +148,156 @@ def tile_attend_gbpr_w_ts_kernel(tc, xT, wT, wt, ts, xm, offs, out):
             else:
                 nc.scalar.activation(out=dst, in_=src, func=ACT.Copy)
 
-        for k in range(T // PIECE):
-            cast_piece(0, k, k == 3)
-        gather_pairs(0, 0, N)
-        for k in range(T // PIECE - 1):
-            cast_piece(1, k, k == 2)
-        cast_piece(1, 3, True, 0, 352)
-        cast_piece(1, 3, False, 352, PIECE)
-
-        def quantize_table(c):
-            for side in range(2):
-                quantize(w_codes, w_scales, w_got, side * HALF + c * CHUNK, CHUNK, E4M3)
-
+        for k in range(3):
+            cast_load(k)
+        nc.vector.tensor_copy(out=stage[:, 0:N], in_=window(0).indirect(offsets[:]))
+        for k in range(3, len(W_LOADS)):
+            cast_load(k)
+        ts_col = []
         for side in range(2):
-            gather_pairs(1, side * HALF, CHUNK)
-        quantize_table(0)
+            ts_col.append(early.tile([P, 4], F32, name="ts_col%d" % side, offset=32 * side))
+            nc.scalar.activation(out=ts_col[side][:], in_=ts_ps[side][:, :, P - 1], func=ACT.Copy, scale=(-1.0, 1.0)[side])
+        gather_second(0)
+        weave(0)
 
-        x_grouped = keep.tile([P, R, PACK], BF16, name="x_grouped", align_bytes=64)
+        x_grouped = stage[:, second[1] : second[1] + 2 * R].bitcast(BF16).rearrange("p (n t) -> p n t", t=PACK)
         x_codes = keep.tile([P, R], U32, name="x_codes", align_bytes=64)
         x_scales = keep.tile([P, R], U8, name="x_scales", align_bytes=64)
         interleave(x_grouped[:, 0 : 2 * P, :], x_raw[0][:])
-        quantize(x_codes, x_scales, x_grouped, 0, 2 * P, E4M3)
-        interleave(x_grouped[:, 2 * P : 3 * P, :], x_raw[1][:, :, 0:P])
-        interleave(x_grouped[:, 3 * P : 4 * P, :], x_raw[1][:, :, P : 2 * P], True)
-        quantize(x_codes, x_scales, x_grouped, 2 * P, 2 * P, E4M3)
-        for side in range(2):
-            gather_pairs(1, side * HALF + CHUNK, CHUNK)
+        interleave(x_grouped[:, 2 * P : 4 * P, :], x_raw[1][:])
+        quantize(w_codes[0], w_scales[0], w_got[0], 0, 2 * CHUNK, E4M3)
+        quantize(x_codes, x_scales, x_grouped, 0, R, E4M3)
 
         xm_codes = keep.tile([P, D], U32, name="xm_codes", align_bytes=64)
         xm_scales = keep.tile([P, D], U8, name="xm_scales", align_bytes=64)
+        xm_grouped = []
+        for k in range(2):
+            xm_grouped.append(keep.tile([P, D // 2, PACK], BF16, name="xm_grouped%d" % k, align_bytes=64))
 
-        def xm_operand(first, count, raw, stage):
-            interleave(stage, raw)
+        def quantize_xm(k):
             nc.vector.quantize_mx(
-                out=xm_codes[:, first : first + count].bitcast(E4M3),
-                scales=xm_scales[:, first : first + count],
-                in_=stage.rearrange("p n t -> p (n t)"),
+                out=xm_codes[:, k * (D // 2) : (k + 1) * (D // 2)].bitcast(E4M3),
+                scales=xm_scales[:, k * (D // 2) : (k + 1) * (D // 2)],
+                in_=xm_grouped[k][:].rearrange("p n t -> p (n t)"),
             )
 
         blocks = range(CHUNK // P)
-        h_codes, h_scales, margin, sig, h = {}, {}, {}, {}, {}
+        h_codes, h_scales = {}, {}
 
-        def pair_weights(c):
+        def scores(c):
             score = {}
             for b in blocks:
                 for side in range(2):
-                    first = side * HALF + c * CHUNK + b * P
+                    first = side * CHUNK + b * P
                     score[b, side] = ps_a.tile([P, R], F32, name="acc")
                     nc.tensor.matmul_mx(
                         out=score[b, side][:],
-                        lhsT=w_codes[:, first : first + P].bitcast(E4M3),
-                        lhsT_scale=w_scales[:, first : first + P],
+                        lhsT=w_codes[c][:, first : first + P].bitcast(E4M3),
+                        lhsT_scale=w_scales[c][:, first : first + P],
                         rhs=x_codes[:].bitcast(E4M3),
                         rhs_scale=x_scales[:],
                         start=True,
                         stop=True,
                     )
+            return score
+
+        def scale_of(c, b, side):
+            col = c * (CHUNK // P) + b
+            return ts_col[side][:, col : col + 1]
+
+        def gradients_by_vector(c):
+            score = scores(c)
+            margin, sig, h = {}, {}, {}
             for b in blocks:
-                col = c * (CHUNK // P) + b
                 neg_pos = ring.tile([P, R], F32, name="neg_pos")
-                nc.scalar.activation(
-                    out=neg_pos[:], in_=score[b, 0][:], func=ACT.Copy, scale=ts_col[0][:, col : col + 1]
-                )
-                margin[c, b] = keep.tile([P, R], F32, name="margin%d_%d" % (c, b), align_bytes=64)
+                nc.scalar.activation(out=neg_pos[:], in_=score[b, 0][:], func=ACT.Copy, scale=scale_of(c, b, 0))
+                margin[b] = ring.tile([P, R], F32, name="margin")
                 nc.vector.scalar_tensor_tensor(
-                    out=margin[c, b][:],
+                    out=margin[b][:],
                     in0=score[b, 1][:],
-                    scalar=ts_col[1][:, col : col + 1],
+                    scalar=scale_of(c, b, 1),
                     in1=neg_pos[:],
                     op0=ALU.mult,
                     op1=ALU.add,
                 )
-                sig[c, b] = keep.tile([P, R], F32, name="sig%d_%d" % (c, b))
-                nc.scalar.activation(out=sig[c, b][:], in_=margin[c, b][:], func=ACT.Sigmoid)
-
-        def row_weights(c):
             for b in blocks:
-                rows = sig[c, b][:].rearrange("p (m t) -> p m t", t=PACK)
-                nc.vector.tensor_tensor(out=rows, in0=rows, in1=wt_row, op=ALU.mult)
+                sig[b] = keep.tile([P, R], F32, name="sig%d" % b, align_bytes=64)
+                nc.scalar.activation(out=sig[b][:], in_=margin[b][:], func=ACT.Sigmoid)
+            for b in blocks:
+                for side in range(2):
+                    h[b, side] = keep.tile([P, R], BF16, name="h%d_%d_%d" % (c, b, side))
+                    nc.vector.scalar_tensor_tensor(
+                        out=h[b, side][:].rearrange("p (m t) -> p m t", t=PACK),
+                        in0=sig[b][:].rearrange("p (m t) -> p m t", t=PACK),
+                        scalar=scale_of(c, b, side),
+                        in1=wt_row,
+                        op0=ALU.mult,
+                        op1=ALU.mult,
+                    )
+            return {key: tile[:].bitcast(F32).rearrange("p (m u) -> p u m", u=2) for key, tile in h.items()}
 
-        def gradient_operand(c):
-            h_grouped = keep.tile([P, 2 * CHUNK, PACK], BF16, name="h_grouped%d" % c, align_bytes=64)
+        def gradients_by_scalar(c):
+            score = scores(c)
+            h = {}
+            for b in blocks:
+                scaled = []
+                for side in range(2):
+                    scaled.append(ring.tile([P, PACK, P], F32, name="scaled%d" % side))
+                    nc.scalar.activation(
+                        out=scaled[side][:],
+                        in_=score[b, side][:].rearrange("p (m t) -> p t m", t=PACK),
+                        func=ACT.Copy,
+                        scale=scale_of(c, b, side),
+                    )
+                margin = ps_a.tile([P, PACK, P], F32, name="acc")
+                for t in range(PACK):
+                    for side in range(2):
+                        nc.tensor.matmul(
+                            margin[:, t, :],
+                            lhsT=scaled[side][:, t, :],
+                            rhs=ident[:],
+                            is_transpose=True,
+                            start=(side == 0),
+                            stop=(side == 1),
+                        )
+                sig = ring.tile([P, PACK, P], F32, name="sig")
+                nc.scalar.activation(out=sig[:], in_=margin[:], func=ACT.Sigmoid)
+                weighted = ring.tile([P, PACK, P], F32, name="weighted")
+                back = ps_a.tile([P, PACK, P], F32, name="acc")
+                for t in range(PACK):
+                    nc.scalar.activation(
+                        out=weighted[:, t, :], in_=sig[:, t, :], func=ACT.Copy, scale=wt_cols[:, t : t + 1]
+                    )
+                    nc.tensor.transpose(back[:, t, :], weighted[:, t, :], ident[:])
+                for side in range(2):
+                    h[b, side] = keep.tile([P, 2, P, 2], BF16, name="h%d_%d_%d" % (c, b, side))
+                    nc.scalar.activation(
+                        out=h[b, side][:],
+                        in_=back[:].rearrange("p (u e) m -> p u m e", u=2),
+                        func=ACT.Copy,
+                        scale=scale_of(c, b, side),
+                    )
+            return {
+                key: tile[:].rearrange("p u m e -> p (u m e)").bitcast(F32).rearrange("p (u m) -> p u m", u=2)
+                for key, tile in h.items()
+            }
+
+        def gradient_operand(c, words, h_grouped, width):
             h_words = h_grouped[:].rearrange("p n t -> p (n t)").bitcast(F32).rearrange("p (n u) -> p n u", u=2)
             h_codes[c] = keep.tile([P, 2 * CHUNK], U32, name="h_codes%d" % c, align_bytes=64)
             h_scales[c] = keep.tile([P, 2 * CHUNK], U8, name="h_scales%d" % c, align_bytes=64)
             for b in blocks:
-                col = c * (CHUNK // P) + b
                 for side in range(2):
-                    h[c, b, side] = keep.tile([P, R], BF16, name="h%d_%d_%d" % (c, b, side))
-                    scale = ts_col[side][:, col : col + 1]
-                    if c == 0:
-                        nc.vector.scalar_tensor_tensor(
-                            out=h[c, b, side][:].rearrange("p (m t) -> p m t", t=PACK),
-                            in0=sig[c, b][:].rearrange("p (m t) -> p m t", t=PACK),
-                            scalar=scale,
-                            in1=wt_row,
-                            op0=ALU.mult,
-                            op1=ALU.mult,
-                        )
-                    else:
-                        nc.scalar.activation(out=h[c, b, side][:], in_=sig[c, b][:], func=ACT.Copy, scale=scale)
-                    words = h[c, b, side][:].bitcast(F32)
-                    bank = ps_t.tile([P, R], F32, name="turned")
+                    bank = ps_b.tile([P, R], F32, name="late")
                     turned = bank[:, 0 : 2 * P].rearrange("p (u i) -> p u i", u=2)
                     for u in range(2):
-                        nc.tensor.transpose(turned[:, u, :], words[:, u : 2 * P : 2], ident[:])
+                        nc.tensor.transpose(turned[:, u, :], words[b, side][:, u, :], ident[:])
                     first = side * CHUNK + b * P
                     nc.scalar.copy(out=h_words[:, first : first + P, :], in_=turned.rearrange("p u i -> p i u"))
-                    if c == 0:
+                    if width == P:
                         quantize(h_codes[c], h_scales[c], h_grouped, first, P, E5M2)
-            if c == 1:
-                quantize(h_codes[c], h_scales[c], h_grouped, 0, 2 * CHUNK, E5M2)
-            return bank
+            if width > P:
+                quantize(h_codes[c], h_scales[c], h_grouped, 0, width, E5M2)
 
         def table_sums(c, j, acc):
             nc.tensor.matmul_mx(
@@ -250,41 +311,45 @@ def tile_attend_gbpr_w_ts_kernel(tc, xT, wT, wt, ts, xm, offs, out):
             )
             return acc
 
-        def scatter(c, j, side, acc):
-            dw = sums.tile([P, CHUNK], F32, name="dw")
+        def scatter(c, j, side, acc, dw):
             nc.scalar.copy(out=dw[:], in_=acc[:, side * CHUNK : (side + 1) * CHUNK])
-            window = out_win[j % WINDOWS][:].indirect(slots(side * HALF + c * CHUNK, CHUNK))
-            nc.vector.tensor_copy(out=window, in_=dw[:])
-
-        def scatter_sums(c, j, acc):
-            table_sums(c, j, acc)
-            for side in range(2):
-                scatter(c, j, side, acc)
+            nc.vector.tensor_copy(out=out_win[j][:].indirect(slots(side * HALF + c * CHUNK, CHUNK)), in_=dw[:])
 
         def store(j):
             nc.sync.dma_start(out=out[j * P : (j + 1) * P, :], in_=out_win[j % WINDOWS][:])
 
-        quantize_table(1)
-        pair_weights(0)
-        gradient_operand(0)
-        xm_stage = keep.tile([P, D // 2, PACK], BF16, name="xm_stage", align_bytes=64)
-        xm_operand(0, D // 2, xm_raw[0][:], xm_stage[:])
-        scatter_sums(0, 0, ps_d.tile([P, 2 * CHUNK], F32, name="acc"))
-        pair_weights(1)
-        row_weights(1)
-        xm_operand(D // 2, D // 2, xm_raw[1][:], margin[1, 0][:].bitcast(BF16).rearrange("p (n t) -> p n t", t=PACK))
-        scatter_sums(0, 1, ps_d.tile([P, 2 * CHUNK], F32, name="acc"))
-        last_bank = gradient_operand(1)
-        scatter_sums(0, 2, last_bank)
-        late = [table_sums(1, j, ps_a.tile([P, 2 * CHUNK], F32, name="acc")) for j in range(WINDOWS)]
-        for j, side in ((0, 0), (1, 0), (0, 1), (2, 0), (1, 1), (2, 1)):
-            scatter(1, j, side, late[j])
+        order = ((0, 0), (1, 0), (0, 1), (2, 0), (1, 1), (2, 1))
+
+        words = gradients_by_vector(0)
+        interleave(xm_grouped[0][:], xm_raw[0][:])
+        h_first = keep.tile([P, 2 * CHUNK, PACK], BF16, name="h_first", tag="h_then_window", align_bytes=64)
+        gradient_operand(0, words, h_first, P)
+        quantize_xm(0)
+        gather_second(1)
+        weave(1)
+        w_codes.append(keep.tile([P, 2 * CHUNK], U32, name="w_codes1", align_bytes=64))
+        quantize(w_codes[1], w_scales[1], w_got[1], 0, 2 * CHUNK, E4M3)
+        interleave(xm_grouped[1][:], xm_raw[1][:])
+        quantize_xm(1)
+        out_win[2] = keep.tile([P, T], F32, name="out_win2", tag="h_then_window", align_bytes=64)
+        nc.gpsimd.memset(out_win[2][:].bitcast(U32), 0)
+        acc = [table_sums(0, j, ps_b.tile([P, 2 * CHUNK], F32, name="late")) for j in range(2)]
+        acc.append(table_sums(0, 2, ps_w.tile([P, 2 * CHUNK], F32, name="wt_ps")))
+        for j, side in order[:-1]:
+            scatter(0, j, side, acc[j], sums.tile([P, CHUNK], F32, name="dw"))
+        words = gradients_by_scalar(1)
+        h_second = keep.tile([P, 2 * CHUNK, PACK], BF16, name="h_second", align_bytes=64)
+        gradient_operand(1, words, h_second, 2 * CHUNK)
+        scatter(0, 2, 1, acc[2], keep.tile([P, CHUNK], F32, name="dw_held", tag="h1_1_1"))
+        acc = [table_sums(1, j, ps_b.tile([P, 2 * CHUNK], F32, name="late")) for j in range(WINDOWS)]
+        for j, side in order:
+            scatter(1, j, side, acc[j], sums.tile([P, CHUNK], F32, name="dw"))
             if side == 1:
                 store(j)
         dw_last = keep.tile([P, 2, 2, CHUNK], F32, name="dw_last")
         for c in range(2):
-            acc = table_sums(c, 3, ps_a.tile([P, 2 * CHUNK], F32, name="acc"))
-            nc.scalar.copy(out=dw_last[:, :, c, :], in_=acc[:].rearrange("p (s n) -> p s n", s=2))
+            last = table_sums(c, 3, ps_a.tile([P, 2 * CHUNK], F32, name="acc"))
+            nc.scalar.copy(out=dw_last[:, :, c, :], in_=last[:].rearrange("p (s n) -> p s n", s=2))
         nc.vector.tensor_copy(
             out=out_win[3 % WINDOWS][:].indirect(offsets[:]), in_=dw_last[:].rearrange("p s c n -> p (s c n)")
         )

@@ -19,7 +19,8 @@ PACK = 4
 N, T, D, R = 1024, 2048, 512, 512
 HALF = N // 2
 CHUNK = 256
-WINDOWS = 3
+WINDOWS = 4
+CLEAR = 512
 W_LOADS = ((0, 0, 1024, 0), (0, 1024, 512, 512), (0, 1536, 512, 384), (1, 0, 1024, 0), (1, 1024, 512, 512), (1, 1536, 512, 384))
 FLOPS = 2 * 2 * N * D * R
 
@@ -71,9 +72,14 @@ def tile_attend_gbpr_w_ts_kernel(tc, xT, wT, wt, ts, xm, offs, out):
             nc.sync.dma_start(out=xm_raw[k][:], in_=xm_rows[:, :, k * (D // 2) : (k + 1) * (D // 2)])
 
         out_win = {}
-        for j in range(2):
+
+        def clear(window):
+            for first in range(0, T, CLEAR):
+                nc.gpsimd.memset(window[:, first : first + CLEAR].bitcast(U32), 0)
+
+        for j in range(WINDOWS - 1):
             out_win[j] = keep.tile([P, T], F32, name="out_win%d" % j)
-            nc.gpsimd.memset(out_win[j][:].bitcast(U32), 0)
+            clear(out_win[j])
 
         ts_got = keep.tile([P, N], F32, name="ts_got")
         nc.vector.tensor_copy(out=ts_got[:], in_=ts_win[:].indirect(offsets[:]))
@@ -128,10 +134,14 @@ def tile_attend_gbpr_w_ts_kernel(tc, xT, wT, wt, ts, xm, offs, out):
 
         def weave(c):
             apart = second[c] - c * CHUNK
-            src = stage[:, c * CHUNK : c * CHUNK + 2 * apart].bitcast(I32).rearrange("p (u s i) -> p s i u", u=2, i=HALF)
+            word = (I32, U32)[c]
+            src = stage[:, c * CHUNK : c * CHUNK + 2 * apart].bitcast(word).rearrange("p (u s i) -> p s i u", u=2, i=HALF)
             src = src[:, 0:2, 0:CHUNK, :]
-            dst = w_got[c][:].rearrange("p n t -> p (n t)").bitcast(I32).rearrange("p (s i u) -> p s i u", s=2, u=2)
-            nc.vector.tensor_copy(out=dst, in_=src)
+            dst = w_got[c][:].rearrange("p n t -> p (n t)").bitcast(word).rearrange("p (s i u) -> p s i u", s=2, u=2)
+            if c == 0:
+                nc.vector.tensor_copy(out=dst, in_=src)
+            else:
+                nc.scalar.copy(out=dst, in_=src)
 
         def quantize(codes, scales, grouped, first, count, fmt):
             nc.vector.quantize_mx(
@@ -182,7 +192,14 @@ def tile_attend_gbpr_w_ts_kernel(tc, xT, wT, wt, ts, xm, offs, out):
             )
 
         blocks = range(CHUNK // P)
-        h_codes, h_scales = {}, {}
+        padded_codes = keep.tile([P, 3 * CHUNK], U32, name="padded_codes", align_bytes=64)
+        padded_scales = keep.tile([P, 3 * CHUNK], U8, name="padded_scales", align_bytes=64)
+        nc.gpsimd.memset(padded_codes[:, 0:CHUNK], 0)
+        nc.gpsimd.memset(padded_scales[:, 0:CHUNK].bitcast(U32), 0)
+        zeros = keep.tile([P, P], F32, name="zeros")
+        nc.gpsimd.memset(zeros[:], 0.0)
+        h_codes = [padded_codes[:, CHUNK:], keep.tile([P, 2 * CHUNK], U32, name="h_codes1", align_bytes=64)[:]]
+        h_scales = [padded_scales[:, CHUNK:], keep.tile([P, 2 * CHUNK], U8, name="h_scales1", align_bytes=64)[:]]
 
         def scores(c):
             score = {}
@@ -284,45 +301,52 @@ def tile_attend_gbpr_w_ts_kernel(tc, xT, wT, wt, ts, xm, offs, out):
 
         def gradient_operand(c, words, h_grouped, width):
             h_words = h_grouped[:].rearrange("p n t -> p (n t)").bitcast(F32).rearrange("p (n u) -> p n u", u=2)
-            h_codes[c] = keep.tile([P, 2 * CHUNK], U32, name="h_codes%d" % c, align_bytes=64)
-            h_scales[c] = keep.tile([P, 2 * CHUNK], U8, name="h_scales%d" % c, align_bytes=64)
             for b in blocks:
                 for side in range(2):
                     bank = ps_b.tile([P, R], F32, name="late")
                     turned = bank[:, 0 : 2 * P].rearrange("p (u i) -> p u i", u=2)
                     for u in range(2):
                         nc.tensor.transpose(turned[:, u, :], words[b, side][:, u, :], ident[:])
-                    first = side * CHUNK + b * P
+                    first = (2 * b + side) * P
                     nc.scalar.copy(out=h_words[:, first : first + P, :], in_=turned.rearrange("p u i -> p i u"))
                     if width == P:
                         quantize(h_codes[c], h_scales[c], h_grouped, first, P, E5M2)
             if width > P:
                 quantize(h_codes[c], h_scales[c], h_grouped, 0, width, E5M2)
 
-        def table_sums(c, j, acc):
+        def table_sums(codes, scales, j, acc):
             nc.tensor.matmul_mx(
                 out=acc[:],
                 lhsT=xm_codes[:, j * P : (j + 1) * P].bitcast(E4M3),
                 lhsT_scale=xm_scales[:, j * P : (j + 1) * P],
-                rhs=h_codes[c][:].bitcast(E5M2),
-                rhs_scale=h_scales[c][:],
+                rhs=codes.bitcast(E5M2),
+                rhs_scale=scales,
                 start=True,
                 stop=True,
             )
             return acc
 
+        def copy_side(dw, acc, side):
+            sums_of_side = acc[:].rearrange("p (b s i) -> p s b i", s=2, i=P)[:, side]
+            nc.scalar.copy(out=dw.rearrange("p (b i) -> p b i", i=P), in_=sums_of_side)
+
         def scatter(c, j, side, acc, dw):
-            nc.scalar.copy(out=dw[:], in_=acc[:, side * CHUNK : (side + 1) * CHUNK])
+            copy_side(dw[:], acc, side)
             nc.vector.tensor_copy(out=out_win[j][:].indirect(slots(side * HALF + c * CHUNK, CHUNK)), in_=dw[:])
 
-        def store(j):
-            nc.sync.dma_start(out=out[j * P : (j + 1) * P, :], in_=out_win[j % WINDOWS][:])
+        def scatter_block(b, acc):
+            dw = keep.tile([P, 2, P], F32, name="dw_block%d" % b, tag=("dw_then_window", "dw_block")[b])
+            for side in range(2):
+                nc.scalar.copy(out=dw[:, side, :], in_=acc[:, CHUNK + side * P : CHUNK + (side + 1) * P])
+                place = out_win[0][:].indirect(slots(side * HALF + b * P, P))
+                nc.vector.tensor_tensor(out=place, in0=dw[:, side, :], in1=zeros[:], op=ALU.add)
 
-        order = ((0, 0), (1, 0), (0, 1), (2, 0), (1, 1), (2, 1))
+        def store(j):
+            nc.sync.dma_start(out=out[j * P : (j + 1) * P, :], in_=out_win[j][:])
 
         words = gradients_by_vector(0)
         interleave(xm_grouped[0][:], xm_raw[0][:])
-        h_first = keep.tile([P, 2 * CHUNK, PACK], BF16, name="h_first", tag="h_then_window", align_bytes=64)
+        h_first = keep.tile([P, 2 * CHUNK, PACK], BF16, name="h_first", align_bytes=64)
         gradient_operand(0, words, h_first, P)
         quantize_xm(0)
         gather_second(1)
@@ -331,26 +355,35 @@ def tile_attend_gbpr_w_ts_kernel(tc, xT, wT, wt, ts, xm, offs, out):
         quantize(w_codes[1], w_scales[1], w_got[1], 0, 2 * CHUNK, E4M3)
         interleave(xm_grouped[1][:], xm_raw[1][:])
         quantize_xm(1)
-        out_win[2] = keep.tile([P, T], F32, name="out_win2", tag="h_then_window", align_bytes=64)
-        nc.gpsimd.memset(out_win[2][:].bitcast(U32), 0)
-        acc = [table_sums(0, j, ps_b.tile([P, 2 * CHUNK], F32, name="late")) for j in range(2)]
-        acc.append(table_sums(0, 2, ps_w.tile([P, 2 * CHUNK], F32, name="wt_ps")))
-        for j, side in order[:-1]:
+        early_acc = ps_b.tile([P, 2 * CHUNK], F32, name="late")
+        scatter_block(0, table_sums(padded_codes[:, 0 : 2 * CHUNK], padded_scales[:, 0 : 2 * CHUNK], 0, early_acc))
+        out_win[3] = keep.tile([P, T], F32, name="out_win3", tag="dw_then_window")
+        clear(out_win[3])
+        acc = {}
+        acc[1] = table_sums(h_codes[0], h_scales[0], 1, ps_b.tile([P, 2 * CHUNK], F32, name="late"))
+        scatter(0, 1, 0, acc[1], sums.tile([P, CHUNK], F32, name="dw"))
+        acc[0] = table_sums(h_codes[0], h_scales[0], 0, ps_b.tile([P, 2 * CHUNK], F32, name="late"))
+        acc[2] = table_sums(h_codes[0], h_scales[0], 2, ps_w.tile([P, 2 * CHUNK], F32, name="wt_ps"))
+        scatter_block(1, acc[0])
+        scatter(0, 1, 1, acc[1], sums.tile([P, CHUNK], F32, name="dw"))
+        acc[3] = table_sums(h_codes[0], h_scales[0], 3, ps_b.tile([P, 2 * CHUNK], F32, name="late"))
+        middle = keep.tile([P, 2, CHUNK], F32, name="middle")
+        for j, side in ((2, 0), (3, 0)):
             scatter(0, j, side, acc[j], sums.tile([P, CHUNK], F32, name="dw"))
+        copy_side(middle[:, 1, :], acc[3], 1)
         words = gradients_by_scalar(1)
         h_second = keep.tile([P, 2 * CHUNK, PACK], BF16, name="h_second", align_bytes=64)
         gradient_operand(1, words, h_second, 2 * CHUNK)
         scatter(0, 2, 1, acc[2], keep.tile([P, CHUNK], F32, name="dw_held", tag="h1_1_1"))
-        acc = [table_sums(1, j, ps_b.tile([P, 2 * CHUNK], F32, name="late")) for j in range(WINDOWS)]
-        for j, side in order:
+        acc = {}
+        for j, side in ((0, 0), (1, 0), (0, 1), (2, 0), (1, 1), (3, 1), (2, 1)):
+            if j not in acc:
+                acc[j] = table_sums(h_codes[1], h_scales[1], j, ps_a.tile([P, 2 * CHUNK], F32, name="acc"))
             scatter(1, j, side, acc[j], sums.tile([P, CHUNK], F32, name="dw"))
-            if side == 1:
+            if side == 1 and j < 3:
                 store(j)
-        dw_last = keep.tile([P, 2, 2, CHUNK], F32, name="dw_last")
-        for c in range(2):
-            last = table_sums(c, 3, ps_a.tile([P, 2 * CHUNK], F32, name="acc"))
-            nc.scalar.copy(out=dw_last[:, :, c, :], in_=last[:].rearrange("p (s n) -> p s n", s=2))
+        copy_side(middle[:, 0, :], acc[3], 0)
         nc.vector.tensor_copy(
-            out=out_win[3 % WINDOWS][:].indirect(offsets[:]), in_=dw_last[:].rearrange("p s c n -> p (s c n)")
+            out=out_win[3][:].indirect(slots(CHUNK, HALF)), in_=middle[:].rearrange("p s n -> p (s n)")
         )
         store(3)

@@ -20,7 +20,6 @@ N, T, D, R = 1024, 2048, 512, 512
 HALF = N // 2
 CHUNK = 256
 WINDOWS = 4
-CLEAR = 512
 W_LOADS = ((0, 0, 1024, 0), (0, 1024, 512, 512), (0, 1536, 512, 384), (1, 0, 1024, 0), (1, 1024, 512, 512), (1, 1536, 512, 384))
 FLOPS = 2 * 2 * N * D * R
 
@@ -72,17 +71,14 @@ def tile_attend_gbpr_w_ts_kernel(tc, xT, wT, wt, ts, xm, offs, out):
             nc.sync.dma_start(out=xm_raw[k][:], in_=xm_rows[:, :, k * (D // 2) : (k + 1) * (D // 2)])
 
         out_win = {}
-
-        def clear(window):
-            for first in range(0, T, CLEAR):
-                nc.gpsimd.memset(window[:, first : first + CLEAR].bitcast(U32), 0)
-
-        for j in range(WINDOWS - 1):
+        for j in (1, 2):
             out_win[j] = keep.tile([P, T], F32, name="out_win%d" % j)
-            clear(out_win[j])
+            nc.gpsimd.memset(out_win[j][:].bitcast(U32), 0)
 
         ts_got = keep.tile([P, N], F32, name="ts_got")
         nc.vector.tensor_copy(out=ts_got[:], in_=ts_win[:].indirect(offsets[:]))
+        out_win[0] = keep.tile([P, T], F32, name="out_win0", tag="ts_win")
+        nc.vector.memset(out_win[0][:].bitcast(U32), 0)
         ts_ps = []
         for side in range(2):
             ts_ps.append(ps_a.tile([P, 4, P], F32, name="acc"))
@@ -334,12 +330,18 @@ def tile_attend_gbpr_w_ts_kernel(tc, xT, wT, wt, ts, xm, offs, out):
             copy_side(dw[:], acc, side)
             nc.vector.tensor_copy(out=out_win[j][:].indirect(slots(side * HALF + c * CHUNK, CHUNK)), in_=dw[:])
 
-        def scatter_block(b, acc):
-            dw = keep.tile([P, 2, P], F32, name="dw_block%d" % b, tag=("dw_then_window", "dw_block")[b])
+        def scatter_block(b, codes, scales):
+            dw = []
+            for j in range(2):
+                acc = table_sums(codes, scales, j, ps_b.tile([P, 2 * CHUNK], F32, name="late"))
+                dw.append(keep.tile([P, CHUNK], F32, name="dw_block%d_%d" % (b, j)))
+                nc.scalar.copy(out=dw[j][:], in_=acc[:, CHUNK:])
             for side in range(2):
-                nc.scalar.copy(out=dw[:, side, :], in_=acc[:, CHUNK + side * P : CHUNK + (side + 1) * P])
-                place = out_win[0][:].indirect(slots(side * HALF + b * P, P))
-                nc.vector.tensor_tensor(out=place, in0=dw[:, side, :], in1=zeros[:], op=ALU.add)
+                for j in range(2):
+                    place = out_win[j][:].indirect(slots(side * HALF + b * P, P))
+                    nc.vector.tensor_tensor(
+                        out=place, in0=dw[j][:, side * P : (side + 1) * P], in1=zeros[:], op=ALU.add
+                    )
 
         def store(j):
             nc.sync.dma_start(out=out[j * P : (j + 1) * P, :], in_=out_win[j][:])
@@ -355,17 +357,11 @@ def tile_attend_gbpr_w_ts_kernel(tc, xT, wT, wt, ts, xm, offs, out):
         quantize(w_codes[1], w_scales[1], w_got[1], 0, 2 * CHUNK, E4M3)
         interleave(xm_grouped[1][:], xm_raw[1][:])
         quantize_xm(1)
-        early_acc = ps_b.tile([P, 2 * CHUNK], F32, name="late")
-        scatter_block(0, table_sums(padded_codes[:, 0 : 2 * CHUNK], padded_scales[:, 0 : 2 * CHUNK], 0, early_acc))
-        out_win[3] = keep.tile([P, T], F32, name="out_win3", tag="dw_then_window")
-        clear(out_win[3])
-        acc = {}
-        acc[1] = table_sums(h_codes[0], h_scales[0], 1, ps_b.tile([P, 2 * CHUNK], F32, name="late"))
-        scatter(0, 1, 0, acc[1], sums.tile([P, CHUNK], F32, name="dw"))
-        acc[0] = table_sums(h_codes[0], h_scales[0], 0, ps_b.tile([P, 2 * CHUNK], F32, name="late"))
-        acc[2] = table_sums(h_codes[0], h_scales[0], 2, ps_w.tile([P, 2 * CHUNK], F32, name="wt_ps"))
-        scatter_block(1, acc[0])
-        scatter(0, 1, 1, acc[1], sums.tile([P, CHUNK], F32, name="dw"))
+        scatter_block(0, padded_codes[:, 0 : 2 * CHUNK], padded_scales[:, 0 : 2 * CHUNK])
+        out_win[3] = keep.tile([P, T], F32, name="out_win3", tag="dw_block0_0")
+        nc.gpsimd.memset(out_win[3][:].bitcast(U32), 0)
+        scatter_block(1, h_codes[0], h_scales[0])
+        acc = {2: table_sums(h_codes[0], h_scales[0], 2, ps_w.tile([P, 2 * CHUNK], F32, name="wt_ps"))}
         acc[3] = table_sums(h_codes[0], h_scales[0], 3, ps_b.tile([P, 2 * CHUNK], F32, name="late"))
         middle = keep.tile([P, 2, CHUNK], F32, name="middle")
         for j, side in ((2, 0), (3, 0)):

@@ -89,7 +89,8 @@ def tile_attend_gbpr_w_ts_kernel(tc, xT, wT, wt, ts, xm, offs, out):
         wt_ps = ps_w.tile([P, PACK, P], F32, name="wt_ps")
         for t in range(PACK):
             nc.tensor.transpose(wt_ps[:, t, :], wt_cols[:, t : t + 1].to_broadcast([P, P]), ident[:])
-        wt_row = wt_ps[:].rearrange("p t m -> p m t")
+        wt_row = keep.tile([P, 2, P, 2], F32, name="wt_row")
+        nc.scalar.copy(out=wt_row[:], in_=wt_ps[:].rearrange("p (u e) m -> p u m e", u=2))
 
         w_pair = [keep.tile([P, T, 2], BF16, name="w_pair%d" % u) for u in range(2)]
         w_got, w_codes, w_scales = [], [], []
@@ -235,19 +236,23 @@ def tile_attend_gbpr_w_ts_kernel(tc, xT, wT, wt, ts, xm, offs, out):
                 )
             for b in blocks:
                 sig[b] = keep.tile([P, R], F32, name="sig%d" % b, align_bytes=64)
-                nc.scalar.activation(out=sig[b][:], in_=margin[b][:], func=ACT.Sigmoid)
+                nc.scalar.activation(
+                    out=sig[b][:].rearrange("p (u m e) -> p u m e", u=2, e=2),
+                    in_=margin[b][:].rearrange("p (m u e) -> p u m e", u=2, e=2),
+                    func=ACT.Sigmoid,
+                )
             for b in blocks:
                 for side in range(2):
                     h[b, side] = keep.tile([P, R], BF16, name="h%d_%d_%d" % (c, b, side))
                     nc.vector.scalar_tensor_tensor(
-                        out=h[b, side][:].rearrange("p (m t) -> p m t", t=PACK),
-                        in0=sig[b][:].rearrange("p (m t) -> p m t", t=PACK),
+                        out=h[b, side][:],
+                        in0=sig[b][:],
                         scalar=scale_of(c, b, side),
-                        in1=wt_row,
+                        in1=wt_row[:].rearrange("p u m e -> p (u m e)"),
                         op0=ALU.mult,
                         op1=ALU.mult,
                     )
-            return {key: tile[:].bitcast(F32).rearrange("p (m u) -> p u m", u=2) for key, tile in h.items()}
+            return {key: tile[:].bitcast(F32).rearrange("p (u m) -> p u m", u=2) for key, tile in h.items()}
 
         def gradients_by_scalar(c):
             score = scores(c)
@@ -361,25 +366,18 @@ def tile_attend_gbpr_w_ts_kernel(tc, xT, wT, wt, ts, xm, offs, out):
         out_win[3] = keep.tile([P, T], F32, name="out_win3", tag="dw_block0_0")
         nc.gpsimd.memset(out_win[3][:].bitcast(U32), 0)
         scatter_block(1, h_codes[0], h_scales[0])
-        acc = {2: table_sums(h_codes[0], h_scales[0], 2, ps_w.tile([P, 2 * CHUNK], F32, name="wt_ps"))}
-        acc[3] = table_sums(h_codes[0], h_scales[0], 3, ps_b.tile([P, 2 * CHUNK], F32, name="late"))
-        middle = keep.tile([P, 2, CHUNK], F32, name="middle")
-        for j, side in ((2, 0), (3, 0)):
+        acc = {2: table_sums(h_codes[0], h_scales[0], 2, ps_b.tile([P, 2 * CHUNK], F32, name="late"))}
+        acc[3] = table_sums(h_codes[0], h_scales[0], 3, ps_w.tile([P, 2 * CHUNK], F32, name="wt_ps"))
+        for j, side in ((2, 0), (3, 0), (2, 1)):
             scatter(0, j, side, acc[j], sums.tile([P, CHUNK], F32, name="dw"))
-        copy_side(middle[:, 1, :], acc[3], 1)
         words = gradients_by_scalar(1)
         h_second = keep.tile([P, 2 * CHUNK, PACK], BF16, name="h_second", align_bytes=64)
         gradient_operand(1, words, h_second, 2 * CHUNK)
-        scatter(0, 2, 1, acc[2], keep.tile([P, CHUNK], F32, name="dw_held", tag="h1_1_1"))
+        scatter(0, 3, 1, acc[3], keep.tile([P, CHUNK], F32, name="dw_held", tag="h1_1_1"))
         acc = {}
-        for j, side in ((0, 0), (1, 0), (0, 1), (2, 0), (1, 1), (3, 1), (2, 1)):
+        for j, side in ((0, 0), (1, 0), (0, 1), (2, 0), (1, 1), (2, 1), (3, 0), (3, 1)):
             if j not in acc:
                 acc[j] = table_sums(h_codes[1], h_scales[1], j, ps_a.tile([P, 2 * CHUNK], F32, name="acc"))
             scatter(1, j, side, acc[j], sums.tile([P, CHUNK], F32, name="dw"))
-            if side == 1 and j < 3:
+            if side == 1:
                 store(j)
-        copy_side(middle[:, 0, :], acc[3], 0)
-        nc.vector.tensor_copy(
-            out=out_win[3][:].indirect(slots(CHUNK, HALF)), in_=middle[:].rearrange("p s n -> p (s n)")
-        )
-        store(3)

@@ -21,6 +21,7 @@ HALF = N // 2
 CHUNK = 256
 WINDOWS = 4
 W_LOADS = ((0, 0, 1024, 0), (0, 1024, 512, 512), (0, 1536, 512, 384), (1, 0, 1024, 0), (1, 1024, 512, 512), (1, 1536, 512, 384))
+PAD = 384
 FLOPS = 2 * 2 * N * D * R
 
 
@@ -189,14 +190,14 @@ def tile_attend_gbpr_w_ts_kernel(tc, xT, wT, wt, ts, xm, offs, out):
             )
 
         blocks = range(CHUNK // P)
-        padded_codes = keep.tile([P, 3 * CHUNK], U32, name="padded_codes", align_bytes=64)
-        padded_scales = keep.tile([P, 3 * CHUNK], U8, name="padded_scales", align_bytes=64)
-        nc.gpsimd.memset(padded_codes[:, 0:CHUNK], 0)
-        nc.gpsimd.memset(padded_scales[:, 0:CHUNK].bitcast(U32), 0)
+        padded_codes = keep.tile([P, PAD + 2 * CHUNK], U32, name="padded_codes", align_bytes=64)
+        padded_scales = keep.tile([P, PAD + 2 * CHUNK], U8, name="padded_scales", align_bytes=64)
+        nc.gpsimd.memset(padded_codes[:, 0:PAD], 0)
+        nc.gpsimd.memset(padded_scales[:, 0:PAD].bitcast(U32), 0)
         zeros = keep.tile([P, P], F32, name="zeros")
         nc.gpsimd.memset(zeros[:], 0.0)
-        h_codes = [padded_codes[:, CHUNK:], keep.tile([P, 2 * CHUNK], U32, name="h_codes1", align_bytes=64)[:]]
-        h_scales = [padded_scales[:, CHUNK:], keep.tile([P, 2 * CHUNK], U8, name="h_scales1", align_bytes=64)[:]]
+        h_codes = [padded_codes[:, PAD:], keep.tile([P, 2 * CHUNK], U32, name="h_codes1", align_bytes=64)[:]]
+        h_scales = [padded_scales[:, PAD:], keep.tile([P, 2 * CHUNK], U8, name="h_scales1", align_bytes=64)[:]]
 
         def scores(c):
             score = {}
@@ -362,8 +363,15 @@ def tile_attend_gbpr_w_ts_kernel(tc, xT, wT, wt, ts, xm, offs, out):
         quantize(w_codes[1], w_scales[1], w_got[1], 0, 2 * CHUNK, E4M3)
         interleave(xm_grouped[1][:], xm_raw[1][:])
         quantize_xm(1)
-        scatter_block(0, padded_codes[:, 0 : 2 * CHUNK], padded_scales[:, 0 : 2 * CHUNK])
-        out_win[3] = keep.tile([P, T], F32, name="out_win3", tag="dw_block0_0")
+        for side in range(2):
+            cols = slice(side * P, side * P + 2 * CHUNK)
+            for j in range(2):
+                ahead = table_sums(padded_codes[:, cols], padded_scales[:, cols], j, ps_b.tile([P, 2 * CHUNK], F32, name="late"))
+                dw = keep.tile([P, P], F32, name="dw_ahead%d_%d" % (side, j))
+                nc.scalar.copy(out=dw[:], in_=ahead[:, PAD:])
+                place = out_win[j][:].indirect(slots(side * HALF, P))
+                nc.vector.tensor_tensor(out=place, in0=dw[:], in1=zeros[:], op=ALU.add)
+        out_win[3] = keep.tile([P, T], F32, name="out_win3", tag="dw_ahead1_0")
         nc.gpsimd.memset(out_win[3][:].bitcast(U32), 0)
         scatter_block(1, h_codes[0], h_scales[0])
         acc = {2: table_sums(h_codes[0], h_scales[0], 2, ps_b.tile([P, 2 * CHUNK], F32, name="late"))}

@@ -20,7 +20,7 @@ N, T, D, R = 1024, 2048, 512, 512
 HALF = N // 2
 CHUNK = 256
 WINDOWS = 4
-W_LOADS = ((0, 0, 1024, 0), (0, 1024, 512, 512), (0, 1536, 512, 384), (1, 0, 1024, 0), (1, 1024, 512, 512), (1, 1536, 512, 384))
+W_LOADS = ((0, 0, 1024, 0), (0, 1024, 512, 512), (0, 1536, 512, 128), (1, 0, 1024, 0), (1, 1024, 512, 512), (1, 1536, 512, 256))
 PAD = 384
 FLOPS = 2 * 2 * N * D * R
 
@@ -39,13 +39,15 @@ def tile_attend_gbpr_w_ts_kernel(tc, xT, wT, wt, ts, xm, offs, out):
         def slots(first, count):
             return offsets[:, first // 16 : (first + count) // 16]
 
-        ts_win = keep.tile([P, T], F32, name="ts_win")
-        nc.sync.dma_start(out=ts_win[P - 1 : P, :], in_=ts[0:1, :])
+        seed = keep.tile([P, 1], F32, name="seed")
+        nc.vector.memset(seed[:], 0.0)
+        ts_win = keep.tile([P, T + 1], F32, name="ts_win")
+        nc.sync.dma_start(out=ts_win[P - 1 : P, 0:T], in_=ts[0:1, :])
         nc.vector.memset(ts_win[0 : P - 1, :].bitcast(U32), 0)
         ident = keep.tile([P, P], F32, name="ident")
         make_identity(nc, ident[:])
         warm = keep.tile([P, 1], F32, name="warm")
-        nc.scalar.activation(out=warm[:], in_=ident[:, 0:1], func=ACT.Sigmoid)
+        nc.scalar.activation(out=warm[:], in_=seed[:], func=ACT.Sigmoid)
 
         offsets = keep.tile([P, N // 16], U16, name="offsets")
         nc.sync.dma_start(offsets[:], offs)
@@ -77,7 +79,7 @@ def tile_attend_gbpr_w_ts_kernel(tc, xT, wT, wt, ts, xm, offs, out):
             nc.gpsimd.memset(out_win[j][:].bitcast(U32), 0)
 
         ts_got = keep.tile([P, N], F32, name="ts_got")
-        nc.vector.tensor_copy(out=ts_got[:], in_=ts_win[:].indirect(offsets[:]))
+        nc.vector.tensor_copy(out=ts_got[:], in_=ts_win[:, 0:T].indirect(offsets[:]))
         out_win[0] = keep.tile([P, T], F32, name="out_win0", tag="ts_win")
         nc.vector.memset(out_win[0][:].bitcast(U32), 0)
         ts_ps = []
@@ -103,8 +105,8 @@ def tile_attend_gbpr_w_ts_kernel(tc, xT, wT, wt, ts, xm, offs, out):
 
         def cast(k, lo, hi, on_vector):
             u, first = W_LOADS[k][0:2]
-            dst = w_pair[u][:, first + lo : first + hi, :]
-            src = w_raw[k][:, :, lo:hi].rearrange("p e c -> p c e")
+            dst = w_pair[u][:, first + lo : first + hi, :].rearrange("p (c i) e -> p c e i", i=4)
+            src = w_raw[k][:, :, lo:hi].rearrange("p e (c i) -> p c e i", i=4)
             if on_vector:
                 nc.vector.tensor_copy(out=dst, in_=src)
             else:
@@ -371,9 +373,9 @@ def tile_attend_gbpr_w_ts_kernel(tc, xT, wT, wt, ts, xm, offs, out):
                 nc.scalar.copy(out=dw[:], in_=ahead[:, PAD:])
                 place = out_win[j][:].indirect(slots(side * HALF, P))
                 nc.vector.tensor_tensor(out=place, in0=dw[:], in1=zeros[:], op=ALU.add)
-        out_win[3] = keep.tile([P, T], F32, name="out_win3", tag="dw_ahead1_0")
-        nc.gpsimd.memset(out_win[3][:].bitcast(U32), 0)
         scatter_block(1, h_codes[0], h_scales[0])
+        out_win[3] = keep.tile([P, T], F32, name="out_win3", tag="dw_block1_0")
+        nc.gpsimd.memset(out_win[3][:].bitcast(U32), 0)
         acc = {2: table_sums(h_codes[0], h_scales[0], 2, ps_b.tile([P, 2 * CHUNK], F32, name="late"))}
         acc[3] = table_sums(h_codes[0], h_scales[0], 3, ps_w.tile([P, 2 * CHUNK], F32, name="wt_ps"))
         for j, side in ((2, 0), (3, 0), (2, 1)):

@@ -21,7 +21,6 @@ HALF = N // 2
 CHUNK = 256
 WINDOWS = 4
 W_LOADS = ((0, 0, 1024, 0), (0, 1024, 512, 512), (0, 1536, 512, 128), (1, 0, 1024, 0), (1, 1024, 512, 512), (1, 1536, 512, 256))
-PAD = 384
 FLOPS = 2 * 2 * N * D * R
 
 
@@ -30,11 +29,10 @@ def tile_attend_gbpr_w_ts_kernel(tc, xT, wT, wt, ts, xm, offs, out):
     with ExitStack() as ctx:
         keep = ctx.enter_context(tc.tile_pool(name="keep", bufs=1))
         ring = ctx.enter_context(tc.tile_pool(name="ring", bufs=2))
-        sums = ctx.enter_context(tc.tile_pool(name="sums", bufs=16))
         early = ctx.enter_context(tc.tile_pool(name="early", bufs=1))
         ps_a = ctx.enter_context(tc.psum_pool(name="ps_a", bufs=4))
-        ps_b = ctx.enter_context(tc.psum_pool(name="ps_b", bufs=3))
-        ps_w = ctx.enter_context(tc.psum_pool(name="ps_w", bufs=1))
+        ps_b = ctx.enter_context(tc.psum_pool(name="ps_b", bufs=2))
+        ps_w = ctx.enter_context(tc.psum_pool(name="ps_w", bufs=2))
 
         def slots(first, count):
             return offsets[:, first // 16 : (first + count) // 16]
@@ -89,7 +87,7 @@ def tile_attend_gbpr_w_ts_kernel(tc, xT, wT, wt, ts, xm, offs, out):
                 first = side * HALF + b * P
                 nc.tensor.transpose(ts_ps[side][:, b, :], ts_got[:, first : first + P], ident[:])
 
-        wt_ps = ps_w.tile([P, PACK, P], F32, name="wt_ps")
+        wt_ps = ps_w.tile([P, PACK, P], F32, name="sum")
         for t in range(PACK):
             nc.tensor.transpose(wt_ps[:, t, :], wt_cols[:, t : t + 1].to_broadcast([P, P]), ident[:])
         wt_row = keep.tile([P, 2, P, 2], F32, name="wt_row")
@@ -192,17 +190,18 @@ def tile_attend_gbpr_w_ts_kernel(tc, xT, wT, wt, ts, xm, offs, out):
             )
 
         blocks = range(CHUNK // P)
-        padded_codes = keep.tile([P, PAD + 2 * CHUNK], U32, name="padded_codes", align_bytes=64)
-        padded_scales = keep.tile([P, PAD + 2 * CHUNK], U8, name="padded_scales", align_bytes=64)
-        nc.gpsimd.memset(padded_codes[:, 0:PAD], 0)
-        nc.gpsimd.memset(padded_scales[:, 0:PAD].bitcast(U32), 0)
-        zeros = keep.tile([P, P], F32, name="zeros")
-        nc.gpsimd.memset(zeros[:], 0.0)
-        h_codes = [padded_codes[:, PAD:], keep.tile([P, 2 * CHUNK], U32, name="h_codes1", align_bytes=64)[:]]
-        h_scales = [padded_scales[:, PAD:], keep.tile([P, 2 * CHUNK], U8, name="h_scales1", align_bytes=64)[:]]
+        h_grouped, h_codes, h_scales = [], [], []
+        for c in range(2):
+            h_grouped.append(keep.tile([P, 2 * CHUNK, PACK], BF16, name="h_grouped%d" % c, align_bytes=64))
+            h_codes.append(keep.tile([P, 2 * CHUNK], U32, name="h_codes%d" % c, align_bytes=64))
+            h_scales.append(keep.tile([P, 2 * CHUNK], U8, name="h_scales%d" % c, align_bytes=64))
 
-        def scores(c):
-            score = {}
+        def scale_of(c, b, side):
+            col = c * (CHUNK // P) + b
+            return ts_col[side][:, col : col + 1]
+
+        def sigmoids(c):
+            score, margin, sig = {}, {}, {}
             for b in blocks:
                 for side in range(2):
                     first = side * CHUNK + b * P
@@ -216,15 +215,6 @@ def tile_attend_gbpr_w_ts_kernel(tc, xT, wT, wt, ts, xm, offs, out):
                         start=True,
                         stop=True,
                     )
-            return score
-
-        def scale_of(c, b, side):
-            col = c * (CHUNK // P) + b
-            return ts_col[side][:, col : col + 1]
-
-        def gradients_by_vector(c):
-            score = scores(c)
-            margin, sig, h = {}, {}, {}
             for b in blocks:
                 neg_pos = ring.tile([P, R], F32, name="neg_pos")
                 nc.scalar.activation(out=neg_pos[:], in_=score[b, 0][:], func=ACT.Copy, scale=scale_of(c, b, 0))
@@ -238,156 +228,99 @@ def tile_attend_gbpr_w_ts_kernel(tc, xT, wT, wt, ts, xm, offs, out):
                     op1=ALU.add,
                 )
             for b in blocks:
-                sig[b] = keep.tile([P, R], F32, name="sig%d" % b, align_bytes=64)
+                sig[b] = keep.tile([P, R], F32, name="sig%d" % (2 * c + b))
                 nc.scalar.activation(
                     out=sig[b][:].rearrange("p (u m e) -> p u m e", u=2, e=2),
                     in_=margin[b][:].rearrange("p (m u e) -> p u m e", u=2, e=2),
                     func=ACT.Sigmoid,
                 )
+            return sig
+
+        def gradients(c, sig):
+            h_words = h_grouped[c][:].rearrange("p n t -> p (n t)").bitcast(F32).rearrange("p (n u) -> p n u", u=2)
             for b in blocks:
+                bank = ps_b.tile([P, 2, 2, P], F32, name="late")
                 for side in range(2):
-                    h[b, side] = keep.tile([P, R], BF16, name="h%d_%d_%d" % (c, b, side))
+                    h = ring.tile([P, R], BF16, name="h%d" % side)
                     nc.vector.scalar_tensor_tensor(
-                        out=h[b, side][:],
+                        out=h[:],
                         in0=sig[b][:],
                         scalar=scale_of(c, b, side),
                         in1=wt_row[:].rearrange("p u m e -> p (u m e)"),
                         op0=ALU.mult,
                         op1=ALU.mult,
                     )
-            return {key: tile[:].bitcast(F32).rearrange("p (u m) -> p u m", u=2) for key, tile in h.items()}
-
-        def gradients_by_scalar(c):
-            score = scores(c)
-            h = {}
-            for b in blocks:
-                scaled = []
-                for side in range(2):
-                    scaled.append(ring.tile([P, PACK, P], F32, name="scaled%d" % side))
-                    nc.scalar.activation(
-                        out=scaled[side][:],
-                        in_=score[b, side][:].rearrange("p (m t) -> p t m", t=PACK),
-                        func=ACT.Copy,
-                        scale=scale_of(c, b, side),
-                    )
-                margin = ps_a.tile([P, PACK, P], F32, name="acc")
-                for t in range(PACK):
-                    for side in range(2):
-                        nc.tensor.matmul(
-                            margin[:, t, :],
-                            lhsT=scaled[side][:, t, :],
-                            rhs=ident[:],
-                            is_transpose=True,
-                            start=(side == 0),
-                            stop=(side == 1),
-                        )
-                sig = ring.tile([P, PACK, P], F32, name="sig")
-                nc.scalar.activation(out=sig[:], in_=margin[:], func=ACT.Sigmoid)
-                weighted = ring.tile([P, PACK, P], F32, name="weighted")
-                back = ps_a.tile([P, PACK, P], F32, name="acc")
-                for t in range(PACK):
-                    nc.scalar.activation(
-                        out=weighted[:, t, :], in_=sig[:, t, :], func=ACT.Copy, scale=wt_cols[:, t : t + 1]
-                    )
-                    nc.tensor.transpose(back[:, t, :], weighted[:, t, :], ident[:])
-                for side in range(2):
-                    h[b, side] = keep.tile([P, 2, P, 2], BF16, name="h%d_%d_%d" % (c, b, side))
-                    nc.scalar.activation(
-                        out=h[b, side][:],
-                        in_=back[:].rearrange("p (u e) m -> p u m e", u=2),
-                        func=ACT.Copy,
-                        scale=scale_of(c, b, side),
-                    )
-            return {
-                key: tile[:].rearrange("p u m e -> p (u m e)").bitcast(F32).rearrange("p (u m) -> p u m", u=2)
-                for key, tile in h.items()
-            }
-
-        def gradient_operand(c, words, h_grouped, width):
-            h_words = h_grouped[:].rearrange("p n t -> p (n t)").bitcast(F32).rearrange("p (n u) -> p n u", u=2)
-            for b in blocks:
-                for side in range(2):
-                    bank = ps_b.tile([P, R], F32, name="late")
-                    turned = bank[:, 0 : 2 * P].rearrange("p (u i) -> p u i", u=2)
+                    words = h[:].bitcast(F32).rearrange("p (u m) -> p u m", u=2)
                     for u in range(2):
-                        nc.tensor.transpose(turned[:, u, :], words[b, side][:, u, :], ident[:])
-                    first = (2 * b + side) * P
-                    nc.scalar.copy(out=h_words[:, first : first + P, :], in_=turned.rearrange("p u i -> p i u"))
-                    if width == P:
-                        quantize(h_codes[c], h_scales[c], h_grouped, first, P, E5M2)
-            if width > P:
-                quantize(h_codes[c], h_scales[c], h_grouped, 0, width, E5M2)
+                        nc.tensor.transpose(bank[:, side, u, :], words[:, u, :], ident[:])
+                first = 2 * b * P
+                nc.scalar.copy(
+                    out=h_words[:, first : first + 2 * P, :].rearrange("p (s i) u -> p s i u", s=2),
+                    in_=bank[:].rearrange("p s u i -> p s i u"),
+                )
+                quantize(h_codes[c], h_scales[c], h_grouped[c], first, 2 * P, E5M2)
 
-        def table_sums(codes, scales, j, acc):
+        dw = {j: keep.tile([P, N], F32, name="dw%d" % j)[:] for j in (0, 2)}
+
+        def table_sums(c, j, acc, on_vector):
             nc.tensor.matmul_mx(
                 out=acc[:],
                 lhsT=xm_codes[:, j * P : (j + 1) * P].bitcast(E4M3),
                 lhsT_scale=xm_scales[:, j * P : (j + 1) * P],
-                rhs=codes.bitcast(E5M2),
-                rhs_scale=scales,
+                rhs=h_codes[c][:].bitcast(E5M2),
+                rhs_scale=h_scales[c][:],
                 start=True,
                 stop=True,
             )
-            return acc
+            dst = dw[j].rearrange("p (s c b i) -> p s c b i", s=2, c=2, i=P)[:, :, c]
+            src = acc[:].rearrange("p (b s i) -> p s b i", s=2, i=P)
+            if on_vector:
+                nc.vector.tensor_copy(out=dst, in_=src)
+            else:
+                nc.scalar.copy(out=dst, in_=src)
 
-        def copy_side(dw, acc, side):
-            sums_of_side = acc[:].rearrange("p (b s i) -> p s b i", s=2, i=P)[:, side]
-            nc.scalar.copy(out=dw.rearrange("p (b i) -> p b i", i=P), in_=sums_of_side)
-
-        def scatter(c, j, side, acc, dw):
-            copy_side(dw[:], acc, side)
-            nc.vector.tensor_copy(out=out_win[j][:].indirect(slots(side * HALF + c * CHUNK, CHUNK)), in_=dw[:])
-
-        def scatter_block(b, codes, scales):
-            dw = []
-            for j in range(2):
-                acc = table_sums(codes, scales, j, ps_b.tile([P, 2 * CHUNK], F32, name="late"))
-                dw.append(keep.tile([P, CHUNK], F32, name="dw_block%d_%d" % (b, j)))
-                nc.scalar.copy(out=dw[j][:], in_=acc[:, CHUNK:])
-            for side in range(2):
-                for j in range(2):
-                    place = out_win[j][:].indirect(slots(side * HALF + b * P, P))
-                    nc.vector.tensor_tensor(
-                        out=place, in0=dw[j][:, side * P : (side + 1) * P], in1=zeros[:], op=ALU.add
-                    )
+        def scatter(j, first, count):
+            place = out_win[j][:].indirect(slots(first, count))
+            if j % 2 == 0:
+                nc.vector.tensor_copy(out=place, in_=dw[j][:, first : first + count])
+            else:
+                nc.scalar.activation(out=place, in_=dw[j][:, first : first + count], func=ACT.Copy)
 
         def store(j):
             nc.sync.dma_start(out=out[j * P : (j + 1) * P, :], in_=out_win[j][:])
 
-        words = gradients_by_vector(0)
+        sig = sigmoids(0)
         interleave(xm_grouped[0][:], xm_raw[0][:])
-        h_first = keep.tile([P, 2 * CHUNK, PACK], BF16, name="h_first", align_bytes=64)
-        gradient_operand(0, words, h_first, P)
+        gradients(0, sig)
+        out_win[3] = keep.tile([P, T], F32, name="out_win3", tag="h_grouped0", align_bytes=64)
+        nc.gpsimd.memset(out_win[3][:].bitcast(U32), 0)
         quantize_xm(0)
         gather_second(1)
         weave(1)
         w_codes.append(keep.tile([P, 2 * CHUNK], U32, name="w_codes1", align_bytes=64))
         quantize(w_codes[1], w_scales[1], w_got[1], 0, 2 * CHUNK, E4M3)
+        sig = sigmoids(1)
         interleave(xm_grouped[1][:], xm_raw[1][:])
         quantize_xm(1)
-        for side in range(2):
-            cols = slice(side * P, side * P + 2 * CHUNK)
-            for j in range(2):
-                ahead = table_sums(padded_codes[:, cols], padded_scales[:, cols], j, ps_b.tile([P, 2 * CHUNK], F32, name="late"))
-                dw = keep.tile([P, P], F32, name="dw_ahead%d_%d" % (side, j))
-                nc.scalar.copy(out=dw[:], in_=ahead[:, PAD:])
-                place = out_win[j][:].indirect(slots(side * HALF, P))
-                nc.vector.tensor_tensor(out=place, in0=dw[:], in1=zeros[:], op=ALU.add)
-        scatter_block(1, h_codes[0], h_scales[0])
-        out_win[3] = keep.tile([P, T], F32, name="out_win3", tag="dw_block1_0")
-        nc.gpsimd.memset(out_win[3][:].bitcast(U32), 0)
-        acc = {2: table_sums(h_codes[0], h_scales[0], 2, ps_b.tile([P, 2 * CHUNK], F32, name="late"))}
-        acc[3] = table_sums(h_codes[0], h_scales[0], 3, ps_w.tile([P, 2 * CHUNK], F32, name="wt_ps"))
-        for j, side in ((2, 0), (3, 0), (2, 1)):
-            scatter(0, j, side, acc[j], sums.tile([P, CHUNK], F32, name="dw"))
-        words = gradients_by_scalar(1)
-        h_second = keep.tile([P, 2 * CHUNK, PACK], BF16, name="h_second", align_bytes=64)
-        gradient_operand(1, words, h_second, 2 * CHUNK)
-        scatter(0, 3, 1, acc[3], keep.tile([P, CHUNK], F32, name="dw_held", tag="h1_1_1"))
-        acc = {}
-        for j, side in ((0, 0), (1, 0), (0, 1), (2, 0), (1, 1), (2, 1), (3, 0), (3, 1)):
-            if j not in acc:
-                acc[j] = table_sums(h_codes[1], h_scales[1], j, ps_a.tile([P, 2 * CHUNK], F32, name="acc"))
-            scatter(1, j, side, acc[j], sums.tile([P, CHUNK], F32, name="dw"))
-            if side == 1:
-                store(j)
+        gradients(1, sig)
+        dw_odd = keep.tile([P, 2, N], F32, name="dw_odd", tag="sig3")
+        dw[1], dw[3] = dw_odd[:, 0, :], dw_odd[:, 1, :]
+        for j in (1, 3):
+            table_sums(0, j, ps_w.tile([P, 2 * CHUNK], F32, name="sum"), True)
+        for j in (1, 3):
+            scatter(j, 0, CHUNK)
+        for j in (0, 2):
+            table_sums(0, j, ps_a.tile([P, 2 * CHUNK], F32, name="acc"), True)
+        table_sums(1, 0, ps_b.tile([P, 2 * CHUNK], F32, name="late"), True)
+        for j in (1, 3):
+            table_sums(1, j, ps_a.tile([P, 2 * CHUNK], F32, name="acc"), False)
+        scatter(0, 0, N)
+        store(0)
+        table_sums(1, 2, ps_b.tile([P, 2 * CHUNK], F32, name="late"), True)
+        for first in (CHUNK, CHUNK + 384):
+            for j in (1, 3):
+                scatter(j, first, 384)
+        store(1)
+        store(3)
+        scatter(2, 0, N)
+        store(2)

@@ -19,8 +19,16 @@ PACK = 4
 N, T, D, R = 1024, 2048, 512, 512
 HALF = N // 2
 CHUNK = 256
-WINDOWS = 4
-W_LOADS = ((0, 0, 1024, 0), (0, 1024, 512, 512), (0, 1536, 512, 128), (1, 0, 1024, 0), (1, 1024, 512, 512), (1, 1536, 512, 256))
+W_LOADS = (
+    (0, 0, 1024, 1024),
+    (0, 1024, 512, 512),
+    (0, 1536, 512, 320),
+    (1, 0, 512, 0),
+    (1, 512, 512, 0),
+    (1, 1024, 512, 512),
+    (1, 1536, 512, 320),
+)
+WIDE = 384
 FLOPS = 2 * 2 * N * D * R
 
 
@@ -30,6 +38,7 @@ def tile_attend_gbpr_w_ts_kernel(tc, xT, wT, wt, ts, xm, offs, out):
         keep = ctx.enter_context(tc.tile_pool(name="keep", bufs=1))
         ring = ctx.enter_context(tc.tile_pool(name="ring", bufs=2))
         early = ctx.enter_context(tc.tile_pool(name="early", bufs=1))
+        tail = ctx.enter_context(tc.tile_pool(name="tail", bufs=1))
         ps_a = ctx.enter_context(tc.psum_pool(name="ps_a", bufs=4))
         ps_b = ctx.enter_context(tc.psum_pool(name="ps_b", bufs=2))
         ps_w = ctx.enter_context(tc.psum_pool(name="ps_w", bufs=2))
@@ -39,9 +48,9 @@ def tile_attend_gbpr_w_ts_kernel(tc, xT, wT, wt, ts, xm, offs, out):
 
         seed = keep.tile([P, 1], F32, name="seed")
         nc.vector.memset(seed[:], 0.0)
-        ts_win = keep.tile([P, T + 1], F32, name="ts_win")
-        nc.sync.dma_start(out=ts_win[P - 1 : P, 0:T], in_=ts[0:1, :])
-        nc.vector.memset(ts_win[0 : P - 1, :].bitcast(U32), 0)
+        ts_win = keep.tile([P, T], F32, name="ts_win")
+        nc.sync.dma_start(out=ts_win[P - 1 : P, :], in_=ts[0:1, :])
+        nc.gpsimd.memset(ts_win[0 : P - 1, :].bitcast(U32), 0)
         ident = keep.tile([P, P], F32, name="ident")
         make_identity(nc, ident[:])
         warm = keep.tile([P, 1], F32, name="warm")
@@ -53,8 +62,8 @@ def tile_attend_gbpr_w_ts_kernel(tc, xT, wT, wt, ts, xm, offs, out):
         w_rows = wT.rearrange("(p u e) c -> p u e c", u=2, e=2)
         w_raw = []
         for k, (u, first, count, on_vector) in enumerate(W_LOADS):
-            if k == 3:
-                w_raw.append(early.tile([P, 2, count], F32, name="w_raw3", offset=0))
+            if k == 2:
+                w_raw.append(early.tile([P, 2, count], F32, name="w_raw2", offset=0))
             else:
                 w_raw.append(keep.tile([P, 2, count], F32, name="w_raw%d" % k))
             nc.sync.dma_start(out=w_raw[k][:], in_=w_rows[:, u, :, first : first + count])
@@ -71,15 +80,13 @@ def tile_attend_gbpr_w_ts_kernel(tc, xT, wT, wt, ts, xm, offs, out):
             xm_raw.append(keep.tile([P, PACK, D // 2], F32, name="xm_raw%d" % k))
             nc.sync.dma_start(out=xm_raw[k][:], in_=xm_rows[:, :, k * (D // 2) : (k + 1) * (D // 2)])
 
-        out_win = {}
-        for j in (1, 2):
-            out_win[j] = keep.tile([P, T], F32, name="out_win%d" % j)
-            nc.gpsimd.memset(out_win[j][:].bitcast(U32), 0)
+        out_win = {j: keep.tile([P, T], F32, name="out_win%d" % j) for j in (0, 1)}
+        nc.vector.memset(out_win[0][:, 0 : T - 1].bitcast(U32), 0)
+        nc.vector.memset(out_win[0][:, T - 1 : T].bitcast(U32), 0)
+        nc.gpsimd.memset(out_win[1][:].bitcast(U32), 0)
 
         ts_got = keep.tile([P, N], F32, name="ts_got")
-        nc.vector.tensor_copy(out=ts_got[:], in_=ts_win[:, 0:T].indirect(offsets[:]))
-        out_win[0] = keep.tile([P, T], F32, name="out_win0", tag="ts_win")
-        nc.vector.memset(out_win[0][:].bitcast(U32), 0)
+        nc.vector.tensor_copy(out=ts_got[:], in_=ts_win[:].indirect(offsets[:]))
         ts_ps = []
         for side in range(2):
             ts_ps.append(ps_a.tile([P, 4, P], F32, name="acc"))
@@ -94,12 +101,8 @@ def tile_attend_gbpr_w_ts_kernel(tc, xT, wT, wt, ts, xm, offs, out):
         nc.scalar.copy(out=wt_row[:], in_=wt_ps[:].rearrange("p (u e) m -> p u m e", u=2))
 
         w_pair = [keep.tile([P, T, 2], BF16, name="w_pair%d" % u) for u in range(2)]
-        w_got, w_codes, w_scales = [], [], []
-        for c in range(2):
-            w_got.append(keep.tile([P, 2 * CHUNK, PACK], BF16, name="w_got%d" % c, align_bytes=64))
-            w_scales.append(keep.tile([P, 2 * CHUNK], U8, name="w_scales%d" % c, align_bytes=64))
-
-        w_codes.append(keep.tile([P, 2 * CHUNK], U32, name="w_codes0", align_bytes=64))
+        w_got = keep.tile([P, N, PACK], BF16, name="w_got", align_bytes=64)
+        w_codes, w_scales = [], []
 
         def cast(k, lo, hi, on_vector):
             u, first = W_LOADS[k][0:2]
@@ -117,29 +120,10 @@ def tile_attend_gbpr_w_ts_kernel(tc, xT, wT, wt, ts, xm, offs, out):
             if on_vector:
                 cast(k, count - on_vector, count, True)
 
-        stage = keep.tile([P, 3 * N + CHUNK], U32, name="stage", align_bytes=64)
-        second = (N, N + HALF + CHUNK)
-
-        def window(u):
-            return w_pair[u][:].rearrange("p c e -> p (c e)").bitcast(U32)
-
-        def gather_second(c):
-            for side in range(2):
-                first = second[c] + side * HALF
-                nc.vector.tensor_copy(
-                    out=stage[:, first : first + CHUNK], in_=window(1).indirect(slots(side * HALF + c * CHUNK, CHUNK))
-                )
-
-        def weave(c):
-            apart = second[c] - c * CHUNK
-            word = (I32, U32)[c]
-            src = stage[:, c * CHUNK : c * CHUNK + 2 * apart].bitcast(word).rearrange("p (u s i) -> p s i u", u=2, i=HALF)
-            src = src[:, 0:2, 0:CHUNK, :]
-            dst = w_got[c][:].rearrange("p n t -> p (n t)").bitcast(word).rearrange("p (s i u) -> p s i u", s=2, u=2)
-            if c == 0:
-                nc.vector.tensor_copy(out=dst, in_=src)
-            else:
-                nc.scalar.copy(out=dst, in_=src)
+        def gather(u):
+            window = w_pair[u][:].rearrange("p c e -> p (c e)").bitcast(U32)
+            words = w_got[:].rearrange("p n t -> p (n t)").bitcast(U32).rearrange("p (n u) -> p n u", u=2)
+            nc.vector.tensor_copy(out=words[:, :, u], in_=window.indirect(offsets[:]))
 
         def quantize(codes, scales, grouped, first, count, fmt):
             nc.vector.quantize_mx(
@@ -147,6 +131,11 @@ def tile_attend_gbpr_w_ts_kernel(tc, xT, wT, wt, ts, xm, offs, out):
                 scales=scales[:, first : first + count],
                 in_=grouped[:, first : first + count, :].rearrange("p n t -> p (n t)"),
             )
+
+        def quantize_side(side, tag):
+            w_codes.append(keep.tile([P, HALF], U32, name="w_codes%d" % side, tag=tag, align_bytes=64))
+            w_scales.append(keep.tile([P, HALF], U8, name="w_scales%d" % side, align_bytes=64))
+            quantize(w_codes[side], w_scales[side], w_got[:, side * HALF : (side + 1) * HALF, :], 0, HALF, E4M3)
 
         def interleave(dst, src, on_vector=False):
             dst = dst.rearrange("p (c i) t -> p c t i", i=4)
@@ -158,109 +147,110 @@ def tile_attend_gbpr_w_ts_kernel(tc, xT, wT, wt, ts, xm, offs, out):
 
         for k in range(3):
             cast_load(k)
-        nc.vector.tensor_copy(out=stage[:, 0:N], in_=window(0).indirect(offsets[:]))
-        for k in range(3, len(W_LOADS)):
-            cast_load(k)
+        gather(0)
         ts_col = []
         for side in range(2):
             ts_col.append(early.tile([P, 4], F32, name="ts_col%d" % side, offset=32 * side))
             nc.scalar.activation(out=ts_col[side][:], in_=ts_ps[side][:, :, P - 1], func=ACT.Copy, scale=(-1.0, 1.0)[side])
-        gather_second(0)
-        weave(0)
+        for k in range(3, len(W_LOADS)):
+            cast_load(k)
+        out_win[3] = keep.tile([P, T], F32, name="out_win3", tag="w_raw%d" % (len(W_LOADS) - 1))
+        nc.gpsimd.memset(out_win[3][:].bitcast(U32), 0)
+        gather(1)
+        quantize_side(0, "w_codes0")
 
-        x_grouped = stage[:, second[1] : second[1] + 2 * R].bitcast(BF16).rearrange("p (n t) -> p n t", t=PACK)
+        x_grouped = keep.tile([P, R, PACK], BF16, name="x_grouped", align_bytes=64)
         x_codes = keep.tile([P, R], U32, name="x_codes", align_bytes=64)
         x_scales = keep.tile([P, R], U8, name="x_scales", align_bytes=64)
-        interleave(x_grouped[:, 0 : 2 * P, :], x_raw[0][:])
-        interleave(x_grouped[:, 2 * P : 4 * P, :], x_raw[1][:])
-        quantize(w_codes[0], w_scales[0], w_got[0], 0, 2 * CHUNK, E4M3)
+        for k in range(2):
+            interleave(x_grouped[:, k * (R // 2) : (k + 1) * (R // 2), :], x_raw[k][:])
         quantize(x_codes, x_scales, x_grouped, 0, R, E4M3)
+        quantize_side(1, "x_grouped")
 
         xm_codes = keep.tile([P, D], U32, name="xm_codes", align_bytes=64)
         xm_scales = keep.tile([P, D], U8, name="xm_scales", align_bytes=64)
-        xm_grouped = []
-        for k in range(2):
-            xm_grouped.append(keep.tile([P, D // 2, PACK], BF16, name="xm_grouped%d" % k, align_bytes=64))
 
-        def quantize_xm(k):
+        def quantize_xm(k, tag):
+            grouped = keep.tile([P, D // 2, PACK], BF16, name="xm_grouped%d" % k, tag=tag, align_bytes=64)
+            if k == 0:
+                interleave(grouped[:], xm_raw[k][:])
+            else:
+                interleave(grouped[:, 0:P, :], xm_raw[k][:, :, 0:P])
+                interleave(grouped[:, P:, :], xm_raw[k][:, :, P:], True)
             nc.vector.quantize_mx(
                 out=xm_codes[:, k * (D // 2) : (k + 1) * (D // 2)].bitcast(E4M3),
                 scales=xm_scales[:, k * (D // 2) : (k + 1) * (D // 2)],
-                in_=xm_grouped[k][:].rearrange("p n t -> p (n t)"),
+                in_=grouped[:].rearrange("p n t -> p (n t)"),
             )
 
-        blocks = range(CHUNK // P)
         h_grouped, h_codes, h_scales = [], [], []
         for c in range(2):
-            h_grouped.append(keep.tile([P, 2 * CHUNK, PACK], BF16, name="h_grouped%d" % c, align_bytes=64))
+            h_grouped.append(tail.tile([P, 2 * CHUNK, PACK], BF16, name="h_grouped%d" % c, align_bytes=64, offset=(0, 4 * T - 1024)[c]))
             h_codes.append(keep.tile([P, 2 * CHUNK], U32, name="h_codes%d" % c, align_bytes=64))
             h_scales.append(keep.tile([P, 2 * CHUNK], U8, name="h_scales%d" % c, align_bytes=64))
 
-        def scale_of(c, b, side):
-            col = c * (CHUNK // P) + b
-            return ts_col[side][:, col : col + 1]
+        margin, sig, turned, scaled = {}, {}, {}, {}
 
-        def sigmoids(c):
-            score, margin, sig = {}, {}, {}
-            for b in blocks:
-                for side in range(2):
-                    first = side * CHUNK + b * P
-                    score[b, side] = ps_a.tile([P, R], F32, name="acc")
-                    nc.tensor.matmul_mx(
-                        out=score[b, side][:],
-                        lhsT=w_codes[c][:, first : first + P].bitcast(E4M3),
-                        lhsT_scale=w_scales[c][:, first : first + P],
-                        rhs=x_codes[:].bitcast(E4M3),
-                        rhs_scale=x_scales[:],
-                        start=True,
-                        stop=True,
-                    )
-            for b in blocks:
-                neg_pos = ring.tile([P, R], F32, name="neg_pos")
-                nc.scalar.activation(out=neg_pos[:], in_=score[b, 0][:], func=ACT.Copy, scale=scale_of(c, b, 0))
-                margin[b] = ring.tile([P, R], F32, name="margin")
+        def margins(b):
+            score = []
+            for side in range(2):
+                cols = slice(b * P, (b + 1) * P)
+                score.append(ps_a.tile([P, R], F32, name="acc"))
+                nc.tensor.matmul_mx(
+                    out=score[side][:],
+                    lhsT=w_codes[side][:, cols].bitcast(E4M3),
+                    lhsT_scale=w_scales[side][:, cols],
+                    rhs=x_codes[:].bitcast(E4M3),
+                    rhs_scale=x_scales[:],
+                    start=True,
+                    stop=True,
+                )
+            neg_pos = scaled[b // 2][:, b % 2, :]
+            nc.scalar.activation(out=neg_pos, in_=score[0][:], func=ACT.Copy, scale=ts_col[0][:, b : b + 1])
+            margin[b] = ring.tile([P, R], F32, name="margin")
+            nc.vector.scalar_tensor_tensor(
+                out=margin[b][:],
+                in0=score[1][:],
+                scalar=ts_col[1][:, b : b + 1],
+                in1=neg_pos,
+                op0=ALU.mult,
+                op1=ALU.add,
+            )
+
+        def sigmoid(b):
+            sig[b] = ring.tile([P, R], F32, name="sig")
+            nc.scalar.activation(
+                out=sig[b][:].rearrange("p (u m e) -> p u m e", u=2, e=2),
+                in_=margin[b][:].rearrange("p (m u e) -> p u m e", u=2, e=2),
+                func=ACT.Sigmoid,
+            )
+
+        def gradient(b):
+            turned[b] = ps_b.tile([P, 2, 2, P], F32, name="late")
+            for side in range(2):
+                h = keep.tile([P, R], BF16, name="h%d_%d" % (b, side))
                 nc.vector.scalar_tensor_tensor(
-                    out=margin[b][:],
-                    in0=score[b, 1][:],
-                    scalar=scale_of(c, b, 1),
-                    in1=neg_pos[:],
+                    out=h[:],
+                    in0=sig[b][:],
+                    scalar=ts_col[side][:, b : b + 1],
+                    in1=wt_row[:].rearrange("p u m e -> p (u m e)"),
                     op0=ALU.mult,
-                    op1=ALU.add,
+                    op1=ALU.mult,
                 )
-            for b in blocks:
-                sig[b] = keep.tile([P, R], F32, name="sig%d" % (2 * c + b))
-                nc.scalar.activation(
-                    out=sig[b][:].rearrange("p (u m e) -> p u m e", u=2, e=2),
-                    in_=margin[b][:].rearrange("p (m u e) -> p u m e", u=2, e=2),
-                    func=ACT.Sigmoid,
-                )
-            return sig
+                words = h[:].bitcast(F32).rearrange("p (u m) -> p u m", u=2)
+                for u in range(2):
+                    nc.tensor.transpose(turned[b][:, side, u, :], words[:, u, :], ident[:])
 
-        def gradients(c, sig):
+        def operand(b):
+            c, first = b // 2, (b % 2) * 2 * P
             h_words = h_grouped[c][:].rearrange("p n t -> p (n t)").bitcast(F32).rearrange("p (n u) -> p n u", u=2)
-            for b in blocks:
-                bank = ps_b.tile([P, 2, 2, P], F32, name="late")
-                for side in range(2):
-                    h = ring.tile([P, R], BF16, name="h%d" % side)
-                    nc.vector.scalar_tensor_tensor(
-                        out=h[:],
-                        in0=sig[b][:],
-                        scalar=scale_of(c, b, side),
-                        in1=wt_row[:].rearrange("p u m e -> p (u m e)"),
-                        op0=ALU.mult,
-                        op1=ALU.mult,
-                    )
-                    words = h[:].bitcast(F32).rearrange("p (u m) -> p u m", u=2)
-                    for u in range(2):
-                        nc.tensor.transpose(bank[:, side, u, :], words[:, u, :], ident[:])
-                first = 2 * b * P
-                nc.scalar.copy(
-                    out=h_words[:, first : first + 2 * P, :].rearrange("p (s i) u -> p s i u", s=2),
-                    in_=bank[:].rearrange("p s u i -> p s i u"),
-                )
-                quantize(h_codes[c], h_scales[c], h_grouped[c], first, 2 * P, E5M2)
+            nc.scalar.copy(
+                out=h_words[:, first : first + 2 * P, :].rearrange("p (s i) u -> p s i u", s=2),
+                in_=turned[b][:].rearrange("p s u i -> p s i u"),
+            )
+            quantize(h_codes[c], h_scales[c], h_grouped[c], first, 2 * P, E5M2)
 
-        dw = {j: keep.tile([P, N], F32, name="dw%d" % j)[:] for j in (0, 2)}
+        dw = {j: keep.tile([P, N], F32, name="dw%d" % j) for j in (3,)}
 
         def table_sums(c, j, acc, on_vector):
             nc.tensor.matmul_mx(
@@ -272,16 +262,16 @@ def tile_attend_gbpr_w_ts_kernel(tc, xT, wT, wt, ts, xm, offs, out):
                 start=True,
                 stop=True,
             )
-            dst = dw[j].rearrange("p (s c b i) -> p s c b i", s=2, c=2, i=P)[:, :, c]
+            dst = dw[j][:].rearrange("p (s c b i) -> p s c b i", s=2, c=2, i=P)[:, :, c]
             src = acc[:].rearrange("p (b s i) -> p s b i", s=2, i=P)
             if on_vector:
                 nc.vector.tensor_copy(out=dst, in_=src)
             else:
                 nc.scalar.copy(out=dst, in_=src)
 
-        def scatter(j, first, count):
+        def scatter(j, first, count, on_vector):
             place = out_win[j][:].indirect(slots(first, count))
-            if j % 2 == 0:
+            if on_vector:
                 nc.vector.tensor_copy(out=place, in_=dw[j][:, first : first + count])
             else:
                 nc.scalar.activation(out=place, in_=dw[j][:, first : first + count], func=ACT.Copy)
@@ -289,38 +279,51 @@ def tile_attend_gbpr_w_ts_kernel(tc, xT, wT, wt, ts, xm, offs, out):
         def store(j):
             nc.sync.dma_start(out=out[j * P : (j + 1) * P, :], in_=out_win[j][:])
 
-        sig = sigmoids(0)
-        interleave(xm_grouped[0][:], xm_raw[0][:])
-        gradients(0, sig)
-        out_win[3] = keep.tile([P, T], F32, name="out_win3", tag="h_grouped0", align_bytes=64)
-        nc.gpsimd.memset(out_win[3][:].bitcast(U32), 0)
-        quantize_xm(0)
-        gather_second(1)
-        weave(1)
-        w_codes.append(keep.tile([P, 2 * CHUNK], U32, name="w_codes1", align_bytes=64))
-        quantize(w_codes[1], w_scales[1], w_got[1], 0, 2 * CHUNK, E4M3)
-        sig = sigmoids(1)
-        interleave(xm_grouped[1][:], xm_raw[1][:])
-        quantize_xm(1)
-        gradients(1, sig)
-        dw_odd = keep.tile([P, 2, N], F32, name="dw_odd", tag="sig3")
-        dw[1], dw[3] = dw_odd[:, 0, :], dw_odd[:, 1, :]
-        for j in (1, 3):
-            table_sums(0, j, ps_w.tile([P, 2 * CHUNK], F32, name="sum"), True)
-        for j in (1, 3):
-            scatter(j, 0, CHUNK)
-        for j in (0, 2):
-            table_sums(0, j, ps_a.tile([P, 2 * CHUNK], F32, name="acc"), True)
-        table_sums(1, 0, ps_b.tile([P, 2 * CHUNK], F32, name="late"), True)
-        for j in (1, 3):
-            table_sums(1, j, ps_a.tile([P, 2 * CHUNK], F32, name="acc"), False)
-        scatter(0, 0, N)
+        def bank(pool, name):
+            return pool.tile([P, 2 * CHUNK], F32, name=name)
+
+        quantize_xm(0, "xm_grouped0")
+        quantize_xm(1, "xm_grouped1")
+        scaled[0] = keep.tile([P, 2, R], F32, name="scaled0", tag="xm_raw1")
+        scaled[1] = keep.tile([P, 2, R], F32, name="scaled1")
+        margins(0)
+        margins(1)
+        sigmoid(0)
+        gradient(0)
+        margins(2)
+        sigmoid(1)
+        gradient(1)
+        margins(3)
+        operand(0)
+        sigmoid(2)
+        operand(1)
+        sigmoid(3)
+        gradient(2)
+        gradient(3)
+        operand(2)
+        operand(3)
+        out_win[2] = tail.tile([P, T], F32, name="out_win2", offset=4 * T)
+        nc.gpsimd.memset(out_win[2][:].bitcast(U32), 0)
+        dw[2] = keep.tile([P, N], F32, name="dw2", tag="h3_0")
+        dw[1] = keep.tile([P, N], F32, name="dw1")
+        table_sums(0, 3, bank(ps_w, "sum"), False)
+        scatter(3, 0, CHUNK, True)
+        table_sums(0, 1, bank(ps_w, "sum"), False)
+        scatter(1, 0, CHUNK, False)
+        dw[0] = tail.tile([P, N], F32, name="dw0", offset=4 * T - 4 * N)
+        table_sums(0, 0, bank(ps_a, "acc"), True)
+        table_sums(0, 2, bank(ps_a, "acc"), False)
+        table_sums(1, 0, bank(ps_a, "acc"), True)
+        table_sums(1, 1, bank(ps_a, "acc"), False)
+        scatter(0, 0, N, True)
         store(0)
-        table_sums(1, 2, ps_b.tile([P, 2 * CHUNK], F32, name="late"), True)
-        for first in (CHUNK, CHUNK + 384):
-            for j in (1, 3):
-                scatter(j, first, 384)
+        scatter(1, CHUNK, WIDE, False)
+        table_sums(1, 2, bank(ps_b, "late"), False)
+        scatter(1, CHUNK + WIDE, WIDE, False)
         store(1)
+        table_sums(1, 3, bank(ps_b, "late"), False)
+        scatter(3, CHUNK, WIDE, False)
+        scatter(3, CHUNK + WIDE, WIDE, False)
         store(3)
-        scatter(2, 0, N)
+        scatter(2, 0, N, True)
         store(2)

@@ -22,7 +22,7 @@ CHUNK = 256
 W_LOADS = (
     (0, 0, 1024, 1024),
     (0, 1024, 512, 512),
-    (0, 1536, 512, 320),
+    (0, 1536, 512, 512),
     (1, 0, 512, 0),
     (1, 512, 512, 0),
     (1, 1024, 512, 512),
@@ -38,10 +38,10 @@ def tile_attend_gbpr_w_ts_kernel(tc, xT, wT, wt, ts, xm, offs, out):
         keep = ctx.enter_context(tc.tile_pool(name="keep", bufs=1))
         ring = ctx.enter_context(tc.tile_pool(name="ring", bufs=2))
         early = ctx.enter_context(tc.tile_pool(name="early", bufs=1))
+        pairs = ctx.enter_context(tc.tile_pool(name="pairs", bufs=1))
         tail = ctx.enter_context(tc.tile_pool(name="tail", bufs=1))
-        ps_a = ctx.enter_context(tc.psum_pool(name="ps_a", bufs=4))
+        ps_a = ctx.enter_context(tc.psum_pool(name="ps_a", bufs=6))
         ps_b = ctx.enter_context(tc.psum_pool(name="ps_b", bufs=2))
-        ps_w = ctx.enter_context(tc.psum_pool(name="ps_w", bufs=2))
 
         def slots(first, count):
             return offsets[:, first // 16 : (first + count) // 16]
@@ -52,7 +52,8 @@ def tile_attend_gbpr_w_ts_kernel(tc, xT, wT, wt, ts, xm, offs, out):
         nc.sync.dma_start(out=ts_win[P - 1 : P, :], in_=ts[0:1, :])
         nc.gpsimd.memset(ts_win[0 : P - 1, :].bitcast(U32), 0)
         ident = keep.tile([P, P], F32, name="ident")
-        make_identity(nc, ident[:])
+        nc.vector.memset(ident[:], 0.0)
+        make_identity(nc, ident[:], nomemset=True)
         warm = keep.tile([P, 1], F32, name="warm")
         nc.scalar.activation(out=warm[:], in_=seed[:], func=ACT.Sigmoid)
 
@@ -65,7 +66,7 @@ def tile_attend_gbpr_w_ts_kernel(tc, xT, wT, wt, ts, xm, offs, out):
             if k == 2:
                 w_raw.append(early.tile([P, 2, count], F32, name="w_raw2", offset=0))
             else:
-                w_raw.append(keep.tile([P, 2, count], F32, name="w_raw%d" % k))
+                w_raw.append(keep.tile([P, 2, count], F32, name="w_raw%d" % k, align_bytes=64))
             nc.sync.dma_start(out=w_raw[k][:], in_=w_rows[:, u, :, first : first + count])
             if k == 2:
                 nc.sync.dma_start(out=wt_cols[:], in_=wt[0].rearrange("(p t) o -> p (t o)", t=PACK))
@@ -86,7 +87,8 @@ def tile_attend_gbpr_w_ts_kernel(tc, xT, wT, wt, ts, xm, offs, out):
         nc.gpsimd.memset(out_win[1][:].bitcast(U32), 0)
 
         ts_got = keep.tile([P, N], F32, name="ts_got")
-        nc.vector.tensor_copy(out=ts_got[:], in_=ts_win[:].indirect(offsets[:]))
+        nc.vector.tensor_copy(out=ts_got[:, 0:HALF], in_=ts_win[:].indirect(slots(0, HALF)))
+        nc.scalar.activation(out=ts_got[:, HALF:], in_=ts_win[:].indirect(slots(HALF, HALF)), func=ACT.Copy)
         ts_ps = []
         for side in range(2):
             ts_ps.append(ps_a.tile([P, 4, P], F32, name="acc"))
@@ -94,13 +96,24 @@ def tile_attend_gbpr_w_ts_kernel(tc, xT, wT, wt, ts, xm, offs, out):
                 first = side * HALF + b * P
                 nc.tensor.transpose(ts_ps[side][:, b, :], ts_got[:, first : first + P], ident[:])
 
-        wt_ps = ps_w.tile([P, PACK, P], F32, name="sum")
-        for t in range(PACK):
-            nc.tensor.transpose(wt_ps[:, t, :], wt_cols[:, t : t + 1].to_broadcast([P, P]), ident[:])
-        wt_row = keep.tile([P, 2, P, 2], F32, name="wt_row")
-        nc.scalar.copy(out=wt_row[:], in_=wt_ps[:].rearrange("p (u e) m -> p u m e", u=2))
+        ts_col = []
+        for side in range(2):
+            ts_col.append(keep.tile([P, 4], F32, name="ts_col%d" % side))
+            nc.scalar.activation(out=ts_col[side][:], in_=ts_ps[side][:, :, P - 1], func=ACT.Copy, scale=(-1.0, 1.0)[side])
+        ts_spread = []
+        for side in range(2):
+            ts_spread.append(pairs.tile([P, 4], F32, name="ts_spread%d" % side, offset=32 * side))
+            nc.scalar.activation(out=ts_spread[side][:], in_=ts_ps[side][:, :, P - 1], func=ACT.Copy, scale=(-1.0, 1.0)[side])
+        ts_rows = keep.tile([P, 2, 2 * CHUNK], F32, name="ts_rows")
+        for c in range(2):
+            spread = ps_b.tile([P, 2, 2, P], F32, name="late")
+            for side in range(2):
+                for b in range(2):
+                    col = ts_spread[side][:, 2 * c + b : 2 * c + b + 1]
+                    nc.tensor.transpose(spread[:, side, b, :], col.to_broadcast([P, P]), ident[:])
+            nc.scalar.copy(out=ts_rows[:, c, :], in_=spread[:].rearrange("p s b i -> p (s b i)"))
 
-        w_pair = [keep.tile([P, T, 2], BF16, name="w_pair%d" % u) for u in range(2)]
+        w_pair = [keep.tile([P, T, 2], BF16, name="w_pair0"), pairs.tile([P, T, 2], BF16, name="w_pair1", offset=0)]
         w_got = keep.tile([P, N, PACK], BF16, name="w_got", align_bytes=64)
         w_codes, w_scales = [], []
 
@@ -148,14 +161,25 @@ def tile_attend_gbpr_w_ts_kernel(tc, xT, wT, wt, ts, xm, offs, out):
         for k in range(3):
             cast_load(k)
         gather(0)
-        ts_col = []
-        for side in range(2):
-            ts_col.append(early.tile([P, 4], F32, name="ts_col%d" % side, offset=32 * side))
-            nc.scalar.activation(out=ts_col[side][:], in_=ts_ps[side][:, :, P - 1], func=ACT.Copy, scale=(-1.0, 1.0)[side])
+        out_win[3] = early.tile([P, T], F32, name="out_win3", offset=0)
+        nc.gpsimd.memset(out_win[3][:].bitcast(U32), 0)
         for k in range(3, len(W_LOADS)):
             cast_load(k)
-        out_win[3] = keep.tile([P, T], F32, name="out_win3", tag="w_raw%d" % (len(W_LOADS) - 1))
-        nc.gpsimd.memset(out_win[3][:].bitcast(U32), 0)
+        factor = {}
+
+        def factors(c, tag):
+            factor[c] = keep.tile([P, PACK, 2 * CHUNK], F32, name="factor%d" % c, tag=tag, align_bytes=64)
+            for t in range(PACK):
+                nc.gpsimd.tensor_scalar(
+                    out=factor[c][:, t, :],
+                    in0=ts_rows[:, c, :],
+                    scalar1=wt_cols[:, t : t + 1],
+                    scalar2=0.0,
+                    op0=ALU.mult,
+                    op1=ALU.add,
+                )
+
+        factors(0, "w_raw%d" % (len(W_LOADS) - 1))
         gather(1)
         quantize_side(0, "w_codes0")
 
@@ -172,11 +196,7 @@ def tile_attend_gbpr_w_ts_kernel(tc, xT, wT, wt, ts, xm, offs, out):
 
         def quantize_xm(k, tag):
             grouped = keep.tile([P, D // 2, PACK], BF16, name="xm_grouped%d" % k, tag=tag, align_bytes=64)
-            if k == 0:
-                interleave(grouped[:], xm_raw[k][:])
-            else:
-                interleave(grouped[:, 0:P, :], xm_raw[k][:, :, 0:P])
-                interleave(grouped[:, P:, :], xm_raw[k][:, :, P:], True)
+            interleave(grouped[:], xm_raw[k][:])
             nc.vector.quantize_mx(
                 out=xm_codes[:, k * (D // 2) : (k + 1) * (D // 2)].bitcast(E4M3),
                 scales=xm_scales[:, k * (D // 2) : (k + 1) * (D // 2)],
@@ -189,7 +209,10 @@ def tile_attend_gbpr_w_ts_kernel(tc, xT, wT, wt, ts, xm, offs, out):
             h_codes.append(keep.tile([P, 2 * CHUNK], U32, name="h_codes%d" % c, align_bytes=64))
             h_scales.append(keep.tile([P, 2 * CHUNK], U8, name="h_scales%d" % c, align_bytes=64))
 
-        margin, sig, turned, scaled = {}, {}, {}, {}
+        margin, turned = {}, {}
+
+        def dealt(acc):
+            return acc[:].rearrange("p (m t) -> p t m", t=PACK)
 
         def margins(b):
             score = []
@@ -205,65 +228,52 @@ def tile_attend_gbpr_w_ts_kernel(tc, xT, wT, wt, ts, xm, offs, out):
                     start=True,
                     stop=True,
                 )
-            neg_pos = scaled[b // 2][:, b % 2, :]
-            nc.scalar.activation(out=neg_pos, in_=score[0][:], func=ACT.Copy, scale=ts_col[0][:, b : b + 1])
-            margin[b] = ring.tile([P, R], F32, name="margin")
+            neg_pos = keep.tile([P, PACK, P], F32, name="neg_pos%d" % b, tag="neg_pos%d" % b if b < 2 else "margin%d" % (b - 2), align_bytes=64)
+            nc.scalar.activation(out=neg_pos[:], in_=dealt(score[0]), func=ACT.Copy, scale=ts_col[0][:, b : b + 1])
+            margin[b] = keep.tile([P, PACK, P], F32, name="margin%d" % b, align_bytes=64)
             nc.vector.scalar_tensor_tensor(
                 out=margin[b][:],
-                in0=score[1][:],
+                in0=dealt(score[1]),
                 scalar=ts_col[1][:, b : b + 1],
-                in1=neg_pos,
+                in1=neg_pos[:],
                 op0=ALU.mult,
                 op1=ALU.add,
             )
 
         def sigmoid(b):
-            sig[b] = ring.tile([P, R], F32, name="sig")
-            nc.scalar.activation(
-                out=sig[b][:].rearrange("p (u m e) -> p u m e", u=2, e=2),
-                in_=margin[b][:].rearrange("p (m u e) -> p u m e", u=2, e=2),
-                func=ACT.Sigmoid,
+            sig = keep.tile([P, PACK, P], F32, name="sig%d" % b, align_bytes=64)
+            nc.scalar.activation(out=sig[:], in_=margin[b][:], func=ACT.Sigmoid)
+            turned[b] = ps_b.tile([P, PACK, P], F32, name="late")
+            for t in range(PACK):
+                nc.tensor.transpose(turned[b][:, t, :], sig[:, t, :], ident[:])
+
+        def gradient(b, side):
+            c, first = b // 2, side * CHUNK + (b % 2) * P
+            nc.vector.tensor_tensor(
+                out=h_grouped[c][:, first : first + P, :].rearrange("p (g i) t -> p g t i", i=4),
+                in0=turned[b][:].rearrange("p t (g i) -> p g t i", i=4),
+                in1=factor[c][:, :, first : first + P].rearrange("p t (g i) -> p g t i", i=4),
+                op=ALU.mult,
             )
 
-        def gradient(b):
-            turned[b] = ps_b.tile([P, 2, 2, P], F32, name="late")
-            for side in range(2):
-                h = keep.tile([P, R], BF16, name="h%d_%d" % (b, side))
-                nc.vector.scalar_tensor_tensor(
-                    out=h[:],
-                    in0=sig[b][:],
-                    scalar=ts_col[side][:, b : b + 1],
-                    in1=wt_row[:].rearrange("p u m e -> p (u m e)"),
-                    op0=ALU.mult,
-                    op1=ALU.mult,
-                )
-                words = h[:].bitcast(F32).rearrange("p (u m) -> p u m", u=2)
-                for u in range(2):
-                    nc.tensor.transpose(turned[b][:, side, u, :], words[:, u, :], ident[:])
+        def operand(c, side):
+            quantize(h_codes[c], h_scales[c], h_grouped[c], side * CHUNK, CHUNK, E5M2)
 
-        def operand(b):
-            c, first = b // 2, (b % 2) * 2 * P
-            h_words = h_grouped[c][:].rearrange("p n t -> p (n t)").bitcast(F32).rearrange("p (n u) -> p n u", u=2)
-            nc.scalar.copy(
-                out=h_words[:, first : first + 2 * P, :].rearrange("p (s i) u -> p s i u", s=2),
-                in_=turned[b][:].rearrange("p s u i -> p s i u"),
-            )
-            quantize(h_codes[c], h_scales[c], h_grouped[c], first, 2 * P, E5M2)
+        dw = {j: keep.tile([P, N], F32, name="dw%d" % j) for j in (0, 1, 3)}
 
-        dw = {j: keep.tile([P, N], F32, name="dw%d" % j) for j in (3,)}
-
-        def table_sums(c, j, acc, on_vector):
+        def table_sums(c, j, acc, on_vector, sides=slice(0, 2)):
+            cols = slice(sides.start * CHUNK, sides.stop * CHUNK)
             nc.tensor.matmul_mx(
-                out=acc[:],
+                out=acc[:, cols],
                 lhsT=xm_codes[:, j * P : (j + 1) * P].bitcast(E4M3),
                 lhsT_scale=xm_scales[:, j * P : (j + 1) * P],
-                rhs=h_codes[c][:].bitcast(E5M2),
-                rhs_scale=h_scales[c][:],
+                rhs=h_codes[c][:, cols].bitcast(E5M2),
+                rhs_scale=h_scales[c][:, cols],
                 start=True,
                 stop=True,
             )
-            dst = dw[j][:].rearrange("p (s c b i) -> p s c b i", s=2, c=2, i=P)[:, :, c]
-            src = acc[:].rearrange("p (b s i) -> p s b i", s=2, i=P)
+            dst = dw[j][:].rearrange("p (s c i) -> p s c i", s=2, c=2)[:, sides, c]
+            src = acc[:].rearrange("p (s i) -> p s i", s=2)[:, sides]
             if on_vector:
                 nc.vector.tensor_copy(out=dst, in_=src)
             else:
@@ -283,47 +293,47 @@ def tile_attend_gbpr_w_ts_kernel(tc, xT, wT, wt, ts, xm, offs, out):
             return pool.tile([P, 2 * CHUNK], F32, name=name)
 
         quantize_xm(0, "xm_grouped0")
-        quantize_xm(1, "xm_grouped1")
-        scaled[0] = keep.tile([P, 2, R], F32, name="scaled0", tag="xm_raw1")
-        scaled[1] = keep.tile([P, 2, R], F32, name="scaled1")
+        factors(1, "xm_grouped0")
         margins(0)
         margins(1)
         sigmoid(0)
-        gradient(0)
-        margins(2)
         sigmoid(1)
-        gradient(1)
+        margins(2)
+        gradient(0, 0)
+        gradient(1, 0)
         margins(3)
-        operand(0)
+        operand(0, 0)
+        gradient(0, 1)
+        gradient(1, 1)
+        operand(0, 1)
         sigmoid(2)
-        operand(1)
         sigmoid(3)
-        gradient(2)
-        gradient(3)
-        operand(2)
-        operand(3)
+        quantize_xm(1, "margin2")
+        for side in range(2):
+            gradient(2, side)
+            gradient(3, side)
+            operand(1, side)
         out_win[2] = tail.tile([P, T], F32, name="out_win2", offset=4 * T)
         nc.gpsimd.memset(out_win[2][:].bitcast(U32), 0)
-        dw[2] = keep.tile([P, N], F32, name="dw2", tag="h3_0")
-        dw[1] = keep.tile([P, N], F32, name="dw1")
-        table_sums(0, 3, bank(ps_w, "sum"), False)
-        scatter(3, 0, CHUNK, True)
-        table_sums(0, 1, bank(ps_w, "sum"), False)
+        table_sums(0, 1, bank(ps_a, "acc"), False, slice(0, 1))
         scatter(1, 0, CHUNK, False)
-        dw[0] = tail.tile([P, N], F32, name="dw0", offset=4 * T - 4 * N)
-        table_sums(0, 0, bank(ps_a, "acc"), True)
-        table_sums(0, 2, bank(ps_a, "acc"), False)
+        table_sums(0, 1, bank(ps_a, "acc"), False, slice(1, 2))
+        table_sums(0, 0, bank(ps_a, "acc"), False)
+        scatter(1, HALF, CHUNK, False)
+        table_sums(0, 3, bank(ps_a, "acc"), False)
+        dw[2] = tail.tile([P, N], F32, name="dw2", offset=4 * T - 4 * N)
+        table_sums(0, 2, bank(ps_a, "acc"), True)
         table_sums(1, 0, bank(ps_a, "acc"), True)
         table_sums(1, 1, bank(ps_a, "acc"), False)
         scatter(0, 0, N, True)
         store(0)
-        scatter(1, CHUNK, WIDE, False)
-        table_sums(1, 2, bank(ps_b, "late"), False)
-        scatter(1, CHUNK + WIDE, WIDE, False)
-        store(1)
+        scatter(1, CHUNK, CHUNK, False)
         table_sums(1, 3, bank(ps_b, "late"), False)
-        scatter(3, CHUNK, WIDE, False)
-        scatter(3, CHUNK + WIDE, WIDE, False)
+        scatter(1, HALF + CHUNK, CHUNK, False)
+        store(1)
+        table_sums(1, 2, bank(ps_b, "late"), True)
+        for first, count in ((0, WIDE), (WIDE, WIDE), (2 * WIDE, CHUNK)):
+            scatter(3, first, count, False)
         store(3)
         scatter(2, 0, N, True)
         store(2)

@@ -37,8 +37,8 @@ def tile_attend_gbpr_w_ts_kernel(tc, xT, wT, wt, ts, xm, offs, out):
     with ExitStack() as ctx:
         keep = ctx.enter_context(tc.tile_pool(name="keep", bufs=1))
         ring = ctx.enter_context(tc.tile_pool(name="ring", bufs=2))
-        early = ctx.enter_context(tc.tile_pool(name="early", bufs=1))
         pairs = ctx.enter_context(tc.tile_pool(name="pairs", bufs=1))
+        woven = ctx.enter_context(tc.tile_pool(name="woven", bufs=1))
         tail = ctx.enter_context(tc.tile_pool(name="tail", bufs=1))
         ps_a = ctx.enter_context(tc.psum_pool(name="ps_a", bufs=6))
         ps_b = ctx.enter_context(tc.psum_pool(name="ps_b", bufs=2))
@@ -63,10 +63,7 @@ def tile_attend_gbpr_w_ts_kernel(tc, xT, wT, wt, ts, xm, offs, out):
         w_rows = wT.rearrange("(p u e) c -> p u e c", u=2, e=2)
         w_raw = []
         for k, (u, first, count, on_vector) in enumerate(W_LOADS):
-            if k == 2:
-                w_raw.append(early.tile([P, 2, count], F32, name="w_raw2", offset=0))
-            else:
-                w_raw.append(keep.tile([P, 2, count], F32, name="w_raw%d" % k, align_bytes=64))
+            w_raw.append(keep.tile([P, 2, count], F32, name="w_raw%d" % k, align_bytes=64))
             nc.sync.dma_start(out=w_raw[k][:], in_=w_rows[:, u, :, first : first + count])
             if k == 2:
                 nc.sync.dma_start(out=wt_cols[:], in_=wt[0].rearrange("(p t) o -> p (t o)", t=PACK))
@@ -114,7 +111,7 @@ def tile_attend_gbpr_w_ts_kernel(tc, xT, wT, wt, ts, xm, offs, out):
             nc.scalar.copy(out=ts_rows[:, c, :], in_=spread[:].rearrange("p s b i -> p (s b i)"))
 
         w_pair = [keep.tile([P, T, 2], BF16, name="w_pair0"), pairs.tile([P, T, 2], BF16, name="w_pair1", offset=0)]
-        w_got = keep.tile([P, N, PACK], BF16, name="w_got", align_bytes=64)
+        w_got = woven.tile([P, N, PACK], BF16, name="w_got", align_bytes=64, offset=0)
         w_codes, w_scales = [], []
 
         def cast(k, lo, hi, on_vector):
@@ -158,20 +155,10 @@ def tile_attend_gbpr_w_ts_kernel(tc, xT, wT, wt, ts, xm, offs, out):
             else:
                 nc.scalar.activation(out=dst, in_=src, func=ACT.Copy)
 
-        for k in range(3):
-            cast_load(k)
-        gather(0)
-        out_win[3] = early.tile([P, T], F32, name="out_win3", offset=0)
-        nc.gpsimd.memset(out_win[3][:].bitcast(U32), 0)
-        for k in range(3, len(W_LOADS)):
-            cast_load(k)
-        factor = {}
-
-        def factors(c, tag):
-            factor[c] = keep.tile([P, PACK, 2 * CHUNK], F32, name="factor%d" % c, tag=tag, align_bytes=64)
+        def factors(c):
             for t in range(PACK):
                 nc.gpsimd.tensor_scalar(
-                    out=factor[c][:, t, :],
+                    out=factor[:, c, t, :],
                     in0=ts_rows[:, c, :],
                     scalar1=wt_cols[:, t : t + 1],
                     scalar2=0.0,
@@ -179,7 +166,11 @@ def tile_attend_gbpr_w_ts_kernel(tc, xT, wT, wt, ts, xm, offs, out):
                     op1=ALU.add,
                 )
 
-        factors(0, "w_raw%d" % (len(W_LOADS) - 1))
+        for k in range(3):
+            cast_load(k)
+        gather(0)
+        for k in range(3, len(W_LOADS)):
+            cast_load(k)
         gather(1)
         quantize_side(0, "w_codes0")
 
@@ -195,7 +186,10 @@ def tile_attend_gbpr_w_ts_kernel(tc, xT, wT, wt, ts, xm, offs, out):
         xm_scales = keep.tile([P, D], U8, name="xm_scales", align_bytes=64)
 
         def quantize_xm(k, tag):
-            grouped = keep.tile([P, D // 2, PACK], BF16, name="xm_grouped%d" % k, tag=tag, align_bytes=64)
+            if k == 0:
+                grouped = woven.tile([P, D // 2, PACK], BF16, name="xm_grouped0", align_bytes=64, offset=2 * PACK * N)
+            else:
+                grouped = keep.tile([P, D // 2, PACK], BF16, name="xm_grouped1", tag=tag, align_bytes=64)
             interleave(grouped[:], xm_raw[k][:])
             nc.vector.quantize_mx(
                 out=xm_codes[:, k * (D // 2) : (k + 1) * (D // 2)].bitcast(E4M3),
@@ -205,7 +199,7 @@ def tile_attend_gbpr_w_ts_kernel(tc, xT, wT, wt, ts, xm, offs, out):
 
         h_grouped, h_codes, h_scales = [], [], []
         for c in range(2):
-            h_grouped.append(tail.tile([P, 2 * CHUNK, PACK], BF16, name="h_grouped%d" % c, align_bytes=64, offset=(0, 4 * T - 1024)[c]))
+            h_grouped.append(tail.tile([P, 2 * CHUNK + c * P, PACK], BF16, name="h_grouped%d" % c, align_bytes=64, offset=c * (4 * N + 4 * T - 512)))
             h_codes.append(keep.tile([P, 2 * CHUNK], U32, name="h_codes%d" % c, align_bytes=64))
             h_scales.append(keep.tile([P, 2 * CHUNK], U8, name="h_scales%d" % c, align_bytes=64))
 
@@ -252,7 +246,7 @@ def tile_attend_gbpr_w_ts_kernel(tc, xT, wT, wt, ts, xm, offs, out):
             nc.vector.tensor_tensor(
                 out=h_grouped[c][:, first : first + P, :].rearrange("p (g i) t -> p g t i", i=4),
                 in0=turned[b][:].rearrange("p t (g i) -> p g t i", i=4),
-                in1=factor[c][:, :, first : first + P].rearrange("p t (g i) -> p g t i", i=4),
+                in1=factor[:, c, :, first : first + P].rearrange("p t (g i) -> p g t i", i=4),
                 op=ALU.mult,
             )
 
@@ -293,7 +287,9 @@ def tile_attend_gbpr_w_ts_kernel(tc, xT, wT, wt, ts, xm, offs, out):
             return pool.tile([P, 2 * CHUNK], F32, name=name)
 
         quantize_xm(0, "xm_grouped0")
-        factors(1, "xm_grouped0")
+        factor = woven.tile([P, 2, PACK, 2 * CHUNK], F32, name="factor", align_bytes=64, offset=0)
+        factors(0)
+        factors(1)
         margins(0)
         margins(1)
         sigmoid(0)
@@ -313,15 +309,16 @@ def tile_attend_gbpr_w_ts_kernel(tc, xT, wT, wt, ts, xm, offs, out):
             gradient(2, side)
             gradient(3, side)
             operand(1, side)
-        out_win[2] = tail.tile([P, T], F32, name="out_win2", offset=4 * T)
-        nc.gpsimd.memset(out_win[2][:].bitcast(U32), 0)
+        for j in (3, 2):
+            out_win[j] = tail.tile([P, T], F32, name="out_win%d" % j, offset=4 * N + (3 - j) * (4 * T + 4 * N))
+            nc.gpsimd.memset(out_win[j][:].bitcast(U32), 0)
         table_sums(0, 1, bank(ps_a, "acc"), False, slice(0, 1))
         scatter(1, 0, CHUNK, False)
         table_sums(0, 1, bank(ps_a, "acc"), False, slice(1, 2))
         table_sums(0, 0, bank(ps_a, "acc"), False)
         scatter(1, HALF, CHUNK, False)
         table_sums(0, 3, bank(ps_a, "acc"), False)
-        dw[2] = tail.tile([P, N], F32, name="dw2", offset=4 * T - 4 * N)
+        dw[2] = tail.tile([P, N], F32, name="dw2", offset=4 * N + 4 * T)
         table_sums(0, 2, bank(ps_a, "acc"), True)
         table_sums(1, 0, bank(ps_a, "acc"), True)
         table_sums(1, 1, bank(ps_a, "acc"), False)

@@ -6,7 +6,6 @@ from concourse.masks import make_identity
 F32 = mybir.dt.float32
 BF16 = mybir.dt.bfloat16
 U32 = mybir.dt.uint32
-I32 = mybir.dt.int32
 U16 = mybir.dt.uint16
 U8 = mybir.dt.uint8
 E4M3 = mybir.dt.float8_e4m3fn_x4
@@ -18,17 +17,24 @@ P = 128
 PACK = 4
 N, T, D, R = 1024, 2048, 512, 512
 HALF = N // 2
-CHUNK = 256
+CHUNK = 2 * P
+BLOCKS = HALF // P
+SIGN = (-1.0, 1.0)
+RUN = 4
 W_LOADS = (
     (0, 0, 1024, 1024),
-    (0, 1024, 512, 512),
-    (0, 1536, 512, 512),
-    (1, 0, 512, 0),
-    (1, 512, 512, 0),
-    (1, 1024, 512, 512),
-    (1, 1536, 512, 320),
+    (0, 1024, 1024, 1024),
+    (1, 0, 1024, 0),
+    (1, 1024, 768, 768),
+    (1, 1792, 256, 160),
 )
+FIRST_PAIR_LOADS = 2
 WIDE = 384
+SCORE_BANKS = 6
+TURN_BANKS = 2
+WINDOW_BYTES = 4 * T
+SUMS_BYTES = 4 * N
+OVERLAP = 512
 FLOPS = 2 * 2 * N * D * R
 
 
@@ -36,12 +42,12 @@ def tile_attend_gbpr_w_ts_kernel(tc, xT, wT, wt, ts, xm, offs, out):
     nc = tc.nc
     with ExitStack() as ctx:
         keep = ctx.enter_context(tc.tile_pool(name="keep", bufs=1))
-        ring = ctx.enter_context(tc.tile_pool(name="ring", bufs=2))
         pairs = ctx.enter_context(tc.tile_pool(name="pairs", bufs=1))
         woven = ctx.enter_context(tc.tile_pool(name="woven", bufs=1))
+        xpool = ctx.enter_context(tc.tile_pool(name="xpool", bufs=1))
         tail = ctx.enter_context(tc.tile_pool(name="tail", bufs=1))
-        ps_a = ctx.enter_context(tc.psum_pool(name="ps_a", bufs=6))
-        ps_b = ctx.enter_context(tc.psum_pool(name="ps_b", bufs=2))
+        ps_score = ctx.enter_context(tc.psum_pool(name="ps_score", bufs=SCORE_BANKS))
+        ps_turn = ctx.enter_context(tc.psum_pool(name="ps_turn", bufs=TURN_BANKS))
 
         def slots(first, count):
             return offsets[:, first // 16 : (first + count) // 16]
@@ -65,7 +71,7 @@ def tile_attend_gbpr_w_ts_kernel(tc, xT, wT, wt, ts, xm, offs, out):
         for k, (u, first, count, on_vector) in enumerate(W_LOADS):
             w_raw.append(keep.tile([P, 2, count], F32, name="w_raw%d" % k, align_bytes=64))
             nc.sync.dma_start(out=w_raw[k][:], in_=w_rows[:, u, :, first : first + count])
-            if k == 2:
+            if k == FIRST_PAIR_LOADS - 1:
                 nc.sync.dma_start(out=wt_cols[:], in_=wt[0].rearrange("(p t) o -> p (t o)", t=PACK))
         x_rows = xT[0].rearrange("(p t) r -> p t r", t=PACK)
         x_raw = []
@@ -86,24 +92,27 @@ def tile_attend_gbpr_w_ts_kernel(tc, xT, wT, wt, ts, xm, offs, out):
         ts_got = keep.tile([P, N], F32, name="ts_got")
         nc.vector.tensor_copy(out=ts_got[:, 0:HALF], in_=ts_win[:].indirect(slots(0, HALF)))
         nc.scalar.activation(out=ts_got[:, HALF:], in_=ts_win[:].indirect(slots(HALF, HALF)), func=ACT.Copy)
-        ts_ps = []
+        ts_turned = []
         for side in range(2):
-            ts_ps.append(ps_a.tile([P, 4, P], F32, name="acc"))
-            for b in range(4):
+            ts_turned.append(ps_score.tile([P, BLOCKS, P], F32, name="score"))
+            for b in range(BLOCKS):
                 first = side * HALF + b * P
-                nc.tensor.transpose(ts_ps[side][:, b, :], ts_got[:, first : first + P], ident[:])
+                nc.tensor.transpose(ts_turned[side][:, b, :], ts_got[:, first : first + P], ident[:])
+
+        def signed_ts(dst, side):
+            nc.scalar.activation(out=dst, in_=ts_turned[side][:, :, P - 1], func=ACT.Copy, scale=SIGN[side])
 
         ts_col = []
         for side in range(2):
-            ts_col.append(keep.tile([P, 4], F32, name="ts_col%d" % side))
-            nc.scalar.activation(out=ts_col[side][:], in_=ts_ps[side][:, :, P - 1], func=ACT.Copy, scale=(-1.0, 1.0)[side])
+            ts_col.append(keep.tile([P, BLOCKS], F32, name="ts_col%d" % side))
+            signed_ts(ts_col[side][:], side)
         ts_spread = []
         for side in range(2):
-            ts_spread.append(pairs.tile([P, 4], F32, name="ts_spread%d" % side, offset=32 * side))
-            nc.scalar.activation(out=ts_spread[side][:], in_=ts_ps[side][:, :, P - 1], func=ACT.Copy, scale=(-1.0, 1.0)[side])
+            ts_spread.append(pairs.tile([P, BLOCKS], F32, name="ts_spread%d" % side, offset=32 * side))
+            signed_ts(ts_spread[side][:], side)
         ts_rows = keep.tile([P, 2, 2 * CHUNK], F32, name="ts_rows")
         for c in range(2):
-            spread = ps_b.tile([P, 2, 2, P], F32, name="late")
+            spread = ps_turn.tile([P, 2, 2, P], F32, name="turn")
             for side in range(2):
                 for b in range(2):
                     col = ts_spread[side][:, 2 * c + b : 2 * c + b + 1]
@@ -111,13 +120,13 @@ def tile_attend_gbpr_w_ts_kernel(tc, xT, wT, wt, ts, xm, offs, out):
             nc.scalar.copy(out=ts_rows[:, c, :], in_=spread[:].rearrange("p s b i -> p (s b i)"))
 
         w_pair = [keep.tile([P, T, 2], BF16, name="w_pair0"), pairs.tile([P, T, 2], BF16, name="w_pair1", offset=0)]
-        w_got = woven.tile([P, N, PACK], BF16, name="w_got", align_bytes=64, offset=0)
-        w_codes, w_scales = [], []
+        w_grouped = woven.tile([P, N, PACK], BF16, name="w_grouped", align_bytes=64, offset=0)
+        w_mx = {}
 
         def cast(k, lo, hi, on_vector):
             u, first = W_LOADS[k][0:2]
-            dst = w_pair[u][:, first + lo : first + hi, :].rearrange("p (c i) e -> p c e i", i=4)
-            src = w_raw[k][:, :, lo:hi].rearrange("p e (c i) -> p c e i", i=4)
+            dst = w_pair[u][:, first + lo : first + hi, :].rearrange("p (c i) e -> p c e i", i=RUN)
+            src = w_raw[k][:, :, lo:hi].rearrange("p e (c i) -> p c e i", i=RUN)
             if on_vector:
                 nc.vector.tensor_copy(out=dst, in_=src)
             else:
@@ -132,97 +141,76 @@ def tile_attend_gbpr_w_ts_kernel(tc, xT, wT, wt, ts, xm, offs, out):
 
         def gather(u):
             window = w_pair[u][:].rearrange("p c e -> p (c e)").bitcast(U32)
-            words = w_got[:].rearrange("p n t -> p (n t)").bitcast(U32).rearrange("p (n u) -> p n u", u=2)
+            words = w_grouped[:].rearrange("p n t -> p (n t)").bitcast(U32).rearrange("p (n u) -> p n u", u=2)
             nc.vector.tensor_copy(out=words[:, :, u], in_=window.indirect(offsets[:]))
 
-        def quantize(codes, scales, grouped, first, count, fmt):
-            nc.vector.quantize_mx(
-                out=codes[:, first : first + count].bitcast(fmt),
-                scales=scales[:, first : first + count],
-                in_=grouped[:, first : first + count, :].rearrange("p n t -> p (n t)"),
-            )
+        def quantize(codes, scales, grouped, fmt):
+            nc.vector.quantize_mx(out=codes.bitcast(fmt), scales=scales, in_=grouped.rearrange("p n t -> p (n t)"))
 
-        def quantize_side(side, tag):
-            w_codes.append(keep.tile([P, HALF], U32, name="w_codes%d" % side, tag=tag, align_bytes=64))
-            w_scales.append(keep.tile([P, HALF], U8, name="w_scales%d" % side, align_bytes=64))
-            quantize(w_codes[side], w_scales[side], w_got[:, side * HALF : (side + 1) * HALF, :], 0, HALF, E4M3)
+        def quantize_table(first, codes):
+            count = codes.shape[1]
+            scales = keep.tile([P, count], U8, name="w_scales%d" % first, align_bytes=64)
+            quantize(codes[:], scales[:], w_grouped[:, first : first + count, :], E4M3)
+            for col in range(0, count, P):
+                w_mx[(first + col) // P] = (codes[:, col : col + P], scales[:, col : col + P])
 
-        def interleave(dst, src, on_vector=False):
-            dst = dst.rearrange("p (c i) t -> p c t i", i=4)
-            src = src.rearrange("p t (c i) -> p c t i", i=4)
-            if on_vector:
-                nc.vector.tensor_copy(out=dst, in_=src)
-            else:
-                nc.scalar.activation(out=dst, in_=src, func=ACT.Copy)
+        def interleave(dst, src):
+            dst = dst.rearrange("p (c i) t -> p c t i", i=RUN)
+            src = src.rearrange("p t (c i) -> p c t i", i=RUN)
+            nc.scalar.activation(out=dst, in_=src, func=ACT.Copy)
 
-        def factors(c):
-            for t in range(PACK):
-                nc.gpsimd.tensor_scalar(
-                    out=factor[:, c, t, :],
-                    in0=ts_rows[:, c, :],
-                    scalar1=wt_cols[:, t : t + 1],
-                    scalar2=0.0,
-                    op0=ALU.mult,
-                    op1=ALU.add,
-                )
-
-        for k in range(3):
+        for k in range(FIRST_PAIR_LOADS):
             cast_load(k)
         gather(0)
-        for k in range(3, len(W_LOADS)):
+        for k in range(FIRST_PAIR_LOADS, len(W_LOADS)):
             cast_load(k)
         gather(1)
-        quantize_side(0, "w_codes0")
-
-        x_grouped = keep.tile([P, R, PACK], BF16, name="x_grouped", align_bytes=64)
+        quantize_table(0, keep.tile([P, CHUNK], U32, name="w_codes_first", align_bytes=64))
+        x_grouped = xpool.tile([P, R, PACK], BF16, name="x_grouped", align_bytes=64, offset=0)
         x_codes = keep.tile([P, R], U32, name="x_codes", align_bytes=64)
         x_scales = keep.tile([P, R], U8, name="x_scales", align_bytes=64)
         for k in range(2):
             interleave(x_grouped[:, k * (R // 2) : (k + 1) * (R // 2), :], x_raw[k][:])
-        quantize(x_codes, x_scales, x_grouped, 0, R, E4M3)
-        quantize_side(1, "x_grouped")
+        quantize(x_codes[:], x_scales[:], x_grouped[:], E4M3)
+        quantize_table(HALF, xpool.tile([P, HALF], U32, name="w_codes_neg", align_bytes=64, offset=0))
+        quantize_table(CHUNK, xpool.tile([P, CHUNK], U32, name="w_codes_rest", align_bytes=64, offset=4 * HALF))
 
         xm_codes = keep.tile([P, D], U32, name="xm_codes", align_bytes=64)
         xm_scales = keep.tile([P, D], U8, name="xm_scales", align_bytes=64)
 
-        def quantize_xm(k, tag):
-            if k == 0:
-                grouped = woven.tile([P, D // 2, PACK], BF16, name="xm_grouped0", align_bytes=64, offset=2 * PACK * N)
-            else:
-                grouped = keep.tile([P, D // 2, PACK], BF16, name="xm_grouped1", tag=tag, align_bytes=64)
+        def quantize_xm(k, grouped):
+            cols = slice(k * (D // 2), (k + 1) * (D // 2))
             interleave(grouped[:], xm_raw[k][:])
-            nc.vector.quantize_mx(
-                out=xm_codes[:, k * (D // 2) : (k + 1) * (D // 2)].bitcast(E4M3),
-                scales=xm_scales[:, k * (D // 2) : (k + 1) * (D // 2)],
-                in_=grouped[:].rearrange("p n t -> p (n t)"),
-            )
+            quantize(xm_codes[:, cols], xm_scales[:, cols], grouped[:], E4M3)
 
         h_grouped, h_codes, h_scales = [], [], []
         for c in range(2):
-            h_grouped.append(tail.tile([P, 2 * CHUNK + c * P, PACK], BF16, name="h_grouped%d" % c, align_bytes=64, offset=c * (4 * N + 4 * T - 512)))
+            shape, place = [P, 2 * CHUNK + c * P, PACK], c * (SUMS_BYTES + WINDOW_BYTES - OVERLAP)
+            h_grouped.append(tail.tile(shape, BF16, name="h_grouped%d" % c, align_bytes=64, offset=place))
             h_codes.append(keep.tile([P, 2 * CHUNK], U32, name="h_codes%d" % c, align_bytes=64))
             h_scales.append(keep.tile([P, 2 * CHUNK], U8, name="h_scales%d" % c, align_bytes=64))
 
         margin, turned = {}, {}
 
-        def dealt(acc):
-            return acc[:].rearrange("p (m t) -> p t m", t=PACK)
+        def dealt(score):
+            return score[:].rearrange("p (m t) -> p t m", t=PACK)
 
         def margins(b):
             score = []
             for side in range(2):
-                cols = slice(b * P, (b + 1) * P)
-                score.append(ps_a.tile([P, R], F32, name="acc"))
+                codes, scales = w_mx[side * BLOCKS + b]
+                score.append(ps_score.tile([P, R], F32, name="score"))
                 nc.tensor.matmul_mx(
                     out=score[side][:],
-                    lhsT=w_codes[side][:, cols].bitcast(E4M3),
-                    lhsT_scale=w_scales[side][:, cols],
+                    lhsT=codes.bitcast(E4M3),
+                    lhsT_scale=scales,
                     rhs=x_codes[:].bitcast(E4M3),
                     rhs_scale=x_scales[:],
                     start=True,
                     stop=True,
                 )
-            neg_pos = keep.tile([P, PACK, P], F32, name="neg_pos%d" % b, tag="neg_pos%d" % b if b < 2 else "margin%d" % (b - 2), align_bytes=64)
+            tag = "neg_pos%d" % b if b < 2 else "margin%d" % (b - 2)
+            neg_pos = keep.tile([P, PACK, P], F32, name="neg_pos%d" % b, tag=tag, align_bytes=64)
             nc.scalar.activation(out=neg_pos[:], in_=dealt(score[0]), func=ACT.Copy, scale=ts_col[0][:, b : b + 1])
             margin[b] = keep.tile([P, PACK, P], F32, name="margin%d" % b, align_bytes=64)
             nc.vector.scalar_tensor_tensor(
@@ -237,25 +225,27 @@ def tile_attend_gbpr_w_ts_kernel(tc, xT, wT, wt, ts, xm, offs, out):
         def sigmoid(b):
             sig = keep.tile([P, PACK, P], F32, name="sig%d" % b, align_bytes=64)
             nc.scalar.activation(out=sig[:], in_=margin[b][:], func=ACT.Sigmoid)
-            turned[b] = ps_b.tile([P, PACK, P], F32, name="late")
+            turned[b] = ps_turn.tile([P, PACK, P], F32, name="turn")
             for t in range(PACK):
                 nc.tensor.transpose(turned[b][:, t, :], sig[:, t, :], ident[:])
 
         def gradient(b, side):
             c, first = b // 2, side * CHUNK + (b % 2) * P
             nc.vector.tensor_tensor(
-                out=h_grouped[c][:, first : first + P, :].rearrange("p (g i) t -> p g t i", i=4),
-                in0=turned[b][:].rearrange("p t (g i) -> p g t i", i=4),
-                in1=factor[:, c, :, first : first + P].rearrange("p t (g i) -> p g t i", i=4),
+                out=h_grouped[c][:, first : first + P, :].rearrange("p (g i) t -> p g t i", i=RUN),
+                in0=turned[b][:].rearrange("p t (g i) -> p g t i", i=RUN),
+                in1=factor[:, c, :, first : first + P].rearrange("p t (g i) -> p g t i", i=RUN),
                 op=ALU.mult,
             )
 
-        def operand(c, side):
-            quantize(h_codes[c], h_scales[c], h_grouped[c], side * CHUNK, CHUNK, E5M2)
+        def quantize_h(c, side):
+            cols = slice(side * CHUNK, (side + 1) * CHUNK)
+            quantize(h_codes[c][:, cols], h_scales[c][:, cols], h_grouped[c][:, cols, :], E5M2)
 
-        dw = {j: keep.tile([P, N], F32, name="dw%d" % j) for j in (0, 1, 3)}
+        sums = {j: keep.tile([P, N], F32, name="sums%d" % j) for j in (0, 1, 3)}
 
-        def table_sums(c, j, acc, on_vector, sides=slice(0, 2)):
+        def table_sums(c, j, pool, on_vector, sides=slice(0, 2)):
+            acc = pool.tile([P, 2 * CHUNK], F32, name="score" if pool is ps_score else "turn")
             cols = slice(sides.start * CHUNK, sides.stop * CHUNK)
             nc.tensor.matmul_mx(
                 out=acc[:, cols],
@@ -266,30 +256,36 @@ def tile_attend_gbpr_w_ts_kernel(tc, xT, wT, wt, ts, xm, offs, out):
                 start=True,
                 stop=True,
             )
-            dst = dw[j][:].rearrange("p (s c i) -> p s c i", s=2, c=2)[:, sides, c]
+            dst = sums[j][:].rearrange("p (s c i) -> p s c i", s=2, c=2)[:, sides, c]
             src = acc[:].rearrange("p (s i) -> p s i", s=2)[:, sides]
             if on_vector:
                 nc.vector.tensor_copy(out=dst, in_=src)
             else:
                 nc.scalar.copy(out=dst, in_=src)
 
-        def scatter(j, first, count, on_vector):
+        def scatter(j, first, count):
             place = out_win[j][:].indirect(slots(first, count))
-            if on_vector:
-                nc.vector.tensor_copy(out=place, in_=dw[j][:, first : first + count])
+            if j % 2 == 0:
+                nc.vector.tensor_copy(out=place, in_=sums[j][:, first : first + count])
             else:
-                nc.scalar.activation(out=place, in_=dw[j][:, first : first + count], func=ACT.Copy)
+                nc.scalar.activation(out=place, in_=sums[j][:, first : first + count], func=ACT.Copy)
 
         def store(j):
             nc.sync.dma_start(out=out[j * P : (j + 1) * P, :], in_=out_win[j][:])
 
-        def bank(pool, name):
-            return pool.tile([P, 2 * CHUNK], F32, name=name)
-
-        quantize_xm(0, "xm_grouped0")
+        xm_first = woven.tile([P, D // 2, PACK], BF16, name="xm_first", align_bytes=64, offset=2 * PACK * N)
+        quantize_xm(0, xm_first)
         factor = woven.tile([P, 2, PACK, 2 * CHUNK], F32, name="factor", align_bytes=64, offset=0)
-        factors(0)
-        factors(1)
+        for c in range(2):
+            for t in range(PACK):
+                nc.gpsimd.tensor_scalar(
+                    out=factor[:, c, t, :],
+                    in0=ts_rows[:, c, :],
+                    scalar1=wt_cols[:, t : t + 1],
+                    scalar2=0.0,
+                    op0=ALU.mult,
+                    op1=ALU.add,
+                )
         margins(0)
         margins(1)
         sigmoid(0)
@@ -298,39 +294,42 @@ def tile_attend_gbpr_w_ts_kernel(tc, xT, wT, wt, ts, xm, offs, out):
         gradient(0, 0)
         gradient(1, 0)
         margins(3)
-        operand(0, 0)
+        quantize_h(0, 0)
         gradient(0, 1)
         gradient(1, 1)
-        operand(0, 1)
+        quantize_h(0, 1)
         sigmoid(2)
         sigmoid(3)
-        quantize_xm(1, "margin2")
+        xm_second = keep.tile([P, D // 2, PACK], BF16, name="xm_second", tag="margin2", align_bytes=64)
+        quantize_xm(1, xm_second)
         for side in range(2):
             gradient(2, side)
             gradient(3, side)
-            operand(1, side)
+            quantize_h(1, side)
+
         for j in (3, 2):
-            out_win[j] = tail.tile([P, T], F32, name="out_win%d" % j, offset=4 * N + (3 - j) * (4 * T + 4 * N))
+            place = SUMS_BYTES + (3 - j) * (WINDOW_BYTES + SUMS_BYTES)
+            out_win[j] = tail.tile([P, T], F32, name="out_win%d" % j, offset=place)
             nc.gpsimd.memset(out_win[j][:].bitcast(U32), 0)
-        table_sums(0, 1, bank(ps_a, "acc"), False, slice(0, 1))
-        scatter(1, 0, CHUNK, False)
-        table_sums(0, 1, bank(ps_a, "acc"), False, slice(1, 2))
-        table_sums(0, 0, bank(ps_a, "acc"), False)
-        scatter(1, HALF, CHUNK, False)
-        table_sums(0, 3, bank(ps_a, "acc"), False)
-        dw[2] = tail.tile([P, N], F32, name="dw2", offset=4 * N + 4 * T)
-        table_sums(0, 2, bank(ps_a, "acc"), True)
-        table_sums(1, 0, bank(ps_a, "acc"), True)
-        table_sums(1, 1, bank(ps_a, "acc"), False)
-        scatter(0, 0, N, True)
+        table_sums(0, 1, ps_score, False, slice(0, 1))
+        scatter(1, 0, CHUNK)
+        table_sums(0, 1, ps_score, False, slice(1, 2))
+        table_sums(0, 0, ps_score, False)
+        scatter(1, HALF, CHUNK)
+        table_sums(0, 3, ps_score, False)
+        sums[2] = tail.tile([P, N], F32, name="sums2", offset=SUMS_BYTES + WINDOW_BYTES)
+        table_sums(0, 2, ps_score, True)
+        table_sums(1, 0, ps_score, True)
+        table_sums(1, 1, ps_score, False)
+        scatter(0, 0, N)
         store(0)
-        scatter(1, CHUNK, CHUNK, False)
-        table_sums(1, 3, bank(ps_b, "late"), False)
-        scatter(1, HALF + CHUNK, CHUNK, False)
+        scatter(1, CHUNK, CHUNK)
+        table_sums(1, 3, ps_turn, False)
+        scatter(1, HALF + CHUNK, CHUNK)
         store(1)
-        table_sums(1, 2, bank(ps_b, "late"), True)
-        for first, count in ((0, WIDE), (WIDE, WIDE), (2 * WIDE, CHUNK)):
-            scatter(3, first, count, False)
+        table_sums(1, 2, ps_turn, True)
+        for first in range(0, N, WIDE):
+            scatter(3, first, min(WIDE, N - first))
         store(3)
-        scatter(2, 0, N, True)
+        scatter(2, 0, N)
         store(2)

@@ -6,6 +6,7 @@ from concourse.masks import make_identity
 F32 = mybir.dt.float32
 BF16 = mybir.dt.bfloat16
 U32 = mybir.dt.uint32
+I32 = mybir.dt.int32
 U16 = mybir.dt.uint16
 U8 = mybir.dt.uint8
 E4M3 = mybir.dt.float8_e4m3fn_x4
@@ -30,11 +31,6 @@ W_LOADS = (
 )
 FIRST_PAIR_LOADS = 2
 WIDE = 384
-SCORE_BANKS = 6
-TURN_BANKS = 2
-WINDOW_BYTES = 4 * T
-SUMS_BYTES = 4 * N
-OVERLAP = 512
 FLOPS = 2 * 2 * N * D * R
 
 
@@ -42,85 +38,87 @@ def tile_attend_gbpr_w_ts_kernel(tc, xT, wT, wt, ts, xm, offs, out):
     nc = tc.nc
     with ExitStack() as ctx:
         keep = ctx.enter_context(tc.tile_pool(name="keep", bufs=1))
-        pairs = ctx.enter_context(tc.tile_pool(name="pairs", bufs=1))
-        woven = ctx.enter_context(tc.tile_pool(name="woven", bufs=1))
-        xpool = ctx.enter_context(tc.tile_pool(name="xpool", bufs=1))
         tail = ctx.enter_context(tc.tile_pool(name="tail", bufs=1))
-        ps_score = ctx.enter_context(tc.psum_pool(name="ps_score", bufs=SCORE_BANKS))
-        ps_turn = ctx.enter_context(tc.psum_pool(name="ps_turn", bufs=TURN_BANKS))
+        psum = ctx.enter_context(tc.psum_pool(name="psum", bufs=1))
+
+        def bank(number, shape):
+            return psum.tile(shape, F32, name="bank%d" % number)
+
+        def sbuf(shape, dtype, name, on=None):
+            return keep.tile(shape, dtype, name=name, tag=on or name, align_bytes=64)
 
         def slots(first, count):
             return offsets[:, first // 16 : (first + count) // 16]
 
-        seed = keep.tile([P, 1], F32, name="seed")
+        seed = sbuf([P, 1], F32, "seed")
         nc.vector.memset(seed[:], 0.0)
-        ts_win = keep.tile([P, T], F32, name="ts_win")
+        ts_win = sbuf([P, T], F32, "ts_win")
         nc.sync.dma_start(out=ts_win[P - 1 : P, :], in_=ts[0:1, :])
         nc.gpsimd.memset(ts_win[0 : P - 1, :].bitcast(U32), 0)
-        ident = keep.tile([P, P], F32, name="ident")
+        ident = sbuf([P, P], F32, "ident")
         nc.vector.memset(ident[:], 0.0)
         make_identity(nc, ident[:], nomemset=True)
-        warm = keep.tile([P, 1], F32, name="warm")
+        warm = sbuf([P, 1], F32, "warm")
         nc.scalar.activation(out=warm[:], in_=seed[:], func=ACT.Sigmoid)
 
         offsets = keep.tile([P, N // 16], U16, name="offsets")
         nc.sync.dma_start(offsets[:], offs)
-        wt_cols = keep.tile([P, PACK], F32, name="wt_cols")
+        wt_cols = sbuf([P, PACK], F32, "wt_cols")
         w_rows = wT.rearrange("(p u e) c -> p u e c", u=2, e=2)
         w_raw = []
         for k, (u, first, count, on_vector) in enumerate(W_LOADS):
-            w_raw.append(keep.tile([P, 2, count], F32, name="w_raw%d" % k, align_bytes=64))
+            w_raw.append(sbuf([P, 2, count], F32, "w_raw%d" % k))
             nc.sync.dma_start(out=w_raw[k][:], in_=w_rows[:, u, :, first : first + count])
-            if k == FIRST_PAIR_LOADS - 1:
+            if k == 0:
                 nc.sync.dma_start(out=wt_cols[:], in_=wt[0].rearrange("(p t) o -> p (t o)", t=PACK))
         x_rows = xT[0].rearrange("(p t) r -> p t r", t=PACK)
         x_raw = []
         for k in range(2):
-            x_raw.append(keep.tile([P, PACK, R // 2], F32, name="x_raw%d" % k))
+            x_raw.append(sbuf([P, PACK, R // 2], F32, "x_raw%d" % k))
             nc.sync.dma_start(out=x_raw[k][:], in_=x_rows[:, :, k * (R // 2) : (k + 1) * (R // 2)])
         xm_rows = xm[0].rearrange("(p t) d -> p t d", t=PACK)
         xm_raw = []
         for k in range(2):
-            xm_raw.append(keep.tile([P, PACK, D // 2], F32, name="xm_raw%d" % k))
+            xm_raw.append(sbuf([P, PACK, D // 2], F32, "xm_raw%d" % k))
             nc.sync.dma_start(out=xm_raw[k][:], in_=xm_rows[:, :, k * (D // 2) : (k + 1) * (D // 2)])
 
-        out_win = {j: keep.tile([P, T], F32, name="out_win%d" % j) for j in (0, 1)}
+        out_win = {j: sbuf([P, T], F32, "out_win%d" % j) for j in (0, 1)}
         nc.vector.memset(out_win[0][:, 0 : T - 1].bitcast(U32), 0)
         nc.vector.memset(out_win[0][:, T - 1 : T].bitcast(U32), 0)
         nc.gpsimd.memset(out_win[1][:].bitcast(U32), 0)
 
-        ts_got = keep.tile([P, N], F32, name="ts_got")
+        ts_got = sbuf([P, N], F32, "ts_got")
         nc.vector.tensor_copy(out=ts_got[:, 0:HALF], in_=ts_win[:].indirect(slots(0, HALF)))
         nc.scalar.activation(out=ts_got[:, HALF:], in_=ts_win[:].indirect(slots(HALF, HALF)), func=ACT.Copy)
-        ts_turned = []
+        ts_first = sbuf([P, 2, BLOCKS], F32, "ts_first")
         for side in range(2):
-            ts_turned.append(ps_score.tile([P, BLOCKS, P], F32, name="score"))
+            turned = bank(side, [P, BLOCKS, P])
             for b in range(BLOCKS):
                 first = side * HALF + b * P
-                nc.tensor.transpose(ts_turned[side][:, b, :], ts_got[:, first : first + P], ident[:])
-
-        def signed_ts(dst, side):
-            nc.scalar.activation(out=dst, in_=ts_turned[side][:, :, P - 1], func=ACT.Copy, scale=SIGN[side])
-
-        ts_col = []
-        for side in range(2):
-            ts_col.append(keep.tile([P, BLOCKS], F32, name="ts_col%d" % side))
-            signed_ts(ts_col[side][:], side)
-        ts_spread = []
-        for side in range(2):
-            ts_spread.append(pairs.tile([P, BLOCKS], F32, name="ts_spread%d" % side, offset=32 * side))
-            signed_ts(ts_spread[side][:], side)
-        ts_rows = keep.tile([P, 2, 2 * CHUNK], F32, name="ts_rows")
+                nc.tensor.transpose(turned[:, b, :], ts_got[:, first : first + P], ident[:])
+            nc.scalar.activation(out=ts_first[:, side, :], in_=turned[:, :, P - 1], func=ACT.Copy, scale=SIGN[side])
+        ts_col = sbuf([P, 2, BLOCKS], F32, "ts_col")
+        nc.gpsimd.tensor_copy(out=ts_col[:], in_=ts_first[:])
+        spread = []
         for c in range(2):
-            spread = ps_turn.tile([P, 2, 2, P], F32, name="turn")
+            spread.append(bank(6 + c, [P, 2, 2, P]))
             for side in range(2):
                 for b in range(2):
-                    col = ts_spread[side][:, 2 * c + b : 2 * c + b + 1]
-                    nc.tensor.transpose(spread[:, side, b, :], col.to_broadcast([P, P]), ident[:])
-            nc.scalar.copy(out=ts_rows[:, c, :], in_=spread[:].rearrange("p s b i -> p (s b i)"))
+                    col = ts_first[:, side, 2 * c + b : 2 * c + b + 1]
+                    nc.tensor.transpose(spread[c][:, side, b, :], col.to_broadcast([P, P]), ident[:])
+        ts_rows = sbuf([P, 2 * CHUNK], F32, "ts_rows")
+        nc.scalar.copy(out=ts_rows[:], in_=spread[0][:].rearrange("p s b i -> p (s b i)"))
+        factor = {1: sbuf([P, PACK, 2 * CHUNK], F32, "factor1")}
+        for t in range(PACK):
+            nc.scalar.activation(
+                out=factor[1][:, t, :],
+                in_=spread[1][:].rearrange("p s b i -> p (s b i)"),
+                func=ACT.Copy,
+                scale=wt_cols[:, t : t + 1],
+            )
 
-        w_pair = [keep.tile([P, T, 2], BF16, name="w_pair0"), pairs.tile([P, T, 2], BF16, name="w_pair1", offset=0)]
-        w_grouped = woven.tile([P, N, PACK], BF16, name="w_grouped", align_bytes=64, offset=0)
+        w_pair = [sbuf([P, T, 2], BF16, "w_pair0"), sbuf([P, T, 2], BF16, "w_pair1", on="ts_first")]
+        w_grouped = [sbuf([P, CHUNK, PACK], BF16, "w_grouped%d" % q) for q in range(4)]
         w_mx = {}
 
         def cast(k, lo, hi, on_vector):
@@ -139,102 +137,176 @@ def tile_attend_gbpr_w_ts_kernel(tc, xT, wT, wt, ts, xm, offs, out):
             if on_vector:
                 cast(k, count - on_vector, count, True)
 
-        def gather(u):
+        def gather(u, q):
             window = w_pair[u][:].rearrange("p c e -> p (c e)").bitcast(U32)
-            words = w_grouped[:].rearrange("p n t -> p (n t)").bitcast(U32).rearrange("p (n u) -> p n u", u=2)
-            nc.vector.tensor_copy(out=words[:, :, u], in_=window.indirect(offsets[:]))
+            words = w_grouped[q][:].rearrange("p n t -> p (n t)").bitcast(U32).rearrange("p (n u) -> p n u", u=2)
+            nc.vector.tensor_copy(out=words[:, :, u], in_=window.indirect(slots(q * CHUNK, CHUNK)))
 
         def quantize(codes, scales, grouped, fmt):
             nc.vector.quantize_mx(out=codes.bitcast(fmt), scales=scales, in_=grouped.rearrange("p n t -> p (n t)"))
 
-        def quantize_table(first, codes):
-            count = codes.shape[1]
-            scales = keep.tile([P, count], U8, name="w_scales%d" % first, align_bytes=64)
-            quantize(codes[:], scales[:], w_grouped[:, first : first + count, :], E4M3)
-            for col in range(0, count, P):
-                w_mx[(first + col) // P] = (codes[:, col : col + P], scales[:, col : col + P])
+        def quantize_table(q, codes):
+            scales = sbuf([P, CHUNK], U8, "w_scales%d" % q)
+            quantize(codes, scales[:], w_grouped[q][:], E4M3)
+            for b in range(2):
+                w_mx[2 * q + b] = (codes[:, b * P : (b + 1) * P], scales[:, b * P : (b + 1) * P])
 
         def interleave(dst, src):
             dst = dst.rearrange("p (c i) t -> p c t i", i=RUN)
             src = src.rearrange("p t (c i) -> p c t i", i=RUN)
             nc.scalar.activation(out=dst, in_=src, func=ACT.Copy)
 
-        for k in range(FIRST_PAIR_LOADS):
-            cast_load(k)
-        gather(0)
+        cast_load(0)
+        cast_load(1)
+        factor[0] = sbuf([P, PACK, 2 * CHUNK], F32, "factor0", on="w_raw1")
+        for t in range(PACK):
+            nc.gpsimd.tensor_scalar(
+                out=factor[0][:, t, :],
+                in0=ts_rows[:],
+                scalar1=wt_cols[:, t : t + 1],
+                scalar2=0.0,
+                op0=ALU.mult,
+                op1=ALU.add,
+            )
+        for q in range(4):
+            gather(0, q)
         for k in range(FIRST_PAIR_LOADS, len(W_LOADS)):
             cast_load(k)
-        gather(1)
-        quantize_table(0, keep.tile([P, CHUNK], U32, name="w_codes_first", align_bytes=64))
-        x_grouped = xpool.tile([P, R, PACK], BF16, name="x_grouped", align_bytes=64, offset=0)
-        x_codes = keep.tile([P, R], U32, name="x_codes", align_bytes=64)
-        x_scales = keep.tile([P, R], U8, name="x_scales", align_bytes=64)
-        for k in range(2):
-            interleave(x_grouped[:, k * (R // 2) : (k + 1) * (R // 2), :], x_raw[k][:])
-        quantize(x_codes[:], x_scales[:], x_grouped[:], E4M3)
-        quantize_table(HALF, xpool.tile([P, HALF], U32, name="w_codes_neg", align_bytes=64, offset=0))
-        quantize_table(CHUNK, xpool.tile([P, CHUNK], U32, name="w_codes_rest", align_bytes=64, offset=4 * HALF))
+        x_codes = sbuf([P, R], U32, "x_codes")
+        x_scales = sbuf([P, R], U8, "x_scales")
+        x_grouped = [sbuf([P, R // 2, PACK], BF16, "x_grouped%d" % k) for k in range(2)]
 
-        xm_codes = keep.tile([P, D], U32, name="xm_codes", align_bytes=64)
-        xm_scales = keep.tile([P, D], U8, name="xm_scales", align_bytes=64)
+        def quantize_x(k):
+            cols = slice(k * (R // 2), (k + 1) * (R // 2))
+            interleave(x_grouped[k][:], x_raw[k][:])
+            quantize(x_codes[:, cols], x_scales[:, cols], x_grouped[k][:], E4M3)
 
-        def quantize_xm(k, grouped):
-            cols = slice(k * (D // 2), (k + 1) * (D // 2))
-            interleave(grouped[:], xm_raw[k][:])
-            quantize(xm_codes[:, cols], xm_scales[:, cols], grouped[:], E4M3)
+        def gather_held(q, on):
+            got = sbuf([P, CHUNK], U32, "w_got%d" % q, on=on)
+            window = w_pair[1][:].rearrange("p c e -> p (c e)").bitcast(U32)
+            nc.vector.tensor_copy(out=got[:], in_=window.indirect(slots(q * CHUNK, CHUNK)))
+            return got
 
-        h_grouped, h_codes, h_scales = [], [], []
-        for c in range(2):
-            shape, place = [P, 2 * CHUNK + c * P, PACK], c * (SUMS_BYTES + WINDOW_BYTES - OVERLAP)
-            h_grouped.append(tail.tile(shape, BF16, name="h_grouped%d" % c, align_bytes=64, offset=place))
-            h_codes.append(keep.tile([P, 2 * CHUNK], U32, name="h_codes%d" % c, align_bytes=64))
-            h_scales.append(keep.tile([P, 2 * CHUNK], U8, name="h_scales%d" % c, align_bytes=64))
+        def odd_words(q, dtype):
+            words = w_grouped[q][:].rearrange("p n t -> p (n t)").bitcast(dtype)
+            return words.rearrange("p (n u) -> p n u", u=2)[:, :, 1]
 
-        margin, turned = {}, {}
+        early_codes = sbuf([P, 2, CHUNK], U32, "early_codes")
+        gather(1, 0)
+        gather(1, 2)
+        quantize_table(0, early_codes[:, 0, :])
+        quantize_table(2, early_codes[:, 1, :])
+        quantize_x(0)
+        got1 = gather_held(1, "x_grouped0")
+        quantize_x(1)
+        got3 = gather_held(3, "x_grouped1")
+        nc.scalar.copy(out=odd_words(1, U32), in_=got1[:])
+        quantize_table(1, sbuf([P, CHUNK], U32, "w_codes1")[:])
+        nc.vector.tensor_copy(out=odd_words(3, I32), in_=got3[:].bitcast(I32))
 
-        def dealt(score):
-            return score[:].rearrange("p (m t) -> p t m", t=PACK)
+        xm_scales = sbuf([P, D], U8, "xm_scales")
 
-        def margins(b):
-            score = []
-            for side in range(2):
-                codes, scales = w_mx[side * BLOCKS + b]
-                score.append(ps_score.tile([P, R], F32, name="score"))
-                nc.tensor.matmul_mx(
-                    out=score[side][:],
-                    lhsT=codes.bitcast(E4M3),
-                    lhsT_scale=scales,
-                    rhs=x_codes[:].bitcast(E4M3),
-                    rhs_scale=x_scales[:],
-                    start=True,
-                    stop=True,
+        xm_grouped = {}
+
+        def round_xm(k, on, on_scalar):
+            xm_grouped[k] = sbuf([P, D // 2, PACK], BF16, "xm_grouped%d" % k, on=on)
+            if on_scalar:
+                interleave(xm_grouped[k][:], xm_raw[k][:])
+            else:
+                nc.gpsimd.tensor_scalar(
+                    out=xm_grouped[k][:],
+                    in0=xm_raw[k][:].rearrange("p t c -> p c t"),
+                    scalar1=1.0,
+                    scalar2=0.0,
+                    op0=ALU.mult,
+                    op1=ALU.add,
                 )
-            tag = "neg_pos%d" % b if b < 2 else "margin%d" % (b - 2)
-            neg_pos = keep.tile([P, PACK, P], F32, name="neg_pos%d" % b, tag=tag, align_bytes=64)
-            nc.scalar.activation(out=neg_pos[:], in_=dealt(score[0]), func=ACT.Copy, scale=ts_col[0][:, b : b + 1])
-            margin[b] = keep.tile([P, PACK, P], F32, name="margin%d" % b, align_bytes=64)
+
+        xm_codes = {}
+
+        def quantize_xm(k, on=None):
+            cols = slice(k * (D // 2), (k + 1) * (D // 2))
+            xm_codes[k] = sbuf([P, D // 2], U32, "xm_codes%d" % k, on=on)
+            quantize(xm_codes[k][:], xm_scales[:, cols], xm_grouped[k][:], E4M3)
+
+        score, scaled, sig = {}, {}, {}
+
+        def scores(b, side, number, cols=slice(0, R)):
+            codes, scales = w_mx[side * BLOCKS + b]
+            if cols.start == 0:
+                score[b, side] = bank(number, [P, R])
+            nc.tensor.matmul_mx(
+                out=score[b, side][:, cols],
+                lhsT=codes.bitcast(E4M3),
+                lhsT_scale=scales,
+                rhs=x_codes[:, cols].bitcast(E4M3),
+                rhs_scale=x_scales[:, cols],
+                start=True,
+                stop=True,
+            )
+
+        def dealt(b, side):
+            return score[b, side][:].rearrange("p (m t) -> p t m", t=PACK)
+
+        def scale(dst, b, side):
+            nc.scalar.activation(out=dst, in_=dealt(b, side), func=ACT.Copy, scale=ts_col[:, side, b : b + 1])
+
+        margin = {}
+
+        def margin_on_vector(b):
+            scaled[b] = sbuf([P, PACK, P], F32, "scaled%d" % b)
+            scale(scaled[b][:], b, 0)
+            margin[b] = sbuf([P, PACK, P], F32, "margin%d" % b)
             nc.vector.scalar_tensor_tensor(
                 out=margin[b][:],
-                in0=dealt(score[1]),
-                scalar=ts_col[1][:, b : b + 1],
-                in1=neg_pos[:],
+                in0=dealt(b, 1),
+                scalar=ts_col[:, 1, b : b + 1],
+                in1=scaled[b][:],
                 op0=ALU.mult,
                 op1=ALU.add,
             )
 
-        def sigmoid(b):
-            sig = keep.tile([P, PACK, P], F32, name="sig%d" % b, align_bytes=64)
-            nc.scalar.activation(out=sig[:], in_=margin[b][:], func=ACT.Sigmoid)
-            turned[b] = ps_turn.tile([P, PACK, P], F32, name="turn")
+        def sigmoid_then_turn(b, number):
+            flat = sbuf([P, PACK, P], F32, "flat%d" % b)
+            nc.scalar.activation(out=flat[:], in_=margin[b][:], func=ACT.Sigmoid)
+            sig[b] = bank(number, [P, PACK, P])
             for t in range(PACK):
-                nc.tensor.transpose(turned[b][:, t, :], sig[:, t, :], ident[:])
+                nc.tensor.transpose(sig[b][:, t, :], flat[:, t, :], ident[:])
+
+        def turn_then_sigmoid(b, number):
+            turned = bank(number, [P, PACK, P])
+            for t in range(PACK):
+                for side in range(2):
+                    nc.tensor.matmul(
+                        turned[:, t, :],
+                        lhsT=late[:, b - 2, side, t, :],
+                        rhs=ident[:],
+                        start=side == 0,
+                        stop=side == 1,
+                        is_transpose=True,
+                    )
+            sig[b] = sbuf([P, PACK, P], F32, "sig%d" % b)
+            nc.scalar.activation(out=sig[b][:], in_=turned[:], func=ACT.Sigmoid)
+
+        h_grouped = {0: sbuf([P, 2 * CHUNK, PACK], BF16, "h_grouped0")}
+        h_codes = [sbuf([P, 2 * CHUNK], U32, "h_codes%d" % c) for c in range(2)]
+        h_scales = [sbuf([P, 2 * CHUNK], U8, "h_scales%d" % c) for c in range(2)]
 
         def gradient(b, side):
             c, first = b // 2, side * CHUNK + (b % 2) * P
             nc.vector.tensor_tensor(
                 out=h_grouped[c][:, first : first + P, :].rearrange("p (g i) t -> p g t i", i=RUN),
-                in0=turned[b][:].rearrange("p t (g i) -> p g t i", i=RUN),
-                in1=factor[:, c, :, first : first + P].rearrange("p t (g i) -> p g t i", i=RUN),
+                in0=sig[b][:].rearrange("p t (g i) -> p g t i", i=RUN),
+                in1=factor[c][:, :, first : first + P].rearrange("p t (g i) -> p g t i", i=RUN),
+                op=ALU.mult,
+            )
+
+        def gradient_on_gpsimd(b, side):
+            c, first = b // 2, side * CHUNK + (b % 2) * P
+            nc.gpsimd.tensor_tensor(
+                out=h_grouped[c][:, first : first + P, :],
+                in0=sig[b][:],
+                in1=factor[c][:, :, first : first + P].rearrange("p t i -> p i t"),
                 op=ALU.mult,
             )
 
@@ -242,22 +314,21 @@ def tile_attend_gbpr_w_ts_kernel(tc, xT, wT, wt, ts, xm, offs, out):
             cols = slice(side * CHUNK, (side + 1) * CHUNK)
             quantize(h_codes[c][:, cols], h_scales[c][:, cols], h_grouped[c][:, cols, :], E5M2)
 
-        sums = {j: keep.tile([P, N], F32, name="sums%d" % j) for j in (0, 1, 3)}
+        sums = {}
 
-        def table_sums(c, j, pool, on_vector, sides=slice(0, 2)):
-            acc = pool.tile([P, 2 * CHUNK], F32, name="score" if pool is ps_score else "turn")
-            cols = slice(sides.start * CHUNK, sides.stop * CHUNK)
+        def table_sums(c, j, number, on_vector):
+            acc = bank(number, [P, 2 * CHUNK])
             nc.tensor.matmul_mx(
-                out=acc[:, cols],
-                lhsT=xm_codes[:, j * P : (j + 1) * P].bitcast(E4M3),
+                out=acc[:],
+                lhsT=xm_codes[j // 2][:, (j % 2) * P : (j % 2 + 1) * P].bitcast(E4M3),
                 lhsT_scale=xm_scales[:, j * P : (j + 1) * P],
-                rhs=h_codes[c][:, cols].bitcast(E5M2),
-                rhs_scale=h_scales[c][:, cols],
+                rhs=h_codes[c][:].bitcast(E5M2),
+                rhs_scale=h_scales[c][:],
                 start=True,
                 stop=True,
             )
-            dst = sums[j][:].rearrange("p (s c i) -> p s c i", s=2, c=2)[:, sides, c]
-            src = acc[:].rearrange("p (s i) -> p s i", s=2)[:, sides]
+            dst = sums[j][:].rearrange("p (s c i) -> p s c i", s=2, c=2)[:, :, c]
+            src = acc[:].rearrange("p (s i) -> p s i", s=2)
             if on_vector:
                 nc.vector.tensor_copy(out=dst, in_=src)
             else:
@@ -273,61 +344,65 @@ def tile_attend_gbpr_w_ts_kernel(tc, xT, wT, wt, ts, xm, offs, out):
         def store(j):
             nc.sync.dma_start(out=out[j * P : (j + 1) * P, :], in_=out_win[j][:])
 
-        xm_first = woven.tile([P, D // 2, PACK], BF16, name="xm_first", align_bytes=64, offset=2 * PACK * N)
-        quantize_xm(0, xm_first)
-        factor = woven.tile([P, 2, PACK, 2 * CHUNK], F32, name="factor", align_bytes=64, offset=0)
-        for c in range(2):
-            for t in range(PACK):
-                nc.gpsimd.tensor_scalar(
-                    out=factor[:, c, t, :],
-                    in0=ts_rows[:, c, :],
-                    scalar1=wt_cols[:, t : t + 1],
-                    scalar2=0.0,
-                    op0=ALU.mult,
-                    op1=ALU.add,
-                )
-        margins(0)
-        margins(1)
-        sigmoid(0)
-        sigmoid(1)
-        margins(2)
+        round_xm(0, "x_grouped1", False)
+        round_xm(1, None, False)
+        for k in range(2):
+            for b in range(2):
+                for side in range(2):
+                    scores(b, side, 2 * b + side, slice(k * (R // 2), (k + 1) * (R // 2)))
+        margin_on_vector(0)
+        margin_on_vector(1)
+        quantize_table(3, sbuf([P, CHUNK], U32, "w_codes3", on="scaled1")[:])
+        scores(2, 0, 4)
+        scores(3, 0, 5)
+        sigmoid_then_turn(0, 6)
+        sigmoid_then_turn(1, 7)
+        scores(2, 1, 1)
+        scores(3, 1, 3)
+        late = sbuf([P, 2, 2, PACK, P], F32, "late", on="margin1")
+        scale(late[:, 0, 0], 2, 0)
+        scale(late[:, 1, 0], 3, 0)
+        scale(late[:, 0, 1], 2, 1)
+        scale(late[:, 1, 1], 3, 1)
         gradient(0, 0)
-        gradient(1, 0)
-        margins(3)
-        quantize_h(0, 0)
         gradient(0, 1)
+        quantize_xm(0, "flat1")
+        gradient(1, 0)
         gradient(1, 1)
+        quantize_h(0, 0)
         quantize_h(0, 1)
-        sigmoid(2)
-        sigmoid(3)
-        xm_second = keep.tile([P, D // 2, PACK], BF16, name="xm_second", tag="margin2", align_bytes=64)
-        quantize_xm(1, xm_second)
-        for side in range(2):
-            gradient(2, side)
-            gradient(3, side)
-            quantize_h(1, side)
-
-        for j in (3, 2):
-            place = SUMS_BYTES + (3 - j) * (WINDOW_BYTES + SUMS_BYTES)
-            out_win[j] = tail.tile([P, T], F32, name="out_win%d" % j, offset=place)
-            nc.gpsimd.memset(out_win[j][:].bitcast(U32), 0)
-        table_sums(0, 1, ps_score, False, slice(0, 1))
+        quantize_xm(1, "h_grouped0")
+        turn_then_sigmoid(2, 0)
+        turn_then_sigmoid(3, 2)
+        h_grouped[1] = tail.tile([P, 2 * CHUNK, PACK], BF16, name="h_grouped1", align_bytes=64, offset=4 * T - 2048)
+        sums[0] = sbuf([P, N], F32, "sums0")
+        sums[1] = sbuf([P, N], F32, "sums1", on="margin1")
+        table_sums(0, 0, 7, False)
+        table_sums(0, 1, 6, False)
+        gradient(2, 0)
+        gradient(2, 1)
+        gradient(3, 0)
+        gradient(3, 1)
+        quantize_h(1, 0)
+        quantize_h(1, 1)
         scatter(1, 0, CHUNK)
-        table_sums(0, 1, ps_score, False, slice(1, 2))
-        table_sums(0, 0, ps_score, False)
         scatter(1, HALF, CHUNK)
-        table_sums(0, 3, ps_score, False)
-        sums[2] = tail.tile([P, N], F32, name="sums2", offset=SUMS_BYTES + WINDOW_BYTES)
-        table_sums(0, 2, ps_score, True)
-        table_sums(1, 0, ps_score, True)
-        table_sums(1, 1, ps_score, False)
+        for j in (3, 2):
+            out_win[j] = tail.tile([P, T], F32, name="out_win%d" % j, align_bytes=64, offset=(3 - j) * 4 * T)
+            nc.gpsimd.memset(out_win[j][:].bitcast(U32), 0)
+        sums[2] = sbuf([P, N], F32, "sums2", on="sig3")
+        sums[3] = sbuf([P, N], F32, "sums3", on="sig2")
+        table_sums(0, 2, 0, True)
+        table_sums(1, 0, 4, True)
+        table_sums(1, 1, 5, False)
         scatter(0, 0, N)
         store(0)
         scatter(1, CHUNK, CHUNK)
-        table_sums(1, 3, ps_turn, False)
+        table_sums(0, 3, 1, False)
         scatter(1, HALF + CHUNK, CHUNK)
         store(1)
-        table_sums(1, 2, ps_turn, True)
+        table_sums(1, 3, 3, False)
+        table_sums(1, 2, 2, True)
         for first in range(0, N, WIDE):
             scatter(3, first, min(WIDE, N - first))
         store(3)

@@ -38,6 +38,7 @@ def tile_attend_gbpr_w_ts_kernel(tc, xT, wT, wt, ts, xm, offs, out):
     nc = tc.nc
     with ExitStack() as ctx:
         keep = ctx.enter_context(tc.tile_pool(name="keep", bufs=1))
+        woven = ctx.enter_context(tc.tile_pool(name="woven", bufs=1))
         tail = ctx.enter_context(tc.tile_pool(name="tail", bufs=1))
         psum = ctx.enter_context(tc.psum_pool(name="psum", bufs=1))
 
@@ -107,18 +108,19 @@ def tile_attend_gbpr_w_ts_kernel(tc, xT, wT, wt, ts, xm, offs, out):
                     col = ts_first[:, side, 2 * c + b : 2 * c + b + 1]
                     nc.tensor.transpose(spread[c][:, side, b, :], col.to_broadcast([P, P]), ident[:])
         ts_rows = sbuf([P, 2 * CHUNK], F32, "ts_rows")
-        nc.scalar.copy(out=ts_rows[:], in_=spread[0][:].rearrange("p s b i -> p (s b i)"))
-        factor = {1: sbuf([P, PACK, 2 * CHUNK], F32, "factor1")}
+        nc.scalar.copy(out=ts_rows[:], in_=spread[1][:].rearrange("p s b i -> p (s b i)"))
+        factor = {0: sbuf([P, PACK, 2 * CHUNK], F32, "factor0")}
         for t in range(PACK):
             nc.scalar.activation(
-                out=factor[1][:, t, :],
-                in_=spread[1][:].rearrange("p s b i -> p (s b i)"),
+                out=factor[0][:, t, :],
+                in_=spread[0][:].rearrange("p s b i -> p (s b i)"),
                 func=ACT.Copy,
                 scale=wt_cols[:, t : t + 1],
             )
 
         w_pair = [sbuf([P, T, 2], BF16, "w_pair0"), sbuf([P, T, 2], BF16, "w_pair1", on="ts_first")]
-        w_grouped = [sbuf([P, CHUNK, PACK], BF16, "w_grouped%d" % q) for q in range(4)]
+        w_grouped = [sbuf([P, CHUNK, PACK], BF16, "w_grouped%d" % q) for q in range(3)]
+        w_grouped.append(woven.tile([P, CHUNK, PACK], BF16, name="w_grouped3", align_bytes=64, offset=0))
         w_mx = {}
 
         def cast(k, lo, hi, on_vector):
@@ -158,16 +160,6 @@ def tile_attend_gbpr_w_ts_kernel(tc, xT, wT, wt, ts, xm, offs, out):
 
         cast_load(0)
         cast_load(1)
-        factor[0] = sbuf([P, PACK, 2 * CHUNK], F32, "factor0", on="w_raw1")
-        for t in range(PACK):
-            nc.gpsimd.tensor_scalar(
-                out=factor[0][:, t, :],
-                in0=ts_rows[:],
-                scalar1=wt_cols[:, t : t + 1],
-                scalar2=0.0,
-                op0=ALU.mult,
-                op1=ALU.add,
-            )
         for q in range(4):
             gather(0, q)
         for k in range(FIRST_PAIR_LOADS, len(W_LOADS)):
@@ -209,7 +201,10 @@ def tile_attend_gbpr_w_ts_kernel(tc, xT, wT, wt, ts, xm, offs, out):
         xm_grouped = {}
 
         def round_xm(k, on, on_scalar):
-            xm_grouped[k] = sbuf([P, D // 2, PACK], BF16, "xm_grouped%d" % k, on=on)
+            if on:
+                xm_grouped[k] = sbuf([P, D // 2, PACK], BF16, "xm_grouped%d" % k, on=on)
+            else:
+                xm_grouped[k] = woven.tile([P, D // 2, PACK], BF16, name="xm_first", align_bytes=64, offset=2048)
             if on_scalar:
                 interleave(xm_grouped[k][:], xm_raw[k][:])
             else:
@@ -251,6 +246,10 @@ def tile_attend_gbpr_w_ts_kernel(tc, xT, wT, wt, ts, xm, offs, out):
         def scale(dst, b, side):
             nc.scalar.activation(out=dst, in_=dealt(b, side), func=ACT.Copy, scale=ts_col[:, side, b : b + 1])
 
+        def scale_on_vector(dst, b, side):
+            col = ts_col[:, side, b : b + 1]
+            nc.vector.tensor_scalar(out=dst, in0=dealt(b, side), scalar1=col, scalar2=None, op0=ALU.mult)
+
         margin = {}
 
         def margin_on_vector(b):
@@ -279,7 +278,7 @@ def tile_attend_gbpr_w_ts_kernel(tc, xT, wT, wt, ts, xm, offs, out):
                 for side in range(2):
                     nc.tensor.matmul(
                         turned[:, t, :],
-                        lhsT=late[:, b - 2, side, t, :],
+                        lhsT=late[side][:, b - 2, t, :],
                         rhs=ident[:],
                         start=side == 0,
                         stop=side == 1,
@@ -316,19 +315,20 @@ def tile_attend_gbpr_w_ts_kernel(tc, xT, wT, wt, ts, xm, offs, out):
 
         sums = {}
 
-        def table_sums(c, j, number, on_vector):
+        def table_sums(c, j, number, on_vector, sides=slice(0, 2)):
             acc = bank(number, [P, 2 * CHUNK])
+            cols = slice(sides.start * CHUNK, sides.stop * CHUNK)
             nc.tensor.matmul_mx(
-                out=acc[:],
+                out=acc[:, cols],
                 lhsT=xm_codes[j // 2][:, (j % 2) * P : (j % 2 + 1) * P].bitcast(E4M3),
                 lhsT_scale=xm_scales[:, j * P : (j + 1) * P],
-                rhs=h_codes[c][:].bitcast(E5M2),
-                rhs_scale=h_scales[c][:],
+                rhs=h_codes[c][:, cols].bitcast(E5M2),
+                rhs_scale=h_scales[c][:, cols],
                 start=True,
                 stop=True,
             )
-            dst = sums[j][:].rearrange("p (s c i) -> p s c i", s=2, c=2)[:, :, c]
-            src = acc[:].rearrange("p (s i) -> p s i", s=2)
+            dst = sums[j][:].rearrange("p (s c i) -> p s c i", s=2, c=2)[:, sides, c]
+            src = acc[:].rearrange("p (s i) -> p s i", s=2)[:, sides]
             if on_vector:
                 nc.vector.tensor_copy(out=dst, in_=src)
             else:
@@ -344,65 +344,77 @@ def tile_attend_gbpr_w_ts_kernel(tc, xT, wT, wt, ts, xm, offs, out):
         def store(j):
             nc.sync.dma_start(out=out[j * P : (j + 1) * P, :], in_=out_win[j][:])
 
-        round_xm(0, "x_grouped1", False)
-        round_xm(1, None, False)
+        quantize_table(3, sbuf([P, CHUNK], U32, "w_codes3")[:])
+        round_xm(0, None, True)
+        quantize_xm(0)
+        factor[1] = woven.tile([P, PACK, 2 * CHUNK], F32, name="factor1", align_bytes=64, offset=0)
+        for t in range(PACK):
+            nc.gpsimd.tensor_scalar(
+                out=factor[1][:, t, :],
+                in0=ts_rows[:],
+                scalar1=wt_cols[:, t : t + 1],
+                scalar2=0.0,
+                op0=ALU.mult,
+                op1=ALU.add,
+            )
+        round_xm(1, "ts_rows", False)
         for k in range(2):
             for b in range(2):
                 for side in range(2):
                     scores(b, side, 2 * b + side, slice(k * (R // 2), (k + 1) * (R // 2)))
         margin_on_vector(0)
         margin_on_vector(1)
-        quantize_table(3, sbuf([P, CHUNK], U32, "w_codes3", on="scaled1")[:])
-        scores(2, 0, 4)
-        scores(3, 0, 5)
+        scores(2, 1, 4)
+        scores(3, 1, 5)
+        scores(2, 0, 0)
+        scores(3, 0, 2)
+        late = {1: sbuf([P, 2, PACK, P], F32, "late1", on="scaled1")}
+        scale_on_vector(late[1][:, 0], 2, 1)
+        scale_on_vector(late[1][:, 1], 3, 1)
         sigmoid_then_turn(0, 6)
         sigmoid_then_turn(1, 7)
-        scores(2, 1, 1)
-        scores(3, 1, 3)
-        late = sbuf([P, 2, 2, PACK, P], F32, "late", on="margin1")
-        scale(late[:, 0, 0], 2, 0)
-        scale(late[:, 1, 0], 3, 0)
-        scale(late[:, 0, 1], 2, 1)
-        scale(late[:, 1, 1], 3, 1)
+        late[0] = sbuf([P, 2, PACK, P], F32, "late0", on="margin1")
+        scale(late[0][:, 0], 2, 0)
+        scale(late[0][:, 1], 3, 0)
         gradient(0, 0)
         gradient(0, 1)
-        quantize_xm(0, "flat1")
         gradient(1, 0)
         gradient(1, 1)
         quantize_h(0, 0)
         quantize_h(0, 1)
         quantize_xm(1, "h_grouped0")
-        turn_then_sigmoid(2, 0)
-        turn_then_sigmoid(3, 2)
+        turn_then_sigmoid(2, 1)
+        turn_then_sigmoid(3, 3)
         h_grouped[1] = tail.tile([P, 2 * CHUNK, PACK], BF16, name="h_grouped1", align_bytes=64, offset=4 * T - 2048)
         sums[0] = sbuf([P, N], F32, "sums0")
         sums[1] = sbuf([P, N], F32, "sums1", on="margin1")
+        table_sums(0, 1, 6, False, slice(0, 1))
+        scatter(1, 0, CHUNK)
+        table_sums(0, 1, 5, False, slice(1, 2))
         table_sums(0, 0, 7, False)
-        table_sums(0, 1, 6, False)
+        scatter(1, HALF, CHUNK)
         gradient(2, 0)
         gradient(2, 1)
         gradient(3, 0)
         gradient(3, 1)
         quantize_h(1, 0)
         quantize_h(1, 1)
-        scatter(1, 0, CHUNK)
-        scatter(1, HALF, CHUNK)
         for j in (3, 2):
             out_win[j] = tail.tile([P, T], F32, name="out_win%d" % j, align_bytes=64, offset=(3 - j) * 4 * T)
             nc.gpsimd.memset(out_win[j][:].bitcast(U32), 0)
         sums[2] = sbuf([P, N], F32, "sums2", on="sig3")
         sums[3] = sbuf([P, N], F32, "sums3", on="sig2")
-        table_sums(0, 2, 0, True)
-        table_sums(1, 0, 4, True)
-        table_sums(1, 1, 5, False)
+        table_sums(0, 2, 4, True)
+        table_sums(1, 0, 0, True)
+        table_sums(1, 1, 6, False)
         scatter(0, 0, N)
         store(0)
         scatter(1, CHUNK, CHUNK)
-        table_sums(0, 3, 1, False)
+        table_sums(0, 3, 2, False)
         scatter(1, HALF + CHUNK, CHUNK)
         store(1)
         table_sums(1, 3, 3, False)
-        table_sums(1, 2, 2, True)
+        table_sums(1, 2, 1, True)
         for first in range(0, N, WIDE):
             scatter(3, first, min(WIDE, N - first))
         store(3)

@@ -54,7 +54,7 @@ def tile_attend_gbpr_w_ts_kernel(tc, xT, wT, wt, ts, xm, offs, out):
         seed = sbuf([P, 1], F32, "seed")
         nc.vector.memset(seed[:], 0.0)
         ts_win = sbuf([P, T], F32, "ts_win")
-        nc.sync.dma_start(out=ts_win[P - 1 : P, :], in_=ts[0:1, :])
+        nc.scalar.dma_start(out=ts_win[P - 1 : P, :], in_=ts[0:1, :])
         nc.gpsimd.memset(ts_win[0 : P - 1, :].bitcast(U32), 0)
         ident = sbuf([P, P], F32, "ident")
         nc.vector.memset(ident[:], 0.0)
@@ -65,13 +65,12 @@ def tile_attend_gbpr_w_ts_kernel(tc, xT, wT, wt, ts, xm, offs, out):
         offsets = keep.tile([P, N // 16], U16, name="offsets")
         nc.sync.dma_start(offsets[:], offs)
         wt_cols = sbuf([P, PACK], F32, "wt_cols")
+        nc.scalar.dma_start(out=wt_cols[:], in_=wt[0].rearrange("(p t) o -> p (t o)", t=PACK))
         w_rows = wT.rearrange("(p u e) c -> p u e c", u=2, e=2)
         w_raw = []
         for k, (u, first, count, on_vector) in enumerate(W_LOADS):
             w_raw.append(sbuf([P, 2, count], F32, "w_raw%d" % k))
             nc.sync.dma_start(out=w_raw[k][:], in_=w_rows[:, u, :, first : first + count])
-            if k == 0:
-                nc.sync.dma_start(out=wt_cols[:], in_=wt[0].rearrange("(p t) o -> p (t o)", t=PACK))
         x_rows = xT[0].rearrange("(p t) r -> p t r", t=PACK)
         x_raw = []
         for k in range(2):
@@ -107,8 +106,6 @@ def tile_attend_gbpr_w_ts_kernel(tc, xT, wT, wt, ts, xm, offs, out):
                 for b in range(2):
                     col = ts_first[:, side, 2 * c + b : 2 * c + b + 1]
                     nc.tensor.transpose(spread[c][:, side, b, :], col.to_broadcast([P, P]), ident[:])
-        ts_rows = sbuf([P, 2 * CHUNK], F32, "ts_rows")
-        nc.scalar.copy(out=ts_rows[:], in_=spread[1][:].rearrange("p s b i -> p (s b i)"))
         factor = {0: sbuf([P, PACK, 2 * CHUNK], F32, "factor0")}
         for t in range(PACK):
             nc.scalar.activation(
@@ -164,6 +161,8 @@ def tile_attend_gbpr_w_ts_kernel(tc, xT, wT, wt, ts, xm, offs, out):
             gather(0, q)
         for k in range(FIRST_PAIR_LOADS, len(W_LOADS)):
             cast_load(k)
+        ts_rows = sbuf([P, 2 * CHUNK], F32, "ts_rows", on="w_raw2")
+        nc.scalar.copy(out=ts_rows[:], in_=spread[1][:].rearrange("p s b i -> p (s b i)"))
         x_codes = sbuf([P, R], U32, "x_codes")
         x_scales = sbuf([P, R], U8, "x_scales")
         x_grouped = [sbuf([P, R // 2, PACK], BF16, "x_grouped%d" % k) for k in range(2)]
@@ -189,11 +188,10 @@ def tile_attend_gbpr_w_ts_kernel(tc, xT, wT, wt, ts, xm, offs, out):
         quantize_table(0, early_codes[:, 0, :])
         quantize_table(2, early_codes[:, 1, :])
         quantize_x(0)
-        got1 = gather_held(1, "x_grouped0")
+        gather(1, 1)
         quantize_x(1)
+        quantize_table(1, sbuf([P, CHUNK], U32, "w_codes1", on="x_grouped0")[:])
         got3 = gather_held(3, "x_grouped1")
-        nc.scalar.copy(out=odd_words(1, U32), in_=got1[:])
-        quantize_table(1, sbuf([P, CHUNK], U32, "w_codes1")[:])
         nc.vector.tensor_copy(out=odd_words(3, I32), in_=got3[:].bitcast(I32))
 
         xm_scales = sbuf([P, D], U8, "xm_scales")
@@ -252,22 +250,30 @@ def tile_attend_gbpr_w_ts_kernel(tc, xT, wT, wt, ts, xm, offs, out):
 
         margin = {}
 
+        def place_groups(b):
+            width = PACK // 2 if b == 0 else PACK
+            return [slice(t, t + width) for t in range(0, PACK, width)]
+
         def margin_on_vector(b):
             scaled[b] = sbuf([P, PACK, P], F32, "scaled%d" % b)
-            scale(scaled[b][:], b, 0)
             margin[b] = sbuf([P, PACK, P], F32, "margin%d" % b)
-            nc.vector.scalar_tensor_tensor(
-                out=margin[b][:],
-                in0=dealt(b, 1),
-                scalar=ts_col[:, 1, b : b + 1],
-                in1=scaled[b][:],
-                op0=ALU.mult,
-                op1=ALU.add,
-            )
+            for places in place_groups(b):
+                col = ts_col[:, 0, b : b + 1]
+                nc.scalar.activation(out=scaled[b][:, places], in_=dealt(b, 0)[:, places], func=ACT.Copy, scale=col)
+            for places in place_groups(b):
+                nc.vector.scalar_tensor_tensor(
+                    out=margin[b][:, places],
+                    in0=dealt(b, 1)[:, places],
+                    scalar=ts_col[:, 1, b : b + 1],
+                    in1=scaled[b][:, places],
+                    op0=ALU.mult,
+                    op1=ALU.add,
+                )
 
         def sigmoid_then_turn(b, number):
             flat = sbuf([P, PACK, P], F32, "flat%d" % b)
-            nc.scalar.activation(out=flat[:], in_=margin[b][:], func=ACT.Sigmoid)
+            for places in place_groups(b):
+                nc.scalar.activation(out=flat[:, places], in_=margin[b][:, places], func=ACT.Sigmoid)
             sig[b] = bank(number, [P, PACK, P])
             for t in range(PACK):
                 nc.tensor.transpose(sig[b][:, t, :], flat[:, t, :], ident[:])
@@ -278,7 +284,7 @@ def tile_attend_gbpr_w_ts_kernel(tc, xT, wT, wt, ts, xm, offs, out):
                 for side in range(2):
                     nc.tensor.matmul(
                         turned[:, t, :],
-                        lhsT=late[side][:, b - 2, t, :],
+                        lhsT=late[b, side][:, t, :],
                         rhs=ident[:],
                         start=side == 0,
                         stop=side == 1,
@@ -357,7 +363,7 @@ def tile_attend_gbpr_w_ts_kernel(tc, xT, wT, wt, ts, xm, offs, out):
                 op0=ALU.mult,
                 op1=ALU.add,
             )
-        round_xm(1, "ts_rows", False)
+        round_xm(1, "w_raw2", False)
         for k in range(2):
             for b in range(2):
                 for side in range(2):
@@ -365,17 +371,17 @@ def tile_attend_gbpr_w_ts_kernel(tc, xT, wT, wt, ts, xm, offs, out):
         margin_on_vector(0)
         margin_on_vector(1)
         scores(2, 1, 4)
-        scores(3, 1, 5)
-        scores(2, 0, 0)
-        scores(3, 0, 2)
-        late = {1: sbuf([P, 2, PACK, P], F32, "late1", on="scaled1")}
-        scale_on_vector(late[1][:, 0], 2, 1)
-        scale_on_vector(late[1][:, 1], 3, 1)
+        scores(2, 0, 5)
+        scores(3, 0, 0)
+        scores(3, 1, 2)
+        late = {(2, 1): sbuf([P, PACK, P], F32, "late_first", on="scaled1")[:]}
+        scale_on_vector(late[2, 1], 2, 1)
         sigmoid_then_turn(0, 6)
         sigmoid_then_turn(1, 7)
-        late[0] = sbuf([P, 2, PACK, P], F32, "late0", on="margin1")
-        scale(late[0][:, 0], 2, 0)
-        scale(late[0][:, 1], 3, 0)
+        rest = sbuf([P, 3, PACK, P], F32, "late", on="margin1")
+        for k, key in enumerate(((2, 0), (3, 0), (3, 1))):
+            late[key] = rest[:, k]
+            scale(late[key], *key)
         gradient(0, 0)
         gradient(0, 1)
         gradient(1, 0)
@@ -406,6 +412,7 @@ def tile_attend_gbpr_w_ts_kernel(tc, xT, wT, wt, ts, xm, offs, out):
         sums[3] = sbuf([P, N], F32, "sums3", on="sig2")
         table_sums(0, 2, 4, True)
         table_sums(1, 0, 0, True)
+        table_sums(1, 2, 1, True)
         table_sums(1, 1, 6, False)
         scatter(0, 0, N)
         store(0)
@@ -414,9 +421,9 @@ def tile_attend_gbpr_w_ts_kernel(tc, xT, wT, wt, ts, xm, offs, out):
         scatter(1, HALF + CHUNK, CHUNK)
         store(1)
         table_sums(1, 3, 3, False)
-        table_sums(1, 2, 1, True)
         for first in range(0, N, WIDE):
             scatter(3, first, min(WIDE, N - first))
         store(3)
         scatter(2, 0, N)
-        store(2)
+        nc.sync.dma_start(out=out[2 * P : 3 * P, 0 : T // 2], in_=out_win[2][:, 0 : T // 2])
+        nc.scalar.dma_start(out=out[2 * P : 3 * P, T // 2 :], in_=out_win[2][:, T // 2 :])

@@ -54,7 +54,7 @@ def tile_attend_gbpr_w_ts_kernel(tc, xT, wT, wt, ts, xm, offs, out):
         seed = sbuf([P, 1], F32, "seed")
         nc.vector.memset(seed[:], 0.0)
         ts_win = sbuf([P, T], F32, "ts_win")
-        nc.scalar.dma_start(out=ts_win[P - 1 : P, :], in_=ts[0:1, :])
+        nc.sync.dma_start(out=ts_win[P - 1 : P, :], in_=ts[0:1, :])
         nc.gpsimd.memset(ts_win[0 : P - 1, :].bitcast(U32), 0)
         ident = sbuf([P, P], F32, "ident")
         nc.vector.memset(ident[:], 0.0)
@@ -65,12 +65,13 @@ def tile_attend_gbpr_w_ts_kernel(tc, xT, wT, wt, ts, xm, offs, out):
         offsets = keep.tile([P, N // 16], U16, name="offsets")
         nc.sync.dma_start(offsets[:], offs)
         wt_cols = sbuf([P, PACK], F32, "wt_cols")
-        nc.scalar.dma_start(out=wt_cols[:], in_=wt[0].rearrange("(p t) o -> p (t o)", t=PACK))
         w_rows = wT.rearrange("(p u e) c -> p u e c", u=2, e=2)
         w_raw = []
         for k, (u, first, count, on_vector) in enumerate(W_LOADS):
             w_raw.append(sbuf([P, 2, count], F32, "w_raw%d" % k))
             nc.sync.dma_start(out=w_raw[k][:], in_=w_rows[:, u, :, first : first + count])
+            if k == 0:
+                nc.sync.dma_start(out=wt_cols[:], in_=wt[0].rearrange("(p t) o -> p (t o)", t=PACK))
         x_rows = xT[0].rearrange("(p t) r -> p t r", t=PACK)
         x_raw = []
         for k in range(2):
@@ -280,14 +281,15 @@ def tile_attend_gbpr_w_ts_kernel(tc, xT, wT, wt, ts, xm, offs, out):
 
         def turn_then_sigmoid(b, number):
             turned = bank(number, [P, PACK, P])
-            for t in range(PACK):
-                for side in range(2):
+            order = (1, 0) if b == 2 else (0, 1)
+            for side in order:
+                for t in range(PACK):
                     nc.tensor.matmul(
                         turned[:, t, :],
                         lhsT=late[b, side][:, t, :],
                         rhs=ident[:],
-                        start=side == 0,
-                        stop=side == 1,
+                        start=side == order[0] and t == 0,
+                        stop=side == order[1] and t == PACK - 1,
                         is_transpose=True,
                     )
             sig[b] = sbuf([P, PACK, P], F32, "sig%d" % b)
@@ -392,12 +394,10 @@ def tile_attend_gbpr_w_ts_kernel(tc, xT, wT, wt, ts, xm, offs, out):
         turn_then_sigmoid(2, 1)
         turn_then_sigmoid(3, 3)
         h_grouped[1] = tail.tile([P, 2 * CHUNK, PACK], BF16, name="h_grouped1", align_bytes=64, offset=4 * T - 2048)
-        sums[0] = sbuf([P, N], F32, "sums0")
         sums[1] = sbuf([P, N], F32, "sums1", on="margin1")
         table_sums(0, 1, 6, False, slice(0, 1))
         scatter(1, 0, CHUNK)
         table_sums(0, 1, 5, False, slice(1, 2))
-        table_sums(0, 0, 7, False)
         scatter(1, HALF, CHUNK)
         gradient(2, 0)
         gradient(2, 1)
@@ -409,8 +409,10 @@ def tile_attend_gbpr_w_ts_kernel(tc, xT, wT, wt, ts, xm, offs, out):
             out_win[j] = tail.tile([P, T], F32, name="out_win%d" % j, align_bytes=64, offset=(3 - j) * 4 * T)
             nc.gpsimd.memset(out_win[j][:].bitcast(U32), 0)
         sums[2] = sbuf([P, N], F32, "sums2", on="sig3")
-        sums[3] = sbuf([P, N], F32, "sums3", on="sig2")
+        sums[0] = sbuf([P, N], F32, "sums0", on="sig2")
+        sums[3] = sbuf([P, N], F32, "sums3", on="scaled1")
         table_sums(0, 2, 4, True)
+        table_sums(0, 0, 7, True)
         table_sums(1, 0, 0, True)
         table_sums(1, 2, 1, True)
         table_sums(1, 1, 6, False)
@@ -425,5 +427,4 @@ def tile_attend_gbpr_w_ts_kernel(tc, xT, wT, wt, ts, xm, offs, out):
             scatter(3, first, min(WIDE, N - first))
         store(3)
         scatter(2, 0, N)
-        nc.sync.dma_start(out=out[2 * P : 3 * P, 0 : T // 2], in_=out_win[2][:, 0 : T // 2])
-        nc.scalar.dma_start(out=out[2 * P : 3 * P, T // 2 :], in_=out_win[2][:, T // 2 :])
+        store(2)

@@ -417,14 +417,15 @@ def tile_attend_gbpr_w_ts_kernel(tc, xT, wT, wt, ts, xm, offs, out):
         table_sums(1, 2, 1, True)
         table_sums(1, 1, 6, False)
         scatter(0, 0, N)
-        store(0)
+        nc.gpsimd.dma_start(out=out[0:P, :], in_=out_win[0][:])
         scatter(1, CHUNK, CHUNK)
         table_sums(0, 3, 2, False)
         scatter(1, HALF + CHUNK, CHUNK)
         store(1)
         table_sums(1, 3, 3, False)
-        for first in range(0, N, WIDE):
-            scatter(3, first, min(WIDE, N - first))
+        scatter(3, 0, CHUNK)
+        for first in range(CHUNK, N, WIDE):
+            scatter(3, first, WIDE)
         store(3)
         scatter(2, 0, N)
         store(2)

@@ -24,13 +24,15 @@ SIGN = (-1.0, 1.0)
 RUN = 4
 W_LOADS = (
     (0, 0, 1024, 1024),
-    (0, 1024, 1024, 1024),
+    (0, 1024, 768, 768),
+    (0, 1792, 256, 256),
     (1, 0, 1024, 0),
     (1, 1024, 768, 768),
     (1, 1792, 256, 160),
 )
-FIRST_PAIR_LOADS = 2
+FIRST_PAIR_LOADS = 3
 WIDE = 384
+TS_SHARE = 640
 FLOPS = 2 * 2 * N * D * R
 
 
@@ -89,8 +91,9 @@ def tile_attend_gbpr_w_ts_kernel(tc, xT, wT, wt, ts, xm, offs, out):
         nc.gpsimd.memset(out_win[1][:].bitcast(U32), 0)
 
         ts_got = sbuf([P, N], F32, "ts_got")
-        nc.vector.tensor_copy(out=ts_got[:, 0:HALF], in_=ts_win[:].indirect(slots(0, HALF)))
-        nc.scalar.activation(out=ts_got[:, HALF:], in_=ts_win[:].indirect(slots(HALF, HALF)), func=ACT.Copy)
+        nc.vector.tensor_copy(out=ts_got[:, 0:TS_SHARE], in_=ts_win[:].indirect(slots(0, TS_SHARE)))
+        rest = ts_win[:].indirect(slots(TS_SHARE, N - TS_SHARE))
+        nc.scalar.activation(out=ts_got[:, TS_SHARE:], in_=rest, func=ACT.Copy)
         ts_first = sbuf([P, 2, BLOCKS], F32, "ts_first")
         for side in range(2):
             turned = bank(side, [P, BLOCKS, P])
@@ -156,13 +159,13 @@ def tile_attend_gbpr_w_ts_kernel(tc, xT, wT, wt, ts, xm, offs, out):
             src = src.rearrange("p t (c i) -> p c t i", i=RUN)
             nc.scalar.activation(out=dst, in_=src, func=ACT.Copy)
 
-        cast_load(0)
-        cast_load(1)
+        for k in range(FIRST_PAIR_LOADS):
+            cast_load(k)
         for q in range(4):
             gather(0, q)
         for k in range(FIRST_PAIR_LOADS, len(W_LOADS)):
             cast_load(k)
-        ts_rows = sbuf([P, 2 * CHUNK], F32, "ts_rows", on="w_raw2")
+        ts_rows = sbuf([P, 2 * CHUNK], F32, "ts_rows", on="w_raw3")
         nc.scalar.copy(out=ts_rows[:], in_=spread[1][:].rearrange("p s b i -> p (s b i)"))
         x_codes = sbuf([P, R], U32, "x_codes")
         x_scales = sbuf([P, R], U8, "x_scales")
@@ -365,7 +368,7 @@ def tile_attend_gbpr_w_ts_kernel(tc, xT, wT, wt, ts, xm, offs, out):
                 op0=ALU.mult,
                 op1=ALU.add,
             )
-        round_xm(1, "w_raw2", False)
+        round_xm(1, "w_raw3", False)
         for k in range(2):
             for b in range(2):
                 for side in range(2):

@@ -192,9 +192,8 @@ def tile_attend_gbpr_w_ts_kernel(tc, xT, wT, wt, ts, xm, offs, out):
         quantize_table(0, early_codes[:, 0, :])
         quantize_table(2, early_codes[:, 1, :])
         quantize_x(0)
-        gather(1, 1)
+        got1 = gather_held(1, "x_grouped0")
         quantize_x(1)
-        quantize_table(1, sbuf([P, CHUNK], U32, "w_codes1", on="x_grouped0")[:])
         got3 = gather_held(3, "x_grouped1")
         nc.vector.tensor_copy(out=odd_words(3, I32), in_=got3[:].bitcast(I32))
 
@@ -357,6 +356,7 @@ def tile_attend_gbpr_w_ts_kernel(tc, xT, wT, wt, ts, xm, offs, out):
 
         quantize_table(3, sbuf([P, CHUNK], U32, "w_codes3")[:])
         round_xm(0, None, True)
+        nc.scalar.copy(out=odd_words(1, U32), in_=got1[:])
         quantize_xm(0)
         factor[1] = woven.tile([P, PACK, 2 * CHUNK], F32, name="factor1", align_bytes=64, offset=0)
         for t in range(PACK):
@@ -376,9 +376,10 @@ def tile_attend_gbpr_w_ts_kernel(tc, xT, wT, wt, ts, xm, offs, out):
         margin_on_vector(0)
         margin_on_vector(1)
         scores(2, 1, 4)
+        scores(3, 1, 2)
+        quantize_table(1, sbuf([P, CHUNK], U32, "w_codes1", on="scaled0")[:])
         scores(2, 0, 5)
         scores(3, 0, 0)
-        scores(3, 1, 2)
         late = {(2, 1): sbuf([P, PACK, P], F32, "late_first", on="scaled1")[:]}
         scale_on_vector(late[2, 1], 2, 1)
         sigmoid_then_turn(0, 6)

@@ -111,13 +111,20 @@ def tile_attend_gbpr_w_ts_kernel(tc, xT, wT, wt, ts, xm, offs, out):
                     col = ts_first[:, side, 2 * c + b : 2 * c + b + 1]
                     nc.tensor.transpose(spread[c][:, side, b, :], col.to_broadcast([P, P]), ident[:])
         factor = {0: sbuf([P, PACK, 2 * CHUNK], F32, "factor0")}
-        for t in range(PACK):
+
+        def first_table(t):
             nc.scalar.activation(
                 out=factor[0][:, t, :],
                 in_=spread[0][:].rearrange("p s b i -> p (s b i)"),
                 func=ACT.Copy,
                 scale=wt_cols[:, t : t + 1],
             )
+
+        first_table(0)
+        ts_rows = sbuf([P, 2 * CHUNK], F32, "ts_rows")
+        nc.scalar.copy(out=ts_rows[:], in_=spread[1][:].rearrange("p s b i -> p (s b i)"))
+        first_table(1)
+        first_table(2)
 
         w_pair = [sbuf([P, T, 2], BF16, "w_pair0"), sbuf([P, T, 2], BF16, "w_pair1", on="ts_first")]
         w_grouped = [sbuf([P, CHUNK, PACK], BF16, "w_grouped%d" % q) for q in range(3)]
@@ -163,10 +170,19 @@ def tile_attend_gbpr_w_ts_kernel(tc, xT, wT, wt, ts, xm, offs, out):
             cast_load(k)
         for q in range(4):
             gather(0, q)
+        factor[1] = sbuf([P, PACK, 2 * CHUNK], F32, "factor1", on="w_raw2")
+        for t in range(PACK):
+            nc.gpsimd.tensor_scalar(
+                out=factor[1][:, t, :],
+                in0=ts_rows[:],
+                scalar1=wt_cols[:, t : t + 1],
+                scalar2=0.0,
+                op0=ALU.mult,
+                op1=ALU.add,
+            )
         for k in range(FIRST_PAIR_LOADS, len(W_LOADS)):
             cast_load(k)
-        ts_rows = sbuf([P, 2 * CHUNK], F32, "ts_rows", on="w_raw3")
-        nc.scalar.copy(out=ts_rows[:], in_=spread[1][:].rearrange("p s b i -> p (s b i)"))
+        first_table(3)
         x_codes = sbuf([P, R], U32, "x_codes")
         x_scales = sbuf([P, R], U8, "x_scales")
         x_grouped = [sbuf([P, R // 2, PACK], BF16, "x_grouped%d" % k) for k in range(2)]
@@ -201,11 +217,8 @@ def tile_attend_gbpr_w_ts_kernel(tc, xT, wT, wt, ts, xm, offs, out):
 
         xm_grouped = {}
 
-        def round_xm(k, on, on_scalar):
-            if on:
-                xm_grouped[k] = sbuf([P, D // 2, PACK], BF16, "xm_grouped%d" % k, on=on)
-            else:
-                xm_grouped[k] = woven.tile([P, D // 2, PACK], BF16, name="xm_first", align_bytes=64, offset=2048)
+        def round_xm(k, offset, on_scalar):
+            xm_grouped[k] = woven.tile([P, D // 2, PACK], BF16, name="xm_half%d" % k, align_bytes=64, offset=offset)
             if on_scalar:
                 interleave(xm_grouped[k][:], xm_raw[k][:])
             else:
@@ -355,20 +368,10 @@ def tile_attend_gbpr_w_ts_kernel(tc, xT, wT, wt, ts, xm, offs, out):
             nc.sync.dma_start(out=out[j * P : (j + 1) * P, :], in_=out_win[j][:])
 
         quantize_table(3, sbuf([P, CHUNK], U32, "w_codes3")[:])
-        round_xm(0, None, True)
+        round_xm(0, 2048, True)
         nc.scalar.copy(out=odd_words(1, U32), in_=got1[:])
         quantize_xm(0)
-        factor[1] = woven.tile([P, PACK, 2 * CHUNK], F32, name="factor1", align_bytes=64, offset=0)
-        for t in range(PACK):
-            nc.gpsimd.tensor_scalar(
-                out=factor[1][:, t, :],
-                in0=ts_rows[:],
-                scalar1=wt_cols[:, t : t + 1],
-                scalar2=0.0,
-                op0=ALU.mult,
-                op1=ALU.add,
-            )
-        round_xm(1, "w_raw3", False)
+        round_xm(1, 1024, False)
         for k in range(2):
             for b in range(2):
                 for side in range(2):

@@ -127,8 +127,8 @@ def tile_attend_gbpr_w_ts_kernel(tc, xT, wT, wt, ts, xm, offs, out):
         first_table(2)
 
         w_pair = [sbuf([P, T, 2], BF16, "w_pair0"), sbuf([P, T, 2], BF16, "w_pair1", on="ts_first")]
-        w_grouped = [sbuf([P, CHUNK, PACK], BF16, "w_grouped%d" % q) for q in range(3)]
-        w_grouped.append(woven.tile([P, CHUNK, PACK], BF16, name="w_grouped3", align_bytes=64, offset=0))
+        w_grouped = {q: sbuf([P, CHUNK, PACK], BF16, "w_grouped%d" % q) for q in (0, 2, 3)}
+        w_grouped[1] = woven.tile([P, CHUNK, PACK], BF16, name="w_second", align_bytes=64, offset=0)
         w_mx = {}
 
         def cast(k, lo, hi, on_vector):
@@ -368,10 +368,10 @@ def tile_attend_gbpr_w_ts_kernel(tc, xT, wT, wt, ts, xm, offs, out):
             nc.sync.dma_start(out=out[j * P : (j + 1) * P, :], in_=out_win[j][:])
 
         quantize_table(3, sbuf([P, CHUNK], U32, "w_codes3")[:])
-        round_xm(0, 2048, True)
+        round_xm(0, 4096, True)
         nc.scalar.copy(out=odd_words(1, U32), in_=got1[:])
         quantize_xm(0)
-        round_xm(1, 1024, False)
+        round_xm(1, 0, False)
         for k in range(2):
             for b in range(2):
                 for side in range(2):

@@ -59,7 +59,8 @@ def tile_attend_gbpr_w_ts_kernel(tc, xT, wT, wt, ts, xm, offs, out):
         nc.sync.dma_start(out=ts_win[P - 1 : P, :], in_=ts[0:1, :])
         nc.gpsimd.memset(ts_win[0 : P - 1, :].bitcast(U32), 0)
         ident = sbuf([P, P], F32, "ident")
-        nc.vector.memset(ident[:], 0.0)
+        nc.vector.memset(ident[:, 0 : P - 1], 0.0)
+        nc.vector.memset(ident[:, P - 1 : P], 0.0)
         make_identity(nc, ident[:], nomemset=True)
         warm = sbuf([P, 1], F32, "warm")
         nc.scalar.activation(out=warm[:], in_=seed[:], func=ACT.Sigmoid)

@@ -129,7 +129,7 @@ def tile_attend_gbpr_w_ts_kernel(tc, xT, wT, wt, ts, xm, offs, out):
 
         w_pair = [sbuf([P, T, 2], BF16, "w_pair0"), sbuf([P, T, 2], BF16, "w_pair1", on="ts_first")]
         w_grouped = {q: sbuf([P, CHUNK, PACK], BF16, "w_grouped%d" % q) for q in (0, 2, 3)}
-        w_grouped[1] = woven.tile([P, CHUNK, PACK], BF16, name="w_second", align_bytes=64, offset=0)
+        w_grouped[1] = woven.tile([P, CHUNK, PACK], BF16, name="w_second", align_bytes=64, offset=1024)
         w_mx = {}
 
         def cast(k, lo, hi, on_vector):
@@ -209,9 +209,9 @@ def tile_attend_gbpr_w_ts_kernel(tc, xT, wT, wt, ts, xm, offs, out):
         quantize_table(0, early_codes[:, 0, :])
         quantize_table(2, early_codes[:, 1, :])
         quantize_x(0)
-        got1 = gather_held(1, "x_grouped0")
+        got1 = gather_held(1, "x_raw0")
         quantize_x(1)
-        got3 = gather_held(3, "x_grouped1")
+        got3 = gather_held(3, "x_raw1")
         nc.vector.tensor_copy(out=odd_words(3, I32), in_=got3[:].bitcast(I32))
 
         xm_scales = sbuf([P, D], U8, "xm_scales")
@@ -272,17 +272,20 @@ def tile_attend_gbpr_w_ts_kernel(tc, xT, wT, wt, ts, xm, offs, out):
             return [slice(t, t + width) for t in range(0, PACK, width)]
 
         def margin_on_vector(b):
-            scaled[b] = sbuf([P, PACK, P], F32, "scaled%d" % b)
             margin[b] = sbuf([P, PACK, P], F32, "margin%d" % b)
             for places in place_groups(b):
                 col = ts_col[:, 0, b : b + 1]
-                nc.scalar.activation(out=scaled[b][:, places], in_=dealt(b, 0)[:, places], func=ACT.Copy, scale=col)
+                name = "scaled%d%d" % (b, places.start)
+                scaled[b, places.start] = sbuf([P, places.stop - places.start, P], F32, name)
+                nc.scalar.activation(
+                    out=scaled[b, places.start][:], in_=dealt(b, 0)[:, places], func=ACT.Copy, scale=col
+                )
             for places in place_groups(b):
                 nc.vector.scalar_tensor_tensor(
                     out=margin[b][:, places],
                     in0=dealt(b, 1)[:, places],
                     scalar=ts_col[:, 1, b : b + 1],
-                    in1=scaled[b][:, places],
+                    in1=scaled[b, places.start][:],
                     op0=ALU.mult,
                     op1=ALU.add,
                 )
@@ -311,31 +314,22 @@ def tile_attend_gbpr_w_ts_kernel(tc, xT, wT, wt, ts, xm, offs, out):
             sig[b] = sbuf([P, PACK, P], F32, "sig%d" % b)
             nc.scalar.activation(out=sig[b][:], in_=turned[:], func=ACT.Sigmoid)
 
-        h_grouped = {0: sbuf([P, 2 * CHUNK, PACK], BF16, "h_grouped0")}
+        h_grouped = {(0, side): sbuf([P, CHUNK, PACK], BF16, "h_first%d" % side)[:] for side in range(2)}
         h_codes = [sbuf([P, 2 * CHUNK], U32, "h_codes%d" % c) for c in range(2)]
         h_scales = [sbuf([P, 2 * CHUNK], U8, "h_scales%d" % c) for c in range(2)]
 
         def gradient(b, side):
             c, first = b // 2, side * CHUNK + (b % 2) * P
             nc.vector.tensor_tensor(
-                out=h_grouped[c][:, first : first + P, :].rearrange("p (g i) t -> p g t i", i=RUN),
+                out=h_grouped[c, side][:, (b % 2) * P : (b % 2 + 1) * P, :].rearrange("p (g i) t -> p g t i", i=RUN),
                 in0=sig[b][:].rearrange("p t (g i) -> p g t i", i=RUN),
                 in1=factor[c][:, :, first : first + P].rearrange("p t (g i) -> p g t i", i=RUN),
                 op=ALU.mult,
             )
 
-        def gradient_on_gpsimd(b, side):
-            c, first = b // 2, side * CHUNK + (b % 2) * P
-            nc.gpsimd.tensor_tensor(
-                out=h_grouped[c][:, first : first + P, :],
-                in0=sig[b][:],
-                in1=factor[c][:, :, first : first + P].rearrange("p t i -> p i t"),
-                op=ALU.mult,
-            )
-
         def quantize_h(c, side):
             cols = slice(side * CHUNK, (side + 1) * CHUNK)
-            quantize(h_codes[c][:, cols], h_scales[c][:, cols], h_grouped[c][:, cols, :], E5M2)
+            quantize(h_codes[c][:, cols], h_scales[c][:, cols], h_grouped[c, side], E5M2)
 
         sums = {}
 
@@ -381,14 +375,14 @@ def tile_attend_gbpr_w_ts_kernel(tc, xT, wT, wt, ts, xm, offs, out):
         margin_on_vector(1)
         scores(2, 1, 4)
         scores(3, 1, 2)
-        quantize_table(1, sbuf([P, CHUNK], U32, "w_codes1", on="scaled0")[:])
+        quantize_table(1, sbuf([P, CHUNK], U32, "w_codes1", on="scaled00")[:])
         scores(2, 0, 5)
         scores(3, 0, 0)
-        late = {(2, 1): sbuf([P, PACK, P], F32, "late_first", on="scaled1")[:]}
+        late = {(2, 1): woven.tile([P, PACK, P], F32, name="late_first", align_bytes=64, offset=2048)[:]}
         scale_on_vector(late[2, 1], 2, 1)
         sigmoid_then_turn(0, 6)
         sigmoid_then_turn(1, 7)
-        rest = sbuf([P, 3, PACK, P], F32, "late", on="margin1")
+        rest = sbuf([P, 3, PACK, P], F32, "late", on="scaled10")
         for k, key in enumerate(((2, 0), (3, 0), (3, 1))):
             late[key] = rest[:, k]
             scale(late[key], *key)
@@ -398,14 +392,18 @@ def tile_attend_gbpr_w_ts_kernel(tc, xT, wT, wt, ts, xm, offs, out):
         gradient(1, 1)
         quantize_h(0, 0)
         quantize_h(0, 1)
-        quantize_xm(1, "h_grouped0")
+        quantize_xm(1, "h_first0")
         turn_then_sigmoid(2, 1)
         turn_then_sigmoid(3, 3)
-        h_grouped[1] = tail.tile([P, 2 * CHUNK, PACK], BF16, name="h_grouped1", align_bytes=64, offset=4 * T - 2048)
-        sums[1] = sbuf([P, N], F32, "sums1", on="margin1")
+        h_late = tail.tile([P, 2, CHUNK, PACK], BF16, name="h_late", align_bytes=64, offset=4 * T - 2048)
+        for side in range(2):
+            h_grouped[1, side] = h_late[:, side]
+        sums[1] = sbuf([P, N], F32, "sums1", on="scaled10")
         table_sums(0, 1, 6, False, slice(0, 1))
-        scatter(1, 0, CHUNK)
         table_sums(0, 1, 5, False, slice(1, 2))
+        scatter(1, 0, CHUNK)
+        sums[3] = sbuf([P, N], F32, "sums3", on="flat1")
+        table_sums(0, 3, 2, False)
         scatter(1, HALF, CHUNK)
         gradient(2, 0)
         gradient(2, 1)
@@ -418,22 +416,20 @@ def tile_attend_gbpr_w_ts_kernel(tc, xT, wT, wt, ts, xm, offs, out):
             nc.gpsimd.memset(out_win[j][:].bitcast(U32), 0)
         sums[2] = sbuf([P, N], F32, "sums2", on="sig3")
         sums[0] = sbuf([P, N], F32, "sums0", on="sig2")
-        sums[3] = sbuf([P, N], F32, "sums3", on="scaled1")
         table_sums(0, 2, 4, True)
         table_sums(0, 0, 7, True)
         table_sums(1, 0, 0, True)
         table_sums(1, 2, 1, True)
         table_sums(1, 1, 6, False)
+        table_sums(1, 3, 3, False)
         scatter(0, 0, N)
         nc.gpsimd.dma_start(out=out[0:P, :], in_=out_win[0][:])
         scatter(1, CHUNK, CHUNK)
-        table_sums(0, 3, 2, False)
+        scatter(3, 0, WIDE)
         scatter(1, HALF + CHUNK, CHUNK)
         store(1)
-        table_sums(1, 3, 3, False)
-        scatter(3, 0, CHUNK)
-        for first in range(CHUNK, N, WIDE):
-            scatter(3, first, WIDE)
+        scatter(3, WIDE, WIDE)
+        scatter(3, 2 * WIDE, CHUNK)
         store(3)
         scatter(2, 0, N)
         store(2)

@@ -27,7 +27,7 @@ W_LOADS = (
     (0, 1024, 768, 768),
     (0, 1792, 256, 256),
     (1, 0, 1024, 0),
-    (1, 1024, 768, 768),
+    (1, 1024, 768, 576),
     (1, 1792, 256, 160),
 )
 FIRST_PAIR_LOADS = 3
@@ -362,10 +362,10 @@ def tile_attend_gbpr_w_ts_kernel(tc, xT, wT, wt, ts, xm, offs, out):
         def store(j):
             nc.sync.dma_start(out=out[j * P : (j + 1) * P, :], in_=out_win[j][:])
 
-        quantize_table(3, sbuf([P, CHUNK], U32, "w_codes3")[:])
         round_xm(0, 4096, True)
         nc.scalar.copy(out=odd_words(1, U32), in_=got1[:])
         quantize_xm(0)
+        quantize_table(3, sbuf([P, CHUNK], U32, "w_codes3", on="xm_raw0")[:])
         round_xm(1, 0, False)
         for k in range(2):
             for b in range(2):
@@ -425,11 +425,11 @@ def tile_attend_gbpr_w_ts_kernel(tc, xT, wT, wt, ts, xm, offs, out):
         scatter(0, 0, N)
         nc.gpsimd.dma_start(out=out[0:P, :], in_=out_win[0][:])
         scatter(1, CHUNK, CHUNK)
-        scatter(3, 0, WIDE)
+        scatter(3, 0, CHUNK)
         scatter(1, HALF + CHUNK, CHUNK)
         store(1)
-        scatter(3, WIDE, WIDE)
-        scatter(3, 2 * WIDE, CHUNK)
+        for first in range(CHUNK, N, WIDE):
+            scatter(3, first, WIDE)
         store(3)
         scatter(2, 0, N)
         store(2)

from contextlib import ExitStack

import concourse.mybir as mybir
from concourse.masks import make_identity

F32 = mybir.dt.float32
BF16 = mybir.dt.bfloat16
U32 = mybir.dt.uint32
I32 = mybir.dt.int32
U16 = mybir.dt.uint16
U8 = mybir.dt.uint8
E4M3 = mybir.dt.float8_e4m3fn_x4
E5M2 = mybir.dt.float8_e5m2_x4
ACT = mybir.ActivationFunctionType
ALU = mybir.AluOpType

P = 128
PACK = 4
N, T, D, R = 1024, 2048, 512, 512
HALF = N // 2
CHUNK = 2 * P
BLOCKS = HALF // P
SIGN = (-1.0, 1.0)
RUN = 4
W_LOADS = (
    (0, 0, 1024, 1024),
    (0, 1024, 768, 768),
    (0, 1792, 256, 256),
    (1, 0, 1024, 0),
    (1, 1024, 768, 576),
    (1, 1792, 256, 160),
)
FIRST_PAIR_LOADS = 3
WIDE = 384
TS_SHARE = 640
FLOPS = 2 * 2 * N * D * R


def tile_attend_gbpr_w_ts_kernel(tc, xT, wT, wt, ts, xm, offs, out):
    nc = tc.nc
    with ExitStack() as ctx:
        keep = ctx.enter_context(tc.tile_pool(name="keep", bufs=1))
        woven = ctx.enter_context(tc.tile_pool(name="woven", bufs=1))
        tail = ctx.enter_context(tc.tile_pool(name="tail", bufs=1))
        psum = ctx.enter_context(tc.psum_pool(name="psum", bufs=1))

        def bank(number, shape):
            return psum.tile(shape, F32, name="bank%d" % number)

        def sbuf(shape, dtype, name, on=None):
            return keep.tile(shape, dtype, name=name, tag=on or name, align_bytes=64)

        def slots(first, count):
            return offsets[:, first // 16 : (first + count) // 16]

        seed = sbuf([P, 1], F32, "seed")
        nc.vector.memset(seed[:], 0.0)
        ts_win = sbuf([P, T], F32, "ts_win")
        nc.sync.dma_start(out=ts_win[P - 1 : P, :], in_=ts[0:1, :])
        nc.gpsimd.memset(ts_win[0 : P - 1, :].bitcast(U32), 0)
        ident = sbuf([P, P], F32, "ident")
        nc.vector.memset(ident[:, 0 : P - 1], 0.0)
        nc.vector.memset(ident[:, P - 1 : P], 0.0)
        make_identity(nc, ident[:], nomemset=True)
        warm = sbuf([P, 1], F32, "warm")
        nc.scalar.activation(out=warm[:], in_=seed[:], func=ACT.Sigmoid)

        offsets = keep.tile([P, N // 16], U16, name="offsets")
        nc.sync.dma_start(offsets[:], offs)
        wt_cols = sbuf([P, PACK], F32, "wt_cols")
        w_rows = wT.rearrange("(p u e) c -> p u e c", u=2, e=2)
        w_raw = []
        for k, (u, first, count, on_vector) in enumerate(W_LOADS):
            w_raw.append(sbuf([P, 2, count], F32, "w_raw%d" % k))
            nc.sync.dma_start(out=w_raw[k][:], in_=w_rows[:, u, :, first : first + count])
            if k == 0:
                nc.sync.dma_start(out=wt_cols[:], in_=wt[0].rearrange("(p t) o -> p (t o)", t=PACK))
        x_rows = xT[0].rearrange("(p t) r -> p t r", t=PACK)
        x_raw = []
        for k in range(2):
            x_raw.append(sbuf([P, PACK, R // 2], F32, "x_raw%d" % k))
            nc.sync.dma_start(out=x_raw[k][:], in_=x_rows[:, :, k * (R // 2) : (k + 1) * (R // 2)])
        xm_rows = xm[0].rearrange("(p t) d -> p t d", t=PACK)
        xm_raw = []
        for k in range(2):
            xm_raw.append(sbuf([P, PACK, D // 2], F32, "xm_raw%d" % k))
            nc.sync.dma_start(out=xm_raw[k][:], in_=xm_rows[:, :, k * (D // 2) : (k + 1) * (D // 2)])

        out_win = {j: sbuf([P, T], F32, "out_win%d" % j) for j in (0, 1)}
        nc.vector.memset(out_win[0][:, 0 : T - 1].bitcast(U32), 0)
        nc.vector.memset(out_win[0][:, T - 1 : T].bitcast(U32), 0)
        nc.gpsimd.memset(out_win[1][:].bitcast(U32), 0)

        ts_got = sbuf([P, N], F32, "ts_got")
        nc.vector.tensor_copy(out=ts_got[:, 0:TS_SHARE], in_=ts_win[:].indirect(slots(0, TS_SHARE)))
        rest = ts_win[:].indirect(slots(TS_SHARE, N - TS_SHARE))
        nc.scalar.activation(out=ts_got[:, TS_SHARE:], in_=rest, func=ACT.Copy)
        ts_first = sbuf([P, 2, BLOCKS], F32, "ts_first")
        for side in range(2):
            turned = bank(side, [P, BLOCKS, P])
            for b in range(BLOCKS):
                first = side * HALF + b * P
                nc.tensor.transpose(turned[:, b, :], ts_got[:, first : first + P], ident[:])
            nc.scalar.activation(out=ts_first[:, side, :], in_=turned[:, :, P - 1], func=ACT.Copy, scale=SIGN[side])
        ts_col = sbuf([P, 2, BLOCKS], F32, "ts_col")
        nc.gpsimd.tensor_copy(out=ts_col[:], in_=ts_first[:])
        spread = []
        for c in range(2):
            spread.append(bank(6 + c, [P, 2, 2, P]))
            for side in range(2):
                for b in range(2):
                    col = ts_first[:, side, 2 * c + b : 2 * c + b + 1]
                    nc.tensor.transpose(spread[c][:, side, b, :], col.to_broadcast([P, P]), ident[:])
        factor = {0: sbuf([P, PACK, 2 * CHUNK], F32, "factor0")}

        def first_table(t):
            nc.scalar.activation(
                out=factor[0][:, t, :],
                in_=spread[0][:].rearrange("p s b i -> p (s b i)"),
                func=ACT.Copy,
                scale=wt_cols[:, t : t + 1],
            )

        first_table(0)
        ts_rows = sbuf([P, 2 * CHUNK], F32, "ts_rows")
        nc.scalar.copy(out=ts_rows[:], in_=spread[1][:].rearrange("p s b i -> p (s b i)"))
        first_table(1)
        first_table(2)

        w_pair = [sbuf([P, T, 2], BF16, "w_pair0"), sbuf([P, T, 2], BF16, "w_pair1", on="ts_first")]
        w_grouped = {q: sbuf([P, CHUNK, PACK], BF16, "w_grouped%d" % q) for q in (0, 2, 3)}
        w_grouped[1] = woven.tile([P, CHUNK, PACK], BF16, name="w_second", align_bytes=64, offset=1024)
        w_mx = {}

        def cast(k, lo, hi, on_vector):
            u, first = W_LOADS[k][0:2]
            dst = w_pair[u][:, first + lo : first + hi, :].rearrange("p (c i) e -> p c e i", i=RUN)
            src = w_raw[k][:, :, lo:hi].rearrange("p e (c i) -> p c e i", i=RUN)
            if on_vector:
                nc.vector.tensor_copy(out=dst, in_=src)
            else:
                nc.scalar.activation(out=dst, in_=src, func=ACT.Copy)

        def cast_load(k):
            count, on_vector = W_LOADS[k][2:4]
            if on_vector < count:
                cast(k, 0, count - on_vector, False)
            if on_vector:
                cast(k, count - on_vector, count, True)

        def gather(u, q):
            window = w_pair[u][:].rearrange("p c e -> p (c e)").bitcast(U32)
            words = w_grouped[q][:].rearrange("p n t -> p (n t)").bitcast(U32).rearrange("p (n u) -> p n u", u=2)
            nc.vector.tensor_copy(out=words[:, :, u], in_=window.indirect(slots(q * CHUNK, CHUNK)))

        def quantize(codes, scales, grouped, fmt):
            nc.vector.quantize_mx(out=codes.bitcast(fmt), scales=scales, in_=grouped.rearrange("p n t -> p (n t)"))

        def quantize_table(q, codes):
            scales = sbuf([P, CHUNK], U8, "w_scales%d" % q)
            quantize(codes, scales[:], w_grouped[q][:], E4M3)
            for b in range(2):
                w_mx[2 * q + b] = (codes[:, b * P : (b + 1) * P], scales[:, b * P : (b + 1) * P])

        def interleave(dst, src):
            dst = dst.rearrange("p (c i) t -> p c t i", i=RUN)
            src = src.rearrange("p t (c i) -> p c t i", i=RUN)
            nc.scalar.activation(out=dst, in_=src, func=ACT.Copy)

        for k in range(FIRST_PAIR_LOADS):
            cast_load(k)
        for q in range(4):
            gather(0, q)
        factor[1] = sbuf([P, PACK, 2 * CHUNK], F32, "factor1", on="w_raw2")
        for t in range(PACK):
            nc.gpsimd.tensor_scalar(
                out=factor[1][:, t, :],
                in0=ts_rows[:],
                scalar1=wt_cols[:, t : t + 1],
                scalar2=0.0,
                op0=ALU.mult,
                op1=ALU.add,
            )
        for k in range(FIRST_PAIR_LOADS, len(W_LOADS)):
            cast_load(k)
        first_table(3)
        x_codes = sbuf([P, R], U32, "x_codes")
        x_scales = sbuf([P, R], U8, "x_scales")
        x_grouped = [sbuf([P, R // 2, PACK], BF16, "x_grouped%d" % k) for k in range(2)]

        def quantize_x(k):
            cols = slice(k * (R // 2), (k + 1) * (R // 2))
            interleave(x_grouped[k][:], x_raw[k][:])
            quantize(x_codes[:, cols], x_scales[:, cols], x_grouped[k][:], E4M3)

        def gather_held(q, on):
            got = sbuf([P, CHUNK], U32, "w_got%d" % q, on=on)
            window = w_pair[1][:].rearrange("p c e -> p (c e)").bitcast(U32)
            nc.vector.tensor_copy(out=got[:], in_=window.indirect(slots(q * CHUNK, CHUNK)))
            return got

        def odd_words(q, dtype):
            words = w_grouped[q][:].rearrange("p n t -> p (n t)").bitcast(dtype)
            return words.rearrange("p (n u) -> p n u", u=2)[:, :, 1]

        early_codes = sbuf([P, 2, CHUNK], U32, "early_codes")
        gather(1, 0)
        gather(1, 2)
        quantize_table(0, early_codes[:, 0, :])
        quantize_table(2, early_codes[:, 1, :])
        quantize_x(0)
        got1 = gather_held(1, "x_raw0")
        quantize_x(1)
        got3 = gather_held(3, "x_raw1")
        nc.vector.tensor_copy(out=odd_words(3, I32), in_=got3[:].bitcast(I32))

        xm_scales = sbuf([P, D], U8, "xm_scales")

        xm_grouped = {}

        def round_xm(k, offset, on_scalar):
            xm_grouped[k] = woven.tile([P, D // 2, PACK], BF16, name="xm_half%d" % k, align_bytes=64, offset=offset)
            if on_scalar:
                interleave(xm_grouped[k][:], xm_raw[k][:])
            else:
                nc.gpsimd.tensor_scalar(
                    out=xm_grouped[k][:],
                    in0=xm_raw[k][:].rearrange("p t c -> p c t"),
                    scalar1=1.0,
                    scalar2=0.0,
                    op0=ALU.mult,
                    op1=ALU.add,
                )

        xm_codes = {}

        def quantize_xm(k, on=None):
            cols = slice(k * (D // 2), (k + 1) * (D // 2))
            xm_codes[k] = sbuf([P, D // 2], U32, "xm_codes%d" % k, on=on)
            quantize(xm_codes[k][:], xm_scales[:, cols], xm_grouped[k][:], E4M3)

        score, scaled, sig = {}, {}, {}

        def scores(b, side, number, cols=slice(0, R)):
            codes, scales = w_mx[side * BLOCKS + b]
            if cols.start == 0:
                score[b, side] = bank(number, [P, R])
            nc.tensor.matmul_mx(
                out=score[b, side][:, cols],
                lhsT=codes.bitcast(E4M3),
                lhsT_scale=scales,
                rhs=x_codes[:, cols].bitcast(E4M3),
                rhs_scale=x_scales[:, cols],
                start=True,
                stop=True,
            )

        def dealt(b, side):
            return score[b, side][:].rearrange("p (m t) -> p t m", t=PACK)

        def scale(dst, b, side):
            nc.scalar.activation(out=dst, in_=dealt(b, side), func=ACT.Copy, scale=ts_col[:, side, b : b + 1])

        def scale_on_vector(dst, b, side):
            col = ts_col[:, side, b : b + 1]
            nc.vector.tensor_scalar(out=dst, in0=dealt(b, side), scalar1=col, scalar2=None, op0=ALU.mult)

        margin = {}

        def place_groups(b):
            width = PACK // 2 if b == 0 else PACK
            return [slice(t, t + width) for t in range(0, PACK, width)]

        def margin_on_vector(b):
            margin[b] = sbuf([P, PACK, P], F32, "margin%d" % b)
            for places in place_groups(b):
                col = ts_col[:, 0, b : b + 1]
                name = "scaled%d%d" % (b, places.start)
                scaled[b, places.start] = sbuf([P, places.stop - places.start, P], F32, name)
                nc.scalar.activation(
                    out=scaled[b, places.start][:], in_=dealt(b, 0)[:, places], func=ACT.Copy, scale=col
                )
            for places in place_groups(b):
                nc.vector.scalar_tensor_tensor(
                    out=margin[b][:, places],
                    in0=dealt(b, 1)[:, places],
                    scalar=ts_col[:, 1, b : b + 1],
                    in1=scaled[b, places.start][:],
                    op0=ALU.mult,
                    op1=ALU.add,
                )

        def sigmoid_then_turn(b, number):
            flat = sbuf([P, PACK, P], F32, "flat%d" % b)
            for places in place_groups(b):
                nc.scalar.activation(out=flat[:, places], in_=margin[b][:, places], func=ACT.Sigmoid)
            sig[b] = bank(number, [P, PACK, P])
            for t in range(PACK):
                nc.tensor.transpose(sig[b][:, t, :], flat[:, t, :], ident[:])

        def turn_then_sigmoid(b, number):
            turned = bank(number, [P, PACK, P])
            order = (1, 0) if b == 2 else (0, 1)
            for side in order:
                for t in range(PACK):
                    nc.tensor.matmul(
                        turned[:, t, :],
                        lhsT=late[b, side][:, t, :],
                        rhs=ident[:],
                        start=side == order[0] and t == 0,
                        stop=side == order[1] and t == PACK - 1,
                        is_transpose=True,
                    )
            sig[b] = sbuf([P, PACK, P], F32, "sig%d" % b)
            nc.scalar.activation(out=sig[b][:], in_=turned[:], func=ACT.Sigmoid)

        h_grouped = {(0, side): sbuf([P, CHUNK, PACK], BF16, "h_first%d" % side)[:] for side in range(2)}
        h_codes = [sbuf([P, 2 * CHUNK], U32, "h_codes%d" % c) for c in range(2)]
        h_scales = [sbuf([P, 2 * CHUNK], U8, "h_scales%d" % c) for c in range(2)]

        def gradient(b, side):
            c, first = b // 2, side * CHUNK + (b % 2) * P
            nc.vector.tensor_tensor(
                out=h_grouped[c, side][:, (b % 2) * P : (b % 2 + 1) * P, :].rearrange("p (g i) t -> p g t i", i=RUN),
                in0=sig[b][:].rearrange("p t (g i) -> p g t i", i=RUN),
                in1=factor[c][:, :, first : first + P].rearrange("p t (g i) -> p g t i", i=RUN),
                op=ALU.mult,
            )

        def quantize_h(c, side):
            cols = slice(side * CHUNK, (side + 1) * CHUNK)
            quantize(h_codes[c][:, cols], h_scales[c][:, cols], h_grouped[c, side], E5M2)

        sums = {}

        def table_sums(c, j, number, on_vector, sides=slice(0, 2)):
            acc = bank(number, [P, 2 * CHUNK])
            cols = slice(sides.start * CHUNK, sides.stop * CHUNK)
            nc.tensor.matmul_mx(
                out=acc[:, cols],
                lhsT=xm_codes[j // 2][:, (j % 2) * P : (j % 2 + 1) * P].bitcast(E4M3),
                lhsT_scale=xm_scales[:, j * P : (j + 1) * P],
                rhs=h_codes[c][:, cols].bitcast(E5M2),
                rhs_scale=h_scales[c][:, cols],
                start=True,
                stop=True,
            )
            dst = sums[j][:].rearrange("p (s c i) -> p s c i", s=2, c=2)[:, sides, c]
            src = acc[:].rearrange("p (s i) -> p s i", s=2)[:, sides]
            if on_vector:
                nc.vector.tensor_copy(out=dst, in_=src)
            else:
                nc.scalar.copy(out=dst, in_=src)

        def scatter(j, first, count):
            place = out_win[j][:].indirect(slots(first, count))
            if j % 2 == 0:
                nc.vector.tensor_copy(out=place, in_=sums[j][:, first : first + count])
            else:
                nc.scalar.activation(out=place, in_=sums[j][:, first : first + count], func=ACT.Copy)

        def store(j):
            nc.sync.dma_start(out=out[j * P : (j + 1) * P, :], in_=out_win[j][:])

        round_xm(0, 4096, True)
        nc.scalar.copy(out=odd_words(1, U32), in_=got1[:])
        quantize_xm(0)
        quantize_table(3, sbuf([P, CHUNK], U32, "w_codes3", on="xm_raw0")[:])
        round_xm(1, 0, False)
        for k in range(2):
            for b in range(2):
                for side in range(2):
                    scores(b, side, 2 * b + side, slice(k * (R // 2), (k + 1) * (R // 2)))
        margin_on_vector(0)
        margin_on_vector(1)
        scores(2, 1, 4)
        scores(3, 1, 2)
        quantize_table(1, sbuf([P, CHUNK], U32, "w_codes1", on="scaled00")[:])
        scores(2, 0, 5)
        scores(3, 0, 0)
        late = {(2, 1): woven.tile([P, PACK, P], F32, name="late_first", align_bytes=64, offset=2048)[:]}
        scale_on_vector(late[2, 1], 2, 1)
        sigmoid_then_turn(0, 6)
        sigmoid_then_turn(1, 7)
        rest = sbuf([P, 3, PACK, P], F32, "late", on="scaled10")
        for k, key in enumerate(((2, 0), (3, 0), (3, 1))):
            late[key] = rest[:, k]
            scale(late[key], *key)
        gradient(0, 0)
        gradient(0, 1)
        gradient(1, 0)
        gradient(1, 1)
        quantize_h(0, 0)
        quantize_h(0, 1)
        quantize_xm(1, "h_first0")
        turn_then_sigmoid(2, 1)
        turn_then_sigmoid(3, 3)
        h_late = tail.tile([P, 2, CHUNK, PACK], BF16, name="h_late", align_bytes=64, offset=4 * T - 2048)
        for side in range(2):
            h_grouped[1, side] = h_late[:, side]
        sums[1] = sbuf([P, N], F32, "sums1", on="scaled10")
        table_sums(0, 1, 6, False, slice(0, 1))
        table_sums(0, 1, 5, False, slice(1, 2))
        scatter(1, 0, CHUNK)
        sums[3] = sbuf([P, N], F32, "sums3", on="flat1")
        table_sums(0, 3, 2, False)
        scatter(1, HALF, CHUNK)
        gradient(2, 0)
        gradient(2, 1)
        gradient(3, 0)
        gradient(3, 1)
        quantize_h(1, 0)
        quantize_h(1, 1)
        for j in (3, 2):
            out_win[j] = tail.tile([P, T], F32, name="out_win%d" % j, align_bytes=64, offset=(3 - j) * 4 * T)
            nc.gpsimd.memset(out_win[j][:].bitcast(U32), 0)
        sums[2] = sbuf([P, N], F32, "sums2", on="sig3")
        sums[0] = sbuf([P, N], F32, "sums0", on="sig2")
        table_sums(0, 2, 4, True)
        table_sums(0, 0, 7, True)
        table_sums(1, 0, 0, True)
        table_sums(1, 2, 1, True)
        table_sums(1, 1, 6, False)
        table_sums(1, 3, 3, False)
        scatter(0, 0, N)
        nc.gpsimd.dma_start(out=out[0:P, :], in_=out_win[0][:])
        scatter(1, CHUNK, CHUNK)
        scatter(3, 0, CHUNK)
        scatter(1, HALF + CHUNK, CHUNK)
        store(1)
        for first in range(CHUNK, N, WIDE):
            scatter(3, first, WIDE)
        store(3)
        scatter(2, 0, N)
        store(2)
